import numpy as np, ml_dtypes
CORES = [25,29,65,69,153,157,193,197]
N = 8
import mx_ref
BF = ml_dtypes.bfloat16
def pick(q, e):
    c = np.concatenate([q[0].reshape(128, -1, 4), np.zeros((128, 1, 4), np.uint8)], axis=1); s = np.concatenate([q[1], np.ones((16, 1), np.uint8)], axis=1)
    return (np.ascontiguousarray(c[:, e].reshape(128, -1)), np.ascontiguousarray(s[:, e]))
def join(*qs):
    return (np.concatenate([q[0] for q in qs], axis=1), np.concatenate([q[1] for q in qs], axis=1))
def put(q, e, v):
    c, s = q[0].reshape(128, -1, 4).copy(), q[1].copy(); c[:, e] = v[0].reshape(128, -1, 4); s[:, e] = v[1]
    return (c.reshape(128, -1), s)
def pk(c, s):
    return (np.ascontiguousarray(c), mx_ref.live(s))
def emit(q):
    return q[0], q[1]
def decode(q):
    o = []
    for b in range(4):
        e = np.zeros((128, 128, 4), np.float32); e[np.arange(128), np.arange(128), b] = 1
        o.append(mx_ref.matmul(mx_ref.quantize(e.reshape(128, 512).astype(BF)), q))
    return np.stack(o, axis=2).reshape(128, -1)
def f(rng, *shape):
    return mx_ref.flush((rng.standard_normal(shape, dtype=np.float32) * np.exp2(rng.integers(-2, 3, shape[:-1] + (1,)))).astype(BF))
def wide(rng, *shape, cols=0):
    v = rng.standard_normal(shape, dtype=np.float32) * np.exp2(rng.integers(-12, 13, shape)).astype(np.float32)
    if cols: v *= np.repeat(np.exp2(rng.integers(-cols, cols + 1, shape[:-2] + (1, shape[-1] // 4))) * (rng.random(shape[:-2] + (1, shape[-1] // 4)) > 0.0625), 4, axis=-1).astype(np.float32)
    return mx_ref.flush(v.astype(BF))
T, CAPP = 128, 32
def quads(q, e):
    c = np.concatenate([q[0].reshape(128, -1, 4), np.zeros((128, 1, 4), np.uint8)], axis=1); s = np.concatenate([q[1], np.ones((16, 1), np.uint8)], axis=1)
    return (np.concatenate([c[32 * h:32 * h + 32][:, e[h]] for h in range(4)]).reshape(128, -1), np.concatenate([s[4 * h:4 * h + 4][:, e[h]] for h in range(4)]))
def level(b, z):
    n, e = z[1].shape[1], []
    for h in range(4):
        only = np.where(np.arange(4)[:, None] == h, np.arange(n)[None, :], -1)
        e.append(np.argmax(mx_ref.matmul(b, quads(z, only)) + np.float32(0), axis=0))
    e = np.stack(e)
    return e, quads(b, e)
def big(v):
    v = v.astype(np.float32)
    v[np.abs(v) < np.float32(2.0 ** -16)] = 0
    return v.astype(BF)
def coarse(v):
    v = v.copy()
    v[:, N:] = 0
    return np.stack([v.reshape(128, 512)] * N)
def planted(rng, cell, low=False):
    at = rng.permutation(N)[np.arange(128) // (128 // N)]
    c = (1 + rng.random((128, 128, 4))) * (at[:, None] == np.arange(128)[None, :])[:, :, None]
    on = at[None, :, None] == cell[:, None, :]
    v = np.where(on[:, :, :, None], 8 + 8 * rng.random((N, 128, T, 4)), 2 * rng.random((N, 128, T, 4)) - 1)
    if low:
        u = 1 + rng.random((N, 128, T // 2, 4))
        v[:, :, 1::2] = np.where(on[:, :, 1::2, None], -0.5 * u, -8 * u)
        c = c * 2.0 ** 20
    v = v * np.exp2(rng.integers(-3, 4, (N, 1, T, 1)))
    return {"x": big(v.reshape(N, 128, 4 * T)), "co": coarse(big(c))}
def setup_inputs(rng):
    return {"x": big(f(rng, N, 128, 4 * T)), "co": coarse(big(f(rng, 128, 512)).reshape(128, 128, 4)), "b1": big(f(rng, N, 128, 512)), "b2": big(f(rng, N, 128, 512)), "w": f(rng, N, 128, 512)}
def setup_inputs_spread(rng):
    d = setup_inputs(rng)
    d["x"], d["b1"] = big(wide(rng, N, 128, 4 * T, cols=6)), big(wide(rng, N, 128, 512))
    return d
def setup_inputs_ties(rng):
    d = setup_inputs(rng)
    for k in ("b1", "b2"):
        b = d[k].reshape(N, 128, 128, 4).copy()
        for r in range(N):
            for h in range(4): b[r, 32 * h:32 * h + 32] = b[r, 32 * h:32 * h + 32][:, rng.permutation(128) % 32]
        d[k] = b.reshape(N, 128, 512)
    c = d["co"][0].reshape(128, 128, 4).copy()
    c[:, :N] = c[:, rng.permutation(N) % (N // 2)]
    d["co"] = coarse(c)
    return d
def setup_inputs_crowd(rng):
    g, cell = int(rng.integers(0, N)), []
    for s in range(N):
        o = rng.permutation(np.delete(np.arange(N), g))
        if o[0] == s: o = o[::-1]
        m = int(rng.integers(1, 17))
        cell.append(rng.permutation(np.concatenate([np.full(CAPP + m, g), np.full(CAPP, o[0]), o[1:][rng.integers(0, N - 2, T - 2 * CAPP - m)]])))
    return {**setup_inputs(rng), **planted(rng, np.stack(cell))}
def setup_inputs_few(rng):
    g, a, b = [int(i) for i in rng.permutation(N)[:3]]
    cell = np.delete(np.arange(N), g)[rng.integers(0, N - 1, (N, T))]
    cell[a], cell[b] = a, a
    return {**setup_inputs(rng), **planted(rng, cell, low=True)}
def setup_inputs_zero(rng):
    d, h = setup_inputs(rng), [int(i) for i in rng.permutation(4)]
    neg, pat, gap = [slice(32 * i, 32 * i + 32) for i in h[:3]]
    p = (1 + rng.random((32, 1, 4))) * np.exp2(rng.integers(-2, 3, (32, 1, 1)))
    v, b, c = d["x"].astype(np.float32).reshape(N, 128, T, 4), d["b1"].astype(np.float32).reshape(N, 128, 128, 4), d["co"][0].reshape(128, 128, 4).copy()
    u = d["b2"].astype(np.float32)
    c[neg], c[pat] = 0, 0
    c[:, int(rng.integers(0, N))] = 0
    v[:, neg], b[:, neg], u[:, neg] = -np.abs(v[:, neg]), np.abs(b[:, neg]), np.abs(u[:, neg])
    v[:, pat] = p
    for r in range(N):
        e, k = rng.permutation(T), rng.integers(0, 4, 128)
        v[r, gap][:, e[T // 8:T // 2]] = 0
        v[r][:, e[:T // 8]] = 0
        k[int(rng.integers(0, 128))] = 0
        b[r, pat] = p * np.exp2(-k.astype(np.float64))[:, None]
        if r % 2 == 0: b[r, neg, int(rng.integers(0, 128))] = 0
    k = np.float32(2.0 ** 20)
    d["x"], d["b1"], d["b2"], d["co"] = big(v.reshape(N, 128, 4 * T) * k), big(b.reshape(N, 128, 512) * k), big(u * k), coarse(c)
    return d
def check_inputs(d):
    b = []
    for k in ("x", "co", "b1", "b2", "w"):
        v = np.abs(d[k].astype(np.float32))
        if not (np.isfinite(v).all() and ((v == 0) | (v >= 2.0 ** -30) & (v <= 2.0 ** 30)).all()): b.append("a value of " + k)
    c = d["co"].astype(np.float32)
    if (c[:, :, 4 * N:] != 0).any(): b.append("co has numbers behind its first N columns")
    if (c != c[:1]).any(): b.append("co isn't the same on all ranks")
    return b
def reference(x, co, b1, b2, w):
    oc, osc = np.zeros((N, 128, 8 * T), np.uint8), np.zeros((N, 16, 2 * T), np.uint8)
    wn, y = np.full((N, 8, T), -1, np.float32), np.zeros((N, 128, T), np.float32)
    q = [mx_ref.quantize(x[s]) for s in range(N)]
    taken = np.full((N, N, CAPP), -1)
    for s in range(N):
        cell = np.argmax(mx_ref.matmul(mx_ref.quantize(co[s]), q[s])[:N] + np.float32(0), axis=0)
        for d in range(N):
            t = np.flatnonzero(cell == d)[:CAPP]
            taken[s, d, :len(t)] = t
    home = [pick(q[s], np.full(2 * T, -1)) for s in range(N)]
    for d in range(N):
        z = join(*[pick(q[s], taken[s, d]) for s in range(N)])
        n1, v1 = level(mx_ref.quantize(b1[d]), z)
        r = mx_ref.quantize((decode(z) - decode(v1)).astype(BF))
        n2, v2 = level(mx_ref.quantize(b2[d]), r)
        for s in range(N):
            k = np.flatnonzero(taken[s, d] >= 0)
            t, i = taken[s, d][k], s * CAPP + k
            wn[s, :4, t], wn[s, 4:, t] = n1[:, i].T, n2[:, i].T
            home[s] = put(put(home[s], t, pick(v1, i)), T + t, pick(v2, i))
    for s in range(N):
        oc[s], osc[s] = emit(home[s])
        m = mx_ref.matmul(mx_ref.quantize(w[s]), home[s])
        y[s] = m[:, :T] + m[:, T:]
    return {"oc": oc, "osc": osc, "wn": wn, "y": y}

@@ -1,0 +1,614 @@
+from concourse.bass import DstId, RemoteDMATransfer
+from concourse.mybir import dt, AluOpType, AxisListType, ActivationFunctionType
+
+OP = AluOpType
+AF = ActivationFunctionType
+F8 = "float8_e4m3fn_x4"
+
+SCRATCH = {}
+
+
+def _codes(name, n):
+    SCRATCH[name] = ("sbuf", [128, n], F8)
+    SCRATCH[name + "_s"] = ("sbuf", [128, n], "uint8")
+
+
+def _buf(name, n, ty="float32"):
+    SCRATCH[name] = ("sbuf", [128, n], ty)
+
+
+for _n, _w in (("qx", 130), ("qc", 128), ("qo", 128), ("qtri", 128), ("qs", 144), ("qw16", 128), ("qln", 136), ("qlf", 136),
+               ("qb1", 512), ("qb2", 512), ("qw", 128), ("qe", 512), ("qm", 512),
+               ("sf", 128), ("sn", 128), ("zn", 128), ("zf", 128),
+               ("v1n", 128), ("v1f", 128), ("v2n", 128), ("v2f", 128), ("rqn", 128), ("rqf", 128),
+               ("lv1", 384), ("lv2", 384), ("h1", 128), ("h2", 128), ("rz", 64), ("rv1", 64), ("rv2", 64)):
+    _codes(_n, _w)
+for _n, _w in (("xt", 520), ("zr", 512), ("zb", 544), ("xb", 608), ("sx", 576), ("b1t", 2048), ("b2t", 2048), ("wt", 512), ("onb", 520),
+               ("gp", 520), ("gm", 520), ("tri", 512), ("w16", 512), ("ir", 128), ("itr", 128), ("ik", 128), ("imx", 32), ("mxx", 32),
+               ("ict", 16), ("rst", 256), ("jk", 512), ("rtn", 512), ("rtf", 512), ("xw", 256), ("xtw", 288)):
+    _buf(_n, _w, "bfloat16")
+for _n, _w in (("pmn", 512), ("pmf", 512), ("cf", 32), ("c256", 8), ("tok", 1), ("pmc", 8), ("le", 16), ("g8", 8),
+               ("n4n", 4), ("n4f", 4), ("n4h", 4), ("xmn", 32), ("xmf", 32), ("zt", 16), ("san", 8), ("saf", 8),
+               ("nnn", 8), ("nnf", 8), ("rn", 4), ("lan", 16), ("wnt", 128), ("yt", 128)):
+    _buf(_n, _w)
+_buf("ip", 1, "int32")
+_buf("ic", 8, "int32")
+for _n, _w in (("offc", 2), ("offs", 16), ("offh", 8), ("off1n", 8), ("off1f", 8), ("off2n", 8), ("off2f", 8)):
+    _buf(_n, _w, "uint16")
+SCRATCH["sc"] = ("psum", [128, 2048], "float32")
+SCRATCH["dd"] = ("psum", [128, 2048], "float32")
+
+SEMAPHORES = (["ev", "es", "et", "ep", "sent", "st"] + ["l%d" % i for i in range(40)]
+              + ["azn", "azf", "hv1n", "hv1f", "hv2n", "hv2f", "hnn", "hnf"]
+              + ["rzc", "rzs", "r1c", "r1s", "rnc", "r2c", "r2s"])
+
+CAPP = 32
+FN = 4
+FM = 8
+FF = 4
+FR = 4
+BIG = -9e29
+M16, M32, M256 = 1.5 * 2.0 ** 27, 1.5 * 2.0 ** 28, 1.5 * 2.0 ** 31
+PLANS = {}
+HS0, HS1 = (0,), (1, 2, 3)
+ORDER = """
+qm2 qe0 qb1 qe1 qe3 qm3 N1.score qm0 N1.scan0 N1.scan1 N1.count0 qm1 N1.count1 F1.score qe2 N1.place0 N1.place1 N1.place2
+N1.place3 N1.place4 qb2 n.given N1.list N1.codes N1.scales n.minus F1.scan0 N1.parts F1.scan1 F1.count0 n.rest0 n.rest1 n.rest2
+n.rest3 n.repack F1.count1 F1.place0 F1.place1 N2.score F1.place2 N2.scan0 F1.place3 N2.count0 F1.place4 f.given N2.scan1
+N2.count1 F1.list F1.codes F1.scales f.minus N2.place0 N1.codesback N2.place1 N1.scalesback F1.parts N2.place2 f.rest0
+F1.codesback f.rest1 N2.place3 f.rest2 F1.number N1.number f.rest3 f.repack F1.scalesback N2.place4 F2.score N2.list N2.codes
+N2.parts N2.scales F2.scan0 F2.scan1 F2.count0 N2.number F2.count1 F2.place0 N2.scalesback F2.place1 N2.codesback F2.place2
+F2.place3 qw F2.place4 F2.list F2.scales F2.parts F2.codes n.nums F2.number F2.codesback F2.scalesback fin hl f.nums"""
+
+
+def plan(T, topo, core):
+    if core in PLANS:
+        return PLANS[core]
+    cs = list(T.cores)
+    here = [c for c in cs if c in topo.cores_of(core)]
+    plane = [c for c in cs if c not in here and topo.same_plane(core, c)]
+    far = [c for c in cs if c not in here and c not in plane]
+    g0 = [c for c in far if c in topo.cores_of(far[0])]
+    g1 = [c for c in far if c not in g0]
+    rel = [c for c in topo.cores_of(core) if c not in cs and topo.die(c) == topo.die(core)
+           and all(topo.may_write(c, d) for d in far)]
+    srel = []
+    for grp in (g0, g1):
+        cand = [c for c in range(256) if topo.mates(c, grp[0]) and topo.die(c) == topo.die(core) and topo.same_plane(core, c)
+                and all(topo.may_write(c, d) for d in grp)]
+        users = [c for c in cs if topo.same_plane(c, cand[0]) and topo.die(c) == topo.die(core)]
+        srel.append(cand[users.index(core)])
+    rk = T.rank_of
+    PLANS[core] = {"near": [[rk(c) for c in plane], [rk(c) for c in here]], "far": [[rk(c) for c in g0], [rk(c) for c in g1]],
+                   "codes": rel[:2], "scales": srel}
+    return PLANS[core]
+
+
+def bits(es):
+    m = 0
+    for e in es:
+        m |= 1 << e
+    return m
+
+
+def rank_program(g, core, T, topo):
+    if T.rank_of(core) is None:
+        relay_program(g, core, T, topo)
+    else:
+        home_program(g, core, T, topo)
+
+
+def xfer(T, topo, src, dst, engs, sem, out, in_):
+    rid, pid = topo.addr(dst, src)
+    return RemoteDMATransfer(dst_ids=[DstId(rid=rid, pnc=pid)], dma_engine_mask=bits(engs), remote_sem=T.sem[sem], src=in_, dst=out)
+
+
+def u8(T, name, a, b):
+    return T[name][:, a:b].bitcast(dt.uint8)
+
+
+def relay_program(g, core, T, topo):
+    src, grp, role = None, None, None
+    for c in T.cores:
+        p = plan(T, topo, c)
+        for i in range(2):
+            for k in ("codes", "scales"):
+                if p[k][i] == core:
+                    src, grp, role = T.rank_of(c), p["far"][i], k
+    if src is None:
+        return
+    sent = [0]
+
+    def hand(wait, sem, mk):
+        ts = []
+        g.wait_ge(T.sem[wait], FF)
+        for j, d in enumerate(grp):
+            dst = T.cores[d]
+            es = topo.engines(core, dst)[FR * j:FR * j + FR]
+            pd = plan(T, topo, dst)
+            at = (pd["far"][0] + pd["far"][1]).index(src)
+            out, in_ = mk(j, at)
+            ts.append(xfer(T, topo, core, dst, es, sem, out, in_))
+            sent[0] += FR
+        g.remote_dma_fused(ts, local_sem=T.sem.sent)
+
+    o = 32 * src
+    if role == "codes":
+        hand("rzc", "azf", lambda j, at: (u8(T, "zf", 32 * at, 32 * at + 32), u8(T, "rz", 32 * j, 32 * j + 32)))
+        hand("r1c", "hv1f", lambda j, at: (u8(T, "lv1", o, o + 32), u8(T, "rv1", 32 * j, 32 * j + 32)))
+        hand("r2c", "hv2f", lambda j, at: (u8(T, "lv2", o, o + 32), u8(T, "rv2", 32 * j, 32 * j + 32)))
+        hand("rnc", "hnf", lambda j, at: (T["lan"][:, 2 * src:2 * src + 2], T["rn"][:, 2 * j:2 * j + 2]))
+    else:
+        hand("rzs", "azf", lambda j, at: (T["zf_s"][:, 32 * at:32 * at + 32], T["rz_s"][:, 32 * j:32 * j + 32]))
+        hand("r1s", "hv1f", lambda j, at: (T["lv1_s"][:, o:o + 32], T["rv1_s"][:, 32 * j:32 * j + 32]))
+        hand("r2s", "hv2f", lambda j, at: (T["lv2_s"][:, o:o + 32], T["rv2_s"][:, 32 * j:32 * j + 32]))
+    g.wait_ge(T.sem.sent, sent[0])
+
+
+def home_program(g, core, T, topo):
+    me = T.rank_of(core)
+    pl = plan(T, topo, core)
+    queue = {"v": g.vector, "s": g.scalar, "t": g.tensor, "p": g, "y": g.sync}
+    engsem = {"v": "ev", "s": "es", "t": "et", "p": "ep"}
+    known = {e: {} for e in queue}
+    count = {e: 0 for e in queue}
+    total, waited, hist = {}, {}, {}
+    PS = ("sc", "dd")
+
+    def clash(a, b):
+        if a[1] >= b[2] or b[1] >= a[2]:
+            return False
+        s, t = (a[3] if len(a) > 3 else 1), (b[3] if len(b) > 3 else 1)
+        if s > 1 and s == t and a[1] % s != b[1] % s:
+            return False
+        return True
+
+    def need(e, reads, writes):
+        deps = []
+        for rs, wr in ((reads, False), (writes, True)):
+            for r in rs:
+                ps = r[0] in PS
+                for (q, qw, qe, ev, clk) in hist.get(r[0], []):
+                    if (wr or qw or (ps and qe != e)) and clash(r, q):
+                        if ps and e == "t" and qe == "t":
+                            continue
+                        deps.append((ev, clk))
+        best = {}
+        for ev, clk in deps:
+            if known[e].get(ev[0], 0) < ev[1] and (ev[0] not in best or best[ev[0]][0] < ev[1]):
+                best[ev[0]] = (ev[1], clk)
+        for s in list(best):
+            v = best[s][0]
+            if any(o != s and best[o][1].get(s, 0) >= v for o in best):
+                del best[s]
+        for s, (v, clk) in best.items():
+            queue[e].wait_ge(T.sem[s], v)
+            waited[s] = max(waited.get(s, 0), v)
+            for k2, v2 in clk.items():
+                known[e][k2] = max(known[e].get(k2, 0), v2)
+            known[e][s] = max(known[e].get(s, 0), v)
+
+    def note(e, reads, writes, ev, clk):
+        for r in reads:
+            hist.setdefault(r[0], []).append((r, False, e, ev, clk))
+        for r in writes:
+            hist.setdefault(r[0], []).append((r, True, e, ev, clk))
+
+    def op(e, call, reads, writes):
+        need(e, reads, writes)
+        count[e] += 1
+        ev = (engsem[e], count[e])
+        call().then_inc(T.sem[ev[0]], 1)
+        total[ev[0]] = count[e]
+        clk = dict(known[e])
+        clk[ev[0]] = ev[1]
+        note(e, reads, writes, ev, clk)
+
+    nl = [0]
+
+    def dma(e, out, in_, reads, writes, store=False):
+        need(e, reads, writes)
+        if store:
+            s = "st"
+        else:
+            s = "l%d" % nl[0]
+            nl[0] += 1
+        total[s] = total.get(s, 0) + 16
+        queue[e].dma_start(out, in_).then_inc(T.sem[s], 16)
+        if not store:
+            clk = dict(known[e])
+            clk[s] = 16
+            note(e, reads, writes, (s, 16), clk)
+
+    def arrive(sem, n, writes):
+        total[sem] = n
+        note("r", [], writes, (sem, n), {sem: n})
+
+    def fused(reads, parts):
+        need("p", reads, [])
+        ts = [xfer(T, topo, core, d, es, sem, out, in_) for (d, es, sem, out, in_) in parts]
+        total["sent"] = total.get("sent", 0) + sum(len(p[1]) for p in parts)
+        g.remote_dma_fused(ts, local_sem=T.sem.sent)
+
+    def ap(r):
+        return T[r[0]][:, r[1]:r[2]:r[3]] if len(r) > 3 and r[3] > 1 else T[r[0]][:, r[1]:r[2]]
+
+    def isr(x):
+        return isinstance(x, tuple)
+
+    def vcopy(o, i):
+        op("v", lambda: g.vector.tensor_copy(ap(o), ap(i)), [i], [o])
+
+    def vset(o, c):
+        op("v", lambda: g.vector.memset(ap(o), c), [], [o])
+
+    def vts(o, i, s1, s2, op0, op1=None):
+        rd = [i] + [s for s in (s1, s2) if isr(s)]
+        a1 = ap(s1) if isr(s1) else s1
+        a2 = ap(s2) if isr(s2) else s2
+        if op1 is None:
+            op("v", lambda: g.vector.tensor_scalar(ap(o), ap(i), a1, None, op0), rd, [o])
+        else:
+            op("v", lambda: g.vector.tensor_scalar(ap(o), ap(i), a1, a2, op0, op1), rd, [o])
+
+    def vtt(o, a, b, o0):
+        op("v", lambda: g.vector.tensor_tensor(ap(o), ap(a), ap(b), o0), [a, b], [o])
+
+    def vscan(o, d0, d1, init, o0, o1):
+        op("v", lambda: g.vector.tensor_tensor_scan(ap(o), ap(d0), ap(d1), init, o0, o1), [d0, d1], [o])
+
+    def vtr(o, i):
+        op("v", lambda: g.vector.transpose(ap(o), ap(i)), [i], [o])
+
+    def vsum(o, i):
+        op("v", lambda: g.vector.tensor_reduce(ap(o), ap(i), AxisListType.X, OP.add), [i], [o])
+
+    def quant(o, n0, i):
+        w = (i[2] - i[1]) // 4
+        a, b = (o, n0, n0 + w), (o + "_s", n0, n0 + w)
+        op("v", lambda: g.vector.quantize_mx(ap(a), ap(b), ap(i)), [i], [a, b])
+
+    def act(o, i, f, bias=None, scale=None, acc=None):
+        rd, kw, wr = [i], {}, [o]
+        if bias is not None:
+            kw["bias"] = ap(bias) if isr(bias) else bias
+            if isr(bias):
+                rd.append(bias)
+        if scale is not None:
+            kw["scale"] = ap(scale) if isr(scale) else scale
+            if isr(scale):
+                rd.append(scale)
+        if acc is not None:
+            kw["accum_out"] = ap(acc)
+            wr.append(acc)
+        op("s", lambda: g.scalar.activation(ap(o), ap(i), f, **kw), rd, wr)
+
+    def pick_codes(o, o0, win, w1, off, c0, c1):
+        oc, wc, of = (o, o0, o0 + 16 * (c1 - c0)), (win, 0, w1), (off, c0, c1)
+        op("v", lambda: g.vector.tensor_copy(ap(oc).bitcast(dt.uint32), ap(wc).bitcast(dt.uint32).indirect(ap(of))), [wc, of], [oc])
+
+    def pick_scales(o, o0, win, w1, off, c0, c1):
+        osn, ws, of = (o + "_s", o0, o0 + 16 * (c1 - c0)), (win + "_s", 0, w1), (off, c0, c1)
+        op("s", lambda: g.scalar.activation(ap(osn), ap(ws).indirect(ap(of)), AF.Copy), [ws, of], [osn])
+
+    def pick(*a):
+        pick_codes(*a)
+        pick_scales(*a)
+
+    def mm(ps, bank, l, l0, r, r0, start=True, stop=True, n=128):
+        o = (ps, 512 * bank, 512 * bank + n)
+        a, sa, b, sb = (l, l0, l0 + 128), (l + "_s", l0, l0 + 128), (r, r0, r0 + n), (r + "_s", r0, r0 + n)
+        op("t", lambda: g.tensor.matmul_mx(ap(o), ap(a), ap(sa), ap(b), ap(sb), start, stop), [a, sa, b, sb], [(ps, 512 * bank, 512 * bank + 512)])
+
+    dma("y", T.xt[:, 0:512], T.x[:], [], [("xt", 0, 512)])
+    dma("s", T.zb[:, 0:32], T.co[:, 0:32], [], [("zb", 0, 32)])
+    dma("y", T.wt[:], T.w[:], [], [("wt", 0, 512)])
+
+    def book(b, hs=range(4)):
+        for h in hs:
+            act((b + "t", 512 * h, 512 * h + 512), ("zr", 0, 512), AF.Copy)
+        for h in hs:
+            dma("y", T[b + "t"][32 * h:32 * h + 32, 512 * h:512 * h + 512], T[b][32 * h:32 * h + 32, :], [], [(b + "t", 512 * h, 512 * h + 512)])
+
+    near, far = pl["near"][0] + pl["near"][1], pl["far"][0] + pl["far"][1]
+    own = near.index(me)
+
+    def both(n, a, b):
+        return [(n, a, b), (n + "_s", a, b)]
+
+    nw, hw1, hw2, nn_ = [], [], [], []
+    for k, r in enumerate(near):
+        if r != me:
+            nw += both("zn", 32 * k, 32 * k + 32)
+            hw1 += both("lv1", 32 * r, 32 * r + 32)
+            hw2 += both("lv2", 32 * r, 32 * r + 32)
+            nn_.append(("lan", 2 * r, 2 * r + 2))
+    from_near = 2 * FN + FM
+    arrive("azn", 2 * from_near, nw)
+    arrive("hv1n", 2 * from_near, hw1)
+    arrive("hv2n", 2 * from_near, hw2)
+    arrive("hnn", from_near, nn_)
+    arrive("azf", 4 * 2 * FR, both("zf", 0, 128))
+    hw1, hw2, nn_ = [], [], []
+    for r in far:
+        hw1 += both("lv1", 32 * r, 32 * r + 32)
+        hw2 += both("lv2", 32 * r, 32 * r + 32)
+        nn_.append(("lan", 2 * r, 2 * r + 2))
+    arrive("hv1f", 4 * 2 * FR, hw1)
+    arrive("hv2f", 4 * 2 * FR, hw2)
+    arrive("hnf", 4 * FR, nn_)
+
+    def iota(o, pat, base, cm):
+        if o[0] == "ip":
+            op("p", lambda: g.iota(ap(o), pat, base, cm), [], [o])
+        else:
+            op("p", lambda: g.iota(ap(o), pat, base, cm, allow_small_or_imprecise_dtypes=True), [], [o])
+
+    def C(k):
+        return ("cf", k, k + 1)
+    R16, HQ, U1, P16, P3, E0, HQ128, CHI, CLO, G, FH, T0, T1, T2, T3, T4, T5 = [C(k) for k in range(17)]
+    TOK = ("tok", 0, 1)
+    pf = [q[0] // 2 for q in pl["far"]]
+    pn = [q[0] // 2 for q in pl["near"]]
+    iota(("c256", 0, 8), [[256, 8]], 0, 0)
+    iota(TOK, [[0, 1]], 0, 1)
+    iota(("itr", 0, 128), [[1, 128]], 0, 0)
+    iota(("ir", 0, 128), [[0, 8], [2, 16]], -15, 0)
+    iota(("ict", 0, 8), [[512 * (pf[1] - pf[0]), 2], [256, 2], [32, 2]], 512 * pf[0], 0)
+    iota(("ict", 8, 16), [[512 * (pn[1] - pn[0]), 2], [256, 2], [32, 2]], 512 * pn[0], 0)
+    iota(("ip", 0, 1), [[1, 1]], 0, 1)
+    iota(("ik", 0, 128), [[0, 2], [1, 16], [64, 4]], 0, 0)
+    iota(("imx", 0, 32), [[1, 8], [0, 4]], 0, 0)
+
+    vset(("zr", 0, 512), 0.0)
+    act(("zb", 32, 544), ("zr", 0, 512), AF.Copy)
+    book("b1")
+    book("b2", HS0)
+    vset(("xt", 512, 520), 0.0)
+    vset(("le", 0, 1), 0.0)
+    vset(("zt", 0, 16), 0.0)
+    vset(("onb", 0, 520), 1.0)
+    op("p", lambda: g.affine_select(T.gp[:, 0:520], T.onb[:, 0:520], [[-1, 520]], OP.is_equal, 0.0, 3, 4),
+       [("onb", 0, 520)], [("gp", 0, 520)])
+    vts(T0, TOK, -128.0, None, OP.add)
+    vts(CHI, T0, M16, M16, OP.add, OP.subtract)
+    vtt(CLO, T0, CHI, OP.subtract)
+    vts(("tri", 0, 512, 4), ("itr", 0, 128), TOK, 2.0, OP.is_gt, OP.mult)
+    vts(("tri", 1, 512, 4), ("itr", 0, 128), TOK, None, OP.is_equal)
+    vset(("zb", 514, 544, 4), -15.0)
+    vcopy(("zb", 513, 544, 4), ("c256", 0, 8))
+    quant("qc", 0, ("zb", 0, 512))
+    vts(("tri", 2, 512, 4), ("itr", 0, 128), TOK, None, OP.is_equal)
+    vset(("tri", 3, 512, 4), 0.0)
+
+    quant("qx", 0, ("xt", 0, 520))
+    mm("sc", 0, "qx", 0, "qc", 0)
+    quant("qtri", 0, ("tri", 0, 512))
+    vscan(("pmc", 0, 8), ("zt", 0, 8), ("sc", 0, 8), BIG, OP.add, OP.max)
+    vts(("le", 1, 9), ("pmc", 0, 8), ("pmc", 7, 8), None, OP.is_ge)
+    vtt(("zb", 512, 544, 4), ("le", 1, 9), ("le", 0, 8), OP.subtract)
+    quant("qo", 0, ("zb", 32, 544))
+    mm("sc", 1, "qtri", 0, "qo", 0)
+    for l in ("lv1", "lv2"):
+        dma("y", u8(T, l, 256, 258), u8(T, "qx", 128, 130), [("qx", 128, 130)], [(l, 256, 258)])
+        dma("y", T[l + "_s"][:, 256:258], T["qx_s"][:, 128:130], [("qx_s", 128, 130)], [(l + "_s", 256, 258)])
+    vset(("sx", 2, 576, 4), 0.0)
+    vset(("sx", 3, 576, 4), 0.0)
+    vtt(("g8", 0, 8), ("zb", 512, 544, 4), ("sc", 632, 640), OP.mult)
+    vsum(G, ("g8", 0, 8))
+    vts(FH, G, M32, M32, OP.add, OP.subtract)
+    vts(("sx", 0, 512, 4), ("ir", 0, 128), FH, G, OP.add, OP.is_equal)
+    vts(("sx", 1, 512, 4), ("ir", 0, 128), FH, G, OP.add, OP.is_equal)
+    vts(("sx", 512, 576, 4), ("ict", 0, 16), FH, CHI, OP.is_equal, OP.mult)
+    vts(("sx", 513, 576, 4), ("ict", 0, 16), FH, CLO, OP.is_equal, OP.mult)
+    quant("qs", 0, ("sx", 0, 576))
+    mm("sc", 2, "qs", 0, "qs", 16)
+    vset(("rst", 0, 256), 0.0)
+    vts(("offs", 0, 16), ("sc", 1136, 1152), 128.0, None, OP.add)
+
+    def to_relays(kind, buf, w, dstbuf, sem):
+        codes = SCRATCH[buf][2] == F8
+        parts = []
+        for i, rc in enumerate(pl[kind]):
+            es = topo.engines(core, rc)
+            k = (len(es) - 2 * FF) + FF * i
+            if codes:
+                parts.append((rc, es[k:k + FF], sem, u8(T, dstbuf, 0, w), u8(T, buf, w * i, w * i + w)))
+            else:
+                parts.append((rc, es[k:k + FF], sem, T[dstbuf][:, 0:w], T[buf][:, w * i:w * i + w]))
+        fused([(buf, 0, 2 * w)], parts)
+
+    def to_near(buf, w, dstbuf, place, sem):
+        codes = SCRATCH[buf][2] == F8
+        parts = []
+        for k, d in enumerate(near):
+            if d == me:
+                continue
+            a, dc, n = place(d), T.cores[d], len(parts)
+            es = topo.engines(core, dc)
+            es = es[len(es) - FM:] if d in pl["near"][1] else es[FN * n:FN * n + FN]
+            if codes:
+                parts.append((dc, es, sem, u8(T, dstbuf, a, a + w), u8(T, buf, w * k, w * k + w)))
+            else:
+                parts.append((dc, es, sem, T[dstbuf][:, a:a + w], T[buf][:, w * k:w * k + w]))
+        fused([(buf, 0, 4 * w)], parts)
+
+    pick("sf", 0, "qx", 130, "offs", 0, 8)
+    to_relays("codes", "sf", 64, "rz", "rzc")
+    to_relays("scales", "sf_s", 64, "rz_s", "rzs")
+    pick("sn", 0, "qx", 130, "offs", 8, 16)
+
+    def at_near(d):
+        p = plan(T, topo, T.cores[d])
+        return 32 * (p["near"][0] + p["near"][1]).index(me)
+    to_near("sn", 32, "zn", at_near, "azn")
+    to_near("sn_s", 32, "zn_s", at_near, "azn")
+
+    def keep(dst, d0, src, s0):
+        dma("y", u8(T, dst, d0, d0 + 32), u8(T, src, s0, s0 + 32), [(src, s0, s0 + 32)], [(dst, d0, d0 + 32)])
+        dma("y", T[dst + "_s"][:, d0:d0 + 32], T[src + "_s"][:, s0:s0 + 32], [(src + "_s", s0, s0 + 32)], [(dst + "_s", d0, d0 + 32)])
+    keep("zn", 32 * own, "sn", 32 * own)
+    book("b2", HS1)
+    act(("gm", 0, 520), ("gp", 0, 520), AF.Copy, scale=-1.0)
+
+    for k, (sh, m) in enumerate(((0, 15), (5, 7), (4, 1), (4, 7), (0, 3))):
+        o = ("ic", k, k + 1)
+        if sh:
+            vts(o, ("ip", 0, 1), sh, m, OP.arith_shift_right, OP.bitwise_and)
+        else:
+            vts(o, ("ip", 0, 1), m, None, OP.bitwise_and)
+    vcopy(("cf", 0, 5), ("ic", 0, 5))
+    vts(HQ128, HQ, 128.0, None, OP.mult)
+    vts(E0, U1, -1.0, 1.0, OP.mult, OP.add)
+    vset(("rst", 0, 256, 128), BIG)
+    for h in range(4):
+        vts(("w16", 128 * h, 128 * h + 128), ("ik", 0, 128), -64.0 * h, R16, OP.add, OP.is_equal)
+    quant("qw16", 0, ("w16", 0, 512))
+    vts(("mxx", 0, 32), ("imx", 0, 32), P16, None, OP.is_equal)
+    vts(("offc", 0, 2), ("zt", 0, 2), P3, None, OP.add)
+    vset(("xb", 64, 544), 0.0)
+
+    def relocate(x, n4, bank):
+        ql, v = "ql" + x, (544 if x == "n" else 0)
+        o, w, f, m = ("xm" + x, 0, 32), (n4, 0, 4), ("offc", 0, 2), ("mxx", 0, 32)
+        a = 64 if x == "n" else 0
+        k = 512 * bank + (120 if x == "n" else 0)
+
+        def spread():
+            op("v", lambda: g.vector.tensor_tensor(ap(o), ap(w).indirect(ap(f)), ap(m), OP.mult), [w, f, m], [o])
+
+        def products():
+            mm("sc", bank, "qw16", 0, ql, 0, True, False)
+            mm("sc", bank, "qw16", 0, ql, 8, False, True)
+        return (spread, lambda: vts(("xb", v, v + 32), o, M16, M16, OP.add, OP.subtract),
+                lambda: vtt(("xb", v + 32, v + 64), o, ("xb", v, v + 32), OP.subtract),
+                lambda: quant(ql, 0, ("xb", a, a + 544)), products), ("sc", k, k + 8)
+
+    def home_list():
+        vts(T0, G, -112.0, M256, OP.add, OP.add)
+        vts(T1, T0, M256, 0.25, OP.subtract, OP.mult)
+        vts(T2, T1, -4.0, G, OP.mult, OP.add)
+        vts(T3, T2, 2.0 * CAPP - 16, 0.5, OP.is_lt, OP.mult)
+        vts(T4, T2, T1, 15.0 - 512.0, OP.add, OP.add)
+        vtt(T5, T4, T3, OP.mult)
+        vts(("n4h", 0, 4), ("zt", 0, 4), T5, None, OP.add)
+        fs, ls = relocate("n", "n4h", 3)
+        for f in fs:
+            f()
+        vts(("offh", 0, 8), ls, 256.0, None, OP.add)
+
+    def level(x, l):
+        win, bk, pm, n4, nn, off, sa = ("z" if l == 1 else "rq") + x, "qb%d" % l, "pm" + x, "n4" + x, "nn" + x, "off%d%s" % (l, x), "sa" + x
+        b0 = 0 if x == "n" else 2
+        fs, ls = relocate(x, n4, b0)
+        a, b = ls[1], ls[2]
+        v = ("v%d%s" % (l, x), 0, bk, 512, off, 0, 8)
+
+        def score():
+            for i in range(2):
+                mm("sc", b0 + i, win, 0, bk, 256 * i, True, True, 256)
+
+        def scan(i):
+            k = 512 * (b0 + i)
+            vscan((pm, 256 * i, 256 * i + 256), ("rst", 0, 256), ("sc", k, k + 256), 0.0, OP.add, OP.max)
+
+        def tally(i):
+            for h in range(2 * i, 2 * i + 2):
+                act(("jk", 128 * h, 128 * h + 128), (pm, 128 * h, 128 * h + 128), AF.Sign, bias=(pm, 128 * h + 127, 128 * h + 128),
+                    scale=-1.0, acc=(n4, h, h + 1))
+
+        def parts():
+            act((sa, 0, 4), ("sc", a, b, 2), AF.Copy, scale=E0)
+            act((sa, 4, 8), ("sc", a + 1, b, 2), AF.Copy, scale=U1)
+
+        d = {"place%d" % i: f for i, f in enumerate(fs)}
+        for i in range(2):
+            d.update({"scan%d" % i: lambda i=i: scan(i), "count%d" % i: lambda i=i: tally(i)})
+        d.update({"score": score, "list": lambda: vts((off, 0, 8), ls, HQ128, None, OP.add), "codes": lambda: pick_codes(*v),
+                  "scales": lambda: pick_scales(*v), "parts": parts,
+                  "number": lambda: vtt((nn, l - 1, 8, 2), (sa, 0, 4), (sa, 4, 8), OP.add),
+                  "codesback": lambda: back(x, l, True), "scalesback": lambda: back(x, l, False)})
+        return d
+
+    def back(x, l, codes):
+        v, lv = "v%d%s" % (l, x), "lv%d" % l
+        if x == "f" and codes:
+            to_relays("codes", v, 64, "rv%d" % l, "r%dc" % l)
+        elif x == "f":
+            to_relays("scales", v + "_s", 64, "rv%d_s" % l, "r%ds" % l)
+        elif codes:
+            to_near(v, 32, lv, lambda d: 32 * me, "hv%dn" % l)
+        else:
+            to_near(v + "_s", 32, lv + "_s", lambda d: 32 * me, "hv%dn" % l)
+            keep(lv, 32 * me, v, 32 * own)
+
+    def given(x):
+        for b in range(4):
+            mm("dd", b, "qe", 128 * b, "z" + x, 0, True, False)
+
+    def minus(x):
+        for b in range(4):
+            mm("dd", b, "qm", 128 * b, "v1" + x, 0, False, True)
+
+    def rest(x, b):
+        o, i = ("rt" + x, b, 512, 4), ("dd", 512 * b, 512 * b + 128)
+        if b % 2:
+            act(o, i, AF.Copy)
+        else:
+            vcopy(o, i)
+
+    def near_numbers():
+        to_near("nnn", 2, "lan", lambda d: 2 * me, "hnn")
+        dma("y", T.lan[:, 2 * me:2 * me + 2], T.nnn[:, 2 * own:2 * own + 2], [("nnn", 2 * own, 2 * own + 2)], [("lan", 2 * me, 2 * me + 2)])
+
+    def last():
+        vset(("xw", 0, 256), 0.0)
+        vset(("xtw", 256, 288), -1.0)
+
+    def steps():
+        d = {}
+        for x in "nf":
+            for l in (1, 2):
+                d.update({"%s%d.%s" % (x.upper(), l, n): f for n, f in level(x, l).items()})
+            d.update({x + ".given": lambda x=x: given(x), x + ".minus": lambda x=x: minus(x),
+                      x + ".repack": lambda x=x: quant("rq" + x, 0, ("rt" + x, 0, 512))})
+            for b in range(4):
+                d[x + ".rest%d" % b] = lambda x=x, b=b: rest(x, b)
+        for b in range(4):
+            d["qe%d" % b] = lambda b=b: quant("qe", 128 * b, ("gp", 3 - b, 515 - b))
+            d["qm%d" % b] = lambda b=b: quant("qm", 128 * b, ("gm", 3 - b, 515 - b))
+        d.update({"hl": home_list, "fin": last,
+                  "qb1": lambda: quant("qb1", 0, ("b1t", 0, 2048)), "qb2": lambda: quant("qb2", 0, ("b2t", 0, 2048)),
+                  "qw": lambda: quant("qw", 0, ("wt", 0, 512)), "f.nums": lambda: to_relays("codes", "nnf", 4, "rn", "rnc"),
+                  "n.nums": near_numbers})
+        return d
+
+    todo = steps()
+    for name in ORDER.split():
+        todo[name]()
+
+    def store(l):
+        h = "h%d" % l
+        o = 128 * (l - 1)
+        dma("y", T.oc[:, 4 * o:4 * o + 512], u8(T, h, 0, 128), [(h, 0, 128)], [], True)
+        for k in range(4):
+            dma("y" if k % 2 else "s", T.osc[4 * k:4 * k + 4, o:o + 128], T[h + "_s"][32 * k:32 * k + 4, 0:128], [(h + "_s", 0, 128)], [], True)
+
+    pick("h1", 0, "lv1", 258, "offh", 0, 8)
+    store(1)
+    mm("sc", 3, "qw", 0, "h1", 0, True, False)
+    pick("h2", 0, "lv2", 258, "offh", 0, 8)
+    mm("sc", 3, "qw", 0, "h2", 0, False, True)
+    store(2)
+    for l in range(2):
+        vcopy(("xw", l, 256, 32), ("lan", l, 16, 2))
+    vtr(("xtw", 0, 256), ("xw", 0, 256))
+    act(("yt", 0, 128), ("sc", 1536, 1664), AF.Copy)
+    dma("s", T.y[:], T.yt[:], [("yt", 0, 128)], [], True)
+    o, w, f = ("wnt", 0, 128), ("xtw", 0, 288), ("offh", 0, 8)
+    op("v", lambda: g.vector.tensor_copy(ap(o), ap(w).indirect(ap(f))), [w, f], [o])
+    for l in range(2):
+        dma("ys"[l], T.wn[4 * l:4 * l + 4, :], T.wnt[l:128:32, 0:128], [o], [], True)
+    for s in total:
+        if waited.get(s, 0) < total[s]:
+            g.wait_ge(T.sem[s], total[s])

@@ -1,5 +1,5 @@
 from concourse.bass import DstId, RemoteDMATransfer
-from concourse.mybir import dt, AluOpType, AxisListType, ActivationFunctionType
+from concourse.mybir import dt, AluOpType, ActivationFunctionType
 
 OP = AluOpType
 AF = ActivationFunctionType
@@ -24,14 +24,14 @@ for _n, _w in (("qx", 130), ("qc", 128), ("qo", 128), ("qtri", 128), ("qs", 144)
                ("lv1", 384), ("lv2", 384), ("h1", 128), ("h2", 128), ("rz", 64), ("rv1", 64), ("rv2", 64)):
     _codes(_n, _w)
 for _n, _w in (("xt", 520), ("zr", 512), ("zb", 544), ("xb", 608), ("sx", 576), ("b1t", 2048), ("b2t", 2048), ("wt", 512), ("onb", 520),
-               ("gp", 520), ("gm", 520), ("tri", 512), ("w16", 512), ("ir", 128), ("itr", 128), ("ik", 128), ("imx", 32), ("mxx", 32),
-               ("ict", 16), ("rst", 256), ("jk", 512), ("rtn", 512), ("rtf", 512), ("xw", 256), ("xtw", 288)):
+               ("gp", 520), ("gm", 520), ("tri", 512), ("w16", 512), ("ir", 256), ("itr", 128), ("ik", 128), ("imx", 2),
+               ("nbn", 8), ("nbf", 8), ("rn", 8),
+               ("ict", 16), ("jk", 512), ("rtn", 512), ("rtf", 512), ("xw", 256), ("xtw", 288)):
     _buf(_n, _w, "bfloat16")
-for _n, _w in (("pmn", 512), ("pmf", 512), ("cf", 32), ("c256", 8), ("tok", 1), ("pmc", 8), ("le", 16), ("g8", 8),
-               ("n4n", 4), ("n4f", 4), ("n4h", 4), ("xmn", 32), ("xmf", 32), ("zt", 16), ("san", 8), ("saf", 8),
-               ("nnn", 8), ("nnf", 8), ("rn", 4), ("lan", 16), ("wnt", 128), ("yt", 128)):
+for _n, _w in (("pmn", 512), ("pmf", 512), ("cf", 32), ("c256", 8), ("tok", 1), ("pmc", 8), ("g8", 8),
+               ("n4n", 16), ("n4f", 16), ("n4h", 16), ("zt", 16), ("eq", 2), ("wnt", 128), ("yt", 128)):
     _buf(_n, _w)
-_buf("ip", 1, "int32")
+_buf("ip", 2, "int32")
 _buf("ic", 8, "int32")
 for _n, _w in (("offc", 2), ("offs", 16), ("offh", 8), ("off1n", 8), ("off1f", 8), ("off2n", 8), ("off2f", 8)):
     _buf(_n, _w, "uint16")
@@ -50,15 +50,17 @@ FR = 4
 BIG = -9e29
 M16, M32, M256 = 1.5 * 2.0 ** 27, 1.5 * 2.0 ** 28, 1.5 * 2.0 ** 31
 PLANS = {}
-HS0, HS1 = (0,), (1, 2, 3)
 ORDER = """
-qm2 qe0 qb1 qe1 qe3 qm3 N1.score qm0 N1.scan0 N1.scan1 N1.count0 qm1 N1.count1 F1.score qe2 N1.place0 N1.place1 N1.place2
-N1.place3 N1.place4 qb2 n.given N1.list N1.codes N1.scales n.minus F1.scan0 N1.parts F1.scan1 F1.count0 n.rest0 n.rest1 n.rest2
-n.rest3 n.repack F1.count1 F1.place0 F1.place1 N2.score F1.place2 N2.scan0 F1.place3 N2.count0 F1.place4 f.given N2.scan1
-N2.count1 F1.list F1.codes F1.scales f.minus N2.place0 N1.codesback N2.place1 N1.scalesback F1.parts N2.place2 f.rest0
-F1.codesback f.rest1 N2.place3 f.rest2 F1.number N1.number f.rest3 f.repack F1.scalesback N2.place4 F2.score N2.list N2.codes
-N2.parts N2.scales F2.scan0 F2.scan1 F2.count0 N2.number F2.count1 F2.place0 N2.scalesback F2.place1 N2.codesback F2.place2
-F2.place3 qw F2.place4 F2.list F2.scales F2.parts F2.codes n.nums F2.number F2.codesback F2.scalesback fin hl f.nums"""
+zr zb zt onb xt k15 k256 tri1 tri3 tri0 qc b10 qx sx0 gp chi cells tri2 top qtri n4f from0 from1 b20 qo wt earlier n4h zeros clo G FH
+sx3 sx2 b21 sx1 b13 b23 qs hq b12 r16 b11 b22 lists offs sf.s n4n sf.c sn.c p16 cf qe2 f.c gm w160 e0 w163 own qe3 w162 qb1 f.s n.c
+qm0 w161 qm1 qe0 sn.s qm2 n.s qw16 eq xb qe1 offc N1.score N1.scan0 N1.scan1 N1.scan2 N1.count0 n.given N1.count1 N1.count2 hl0
+N1.scan3 N1.count3 qm3 N1.place0 N1.place1 N1.place2 qb2 N1.place3 N1.list N1.codes F1.score N1.scales F1.scan0 F1.scan1 F1.scan3
+n.minus F1.count0 n.rest0 n.rest2 F1.count1 n.rest1 n.rest3 F1.count3 F1.scan2 n.repack F1.count2 F1.place0 hl1 f.given N1.number
+F1.place1 N2.score N2.scan1 N2.count1 F1.place2 N2.scan0 N1.codesback N2.count0 N2.scan3 N1.scalesback N2.scan2 F1.place3 F1.list
+N2.count3 N2.count2 F1.codes N2.place0 qw hl2 F1.scales N2.place1 F1.codesback F1.scalesback f.minus f.rest1 N2.place2 f.rest0
+f.rest2 f.rest3 F1.number N2.place3 f.repack N2.number n.nums F2.score F2.scan0 F2.scan1 F2.count0 F2.scan2 F2.count1 F2.count2
+F2.scan3 F2.count3 F2.number f.nums hl3 hl4 F2.place0 F2.place1 F2.place2 F2.place3 N2.list hl5 N2.codes F2.list N2.scales
+F2.scales F2.codes hl6 F2.codesback F2.scalesback N1.own fin N2.own hl7 hl8 hl9 N2.scalesback N2.codesback hl10"""
 
 
 def plan(T, topo, core):
@@ -79,8 +81,8 @@ def plan(T, topo, core):
         users = [c for c in cs if topo.same_plane(c, cand[0]) and topo.die(c) == topo.die(core)]
         srel.append(cand[users.index(core)])
     rk = T.rank_of
-    PLANS[core] = {"near": [[rk(c) for c in plane], [rk(c) for c in here]], "far": [[rk(c) for c in g0], [rk(c) for c in g1]],
-                   "codes": rel[:2], "scales": srel}
+    PLANS[core] = {"near": sorted([[rk(c) for c in plane], [rk(c) for c in here]]), "here": [rk(c) for c in here],
+                   "far": [[rk(c) for c in g0], [rk(c) for c in g1]], "codes": rel[:2], "scales": srel}
     return PLANS[core]
 
 
@@ -136,8 +138,8 @@ def relay_program(g, core, T, topo):
     if role == "codes":
         hand("rzc", "azf", lambda j, at: (u8(T, "zf", 32 * at, 32 * at + 32), u8(T, "rz", 32 * j, 32 * j + 32)))
         hand("r1c", "hv1f", lambda j, at: (u8(T, "lv1", o, o + 32), u8(T, "rv1", 32 * j, 32 * j + 32)))
+        hand("rnc", "hnf", lambda j, at: (T["xw"][:, o:o + 8], T["rn"][:, 0:8]))
         hand("r2c", "hv2f", lambda j, at: (u8(T, "lv2", o, o + 32), u8(T, "rv2", 32 * j, 32 * j + 32)))
-        hand("rnc", "hnf", lambda j, at: (T["lan"][:, 2 * src:2 * src + 2], T["rn"][:, 2 * j:2 * j + 2]))
     else:
         hand("rzs", "azf", lambda j, at: (T["zf_s"][:, 32 * at:32 * at + 32], T["rz_s"][:, 32 * j:32 * j + 32]))
         hand("r1s", "hv1f", lambda j, at: (T["lv1_s"][:, o:o + 32], T["rv1_s"][:, 32 * j:32 * j + 32]))
@@ -260,9 +262,6 @@ def home_program(g, core, T, topo):
     def vtr(o, i):
         op("v", lambda: g.vector.transpose(ap(o), ap(i)), [i], [o])
 
-    def vsum(o, i):
-        op("v", lambda: g.vector.tensor_reduce(ap(o), ap(i), AxisListType.X, OP.add), [i], [o])
-
     def quant(o, n0, i):
         w = (i[2] - i[1]) // 4
         a, b = (o, n0, n0 + w), (o + "_s", n0, n0 + w)
@@ -302,13 +301,10 @@ def home_program(g, core, T, topo):
 
     dma("y", T.xt[:, 0:512], T.x[:], [], [("xt", 0, 512)])
     dma("s", T.zb[:, 0:32], T.co[:, 0:32], [], [("zb", 0, 32)])
-    dma("y", T.wt[:], T.w[:], [], [("wt", 0, 512)])
 
-    def book(b, hs=range(4)):
-        for h in hs:
-            act((b + "t", 512 * h, 512 * h + 512), ("zr", 0, 512), AF.Copy)
-        for h in hs:
-            dma("y", T[b + "t"][32 * h:32 * h + 32, 512 * h:512 * h + 512], T[b][32 * h:32 * h + 32, :], [], [(b + "t", 512 * h, 512 * h + 512)])
+    def book(b, h):
+        act((b + "t", 512 * h, 512 * h + 512), ("zr", 0, 512), AF.Copy)
+        dma("y", T[b + "t"][32 * h:32 * h + 32, 512 * h:512 * h + 512], T[b][32 * h:32 * h + 32, :], [], [(b + "t", 512 * h, 512 * h + 512)])
 
     near, far = pl["near"][0] + pl["near"][1], pl["far"][0] + pl["far"][1]
     own = near.index(me)
@@ -322,7 +318,7 @@ def home_program(g, core, T, topo):
             nw += both("zn", 32 * k, 32 * k + 32)
             hw1 += both("lv1", 32 * r, 32 * r + 32)
             hw2 += both("lv2", 32 * r, 32 * r + 32)
-            nn_.append(("lan", 2 * r, 2 * r + 2))
+            nn_.append(("xw", 32 * r, 32 * r + 8))
     from_near = 2 * FN + FM
     arrive("azn", 2 * from_near, nw)
     arrive("hv1n", 2 * from_near, hw1)
@@ -333,7 +329,7 @@ def home_program(g, core, T, topo):
     for r in far:
         hw1 += both("lv1", 32 * r, 32 * r + 32)
         hw2 += both("lv2", 32 * r, 32 * r + 32)
-        nn_.append(("lan", 2 * r, 2 * r + 2))
+        nn_.append(("xw", 32 * r, 32 * r + 8))
     arrive("hv1f", 4 * 2 * FR, hw1)
     arrive("hv2f", 4 * 2 * FR, hw2)
     arrive("hnf", 4 * FR, nn_)
@@ -346,67 +342,83 @@ def home_program(g, core, T, topo):
 
     def C(k):
         return ("cf", k, k + 1)
-    R16, HQ, U1, P16, P3, E0, HQ128, CHI, CLO, G, FH, T0, T1, T2, T3, T4, T5 = [C(k) for k in range(17)]
+    R16, HQ128, P16, E0, CHI, CLO, FH, T0, T1, T2, T3, T4, T5 = [C(k) for k in range(13)]
+    G = ("g8", 7, 8)
     TOK = ("tok", 0, 1)
     pf = [q[0] // 2 for q in pl["far"]]
     pn = [q[0] // 2 for q in pl["near"]]
-    iota(("c256", 0, 8), [[256, 8]], 0, 0)
+    iota(("c256", 0, 8), [[-256, 8]], 2048, 0)
     iota(TOK, [[0, 1]], 0, 1)
+    iota(T0, [[0, 1]], -128, 1)
     iota(("itr", 0, 128), [[1, 128]], 0, 0)
-    iota(("ir", 0, 128), [[0, 8], [2, 16]], -15, 0)
-    iota(("ict", 0, 8), [[512 * (pf[1] - pf[0]), 2], [256, 2], [32, 2]], 512 * pf[0], 0)
-    iota(("ict", 8, 16), [[512 * (pn[1] - pn[0]), 2], [256, 2], [32, 2]], 512 * pn[0], 0)
+    iota(("ir", 0, 256), [[0, 8], [2, 16], [0, 2]], -15, 0)
+    iota(("ict", 0, 8), [[-512 * (pf[1] - pf[0]), 2], [-256, 2], [32, 2]], 2048 - 512 * pf[0], 0)
+    iota(("ict", 8, 16), [[-512 * (pn[1] - pn[0]), 2], [-256, 2], [32, 2]], 2048 - 512 * pn[0], 0)
     iota(("ip", 0, 1), [[1, 1]], 0, 1)
+    iota(("ip", 1, 2), [[1, 1]], 0, 4)
     iota(("ik", 0, 128), [[0, 2], [1, 16], [64, 4]], 0, 0)
-    iota(("imx", 0, 32), [[1, 8], [0, 4]], 0, 0)
+    iota(("imx", 0, 2), [[16, 2]], 1, 0)
 
-    vset(("zr", 0, 512), 0.0)
-    act(("zb", 32, 544), ("zr", 0, 512), AF.Copy)
-    book("b1")
-    book("b2", HS0)
-    vset(("xt", 512, 520), 0.0)
-    vset(("le", 0, 1), 0.0)
-    vset(("zt", 0, 16), 0.0)
-    vset(("onb", 0, 520), 1.0)
-    op("p", lambda: g.affine_select(T.gp[:, 0:520], T.onb[:, 0:520], [[-1, 520]], OP.is_equal, 0.0, 3, 4),
-       [("onb", 0, 520)], [("gp", 0, 520)])
-    vts(T0, TOK, -128.0, None, OP.add)
-    vts(CHI, T0, M16, M16, OP.add, OP.subtract)
-    vtt(CLO, T0, CHI, OP.subtract)
-    vts(("tri", 0, 512, 4), ("itr", 0, 128), TOK, 2.0, OP.is_gt, OP.mult)
-    vts(("tri", 1, 512, 4), ("itr", 0, 128), TOK, None, OP.is_equal)
-    vset(("zb", 514, 544, 4), -15.0)
-    vcopy(("zb", 513, 544, 4), ("c256", 0, 8))
-    quant("qc", 0, ("zb", 0, 512))
-    vts(("tri", 2, 512, 4), ("itr", 0, 128), TOK, None, OP.is_equal)
-    vset(("tri", 3, 512, 4), 0.0)
+    H = {}
+    H["zr"] = lambda: vset(("zr", 0, 512), 0.0)
+    H["zb"] = lambda: act(("zb", 32, 544), ("zr", 0, 512), AF.Copy)
+    for h in range(4):
+        H["b1%d" % h] = lambda h=h: book("b1", h)
+        H["b2%d" % h] = lambda h=h: book("b2", h)
+        H["w16%d" % h] = lambda h=h: vts(("w16", 128 * h, 128 * h + 128), ("ik", 0, 128), -64.0 * h, R16, OP.add, OP.is_equal)
+    H["wt"] = lambda: dma("y", T.wt[:], T.w[:], [], [("wt", 0, 512)])
+    H["xt"] = lambda: vset(("xt", 512, 520), 0.0)
+    H["zt"] = lambda: vset(("zt", 0, 16), 0.0)
+    H["onb"] = lambda: vset(("onb", 0, 520), 1.0)
+    H["gp"] = lambda: op("p", lambda: g.affine_select(T.gp[:, 0:520], T.onb[:, 0:520], [[-1, 520]], OP.is_equal, 0.0, 3, 4),
+                         [("onb", 0, 520)], [("gp", 0, 520)])
+    H["gm"] = lambda: act(("gm", 0, 520), ("gp", 0, 520), AF.Copy, scale=-1.0)
+    H["chi"] = lambda: vts(CHI, T0, M16, M16, OP.add, OP.subtract)
+    H["clo"] = lambda: vtt(CLO, T0, CHI, OP.subtract)
+    H["tri0"] = lambda: vts(("tri", 0, 512, 4), ("itr", 0, 128), TOK, 2.0, OP.is_gt, OP.mult)
+    H["tri1"] = lambda: vts(("tri", 1, 512, 4), ("itr", 0, 128), TOK, None, OP.is_equal)
+    H["tri2"] = lambda: vts(("tri", 2, 512, 4), ("itr", 0, 128), TOK, None, OP.is_equal)
+    H["tri3"] = lambda: vts(("tri", 3, 512, 4), ("itr", 0, 128), TOK, -2.0, OP.is_gt, OP.mult)
+    H["k15"] = lambda: vset(("zb", 514, 544, 4), -15.0)
+    H["k256"] = lambda: vcopy(("zb", 513, 544, 4), ("c256", 0, 8))
+    H["qc"] = lambda: quant("qc", 0, ("zb", 0, 512))
+    H["qtri"] = lambda: quant("qtri", 0, ("tri", 0, 512))
+    H["r16"] = lambda: vts(("ic", 0, 1), ("ip", 0, 1), 15, None, OP.bitwise_and)
+    H["hq"] = lambda: vts(("ic", 1, 2), ("ip", 1, 2), 384, None, OP.bitwise_and)
+    H["p16"] = lambda: vts(("ic", 2, 3), ("ip", 0, 1), 4, None, OP.arith_shift_right)
+    H["cf"] = lambda: vcopy(("cf", 0, 3), ("ic", 0, 3))
+    H["e0"] = lambda: vts(E0, P16, -20.0, TOK, OP.mult, OP.add)
+    H["eq"] = lambda: vts(("eq", 0, 2), ("imx", 0, 2), E0, 5.0, OP.add, OP.min)
+    H["offc"] = lambda: vts(("offc", 0, 2), ("eq", 0, 2), 0.0, None, OP.max)
+    for n4 in ("n4n", "n4f", "n4h"):
+        H[n4] = lambda n4=n4: act((n4, 0, 16), ("zr", 0, 16), AF.Copy)
+    H["xb"] = lambda: act(("xb", 64, 544), ("zr", 0, 480), AF.Copy)
+    H["qw16"] = lambda: quant("qw16", 0, ("w16", 0, 512))
 
-    quant("qx", 0, ("xt", 0, 520))
-    mm("sc", 0, "qx", 0, "qc", 0)
-    quant("qtri", 0, ("tri", 0, 512))
-    vscan(("pmc", 0, 8), ("zt", 0, 8), ("sc", 0, 8), BIG, OP.add, OP.max)
-    vts(("le", 1, 9), ("pmc", 0, 8), ("pmc", 7, 8), None, OP.is_ge)
-    vtt(("zb", 512, 544, 4), ("le", 1, 9), ("le", 0, 8), OP.subtract)
-    quant("qo", 0, ("zb", 32, 544))
-    mm("sc", 1, "qtri", 0, "qo", 0)
-    for l in ("lv1", "lv2"):
-        dma("y", u8(T, l, 256, 258), u8(T, "qx", 128, 130), [("qx", 128, 130)], [(l, 256, 258)])
-        dma("y", T[l + "_s"][:, 256:258], T["qx_s"][:, 128:130], [("qx_s", 128, 130)], [(l + "_s", 256, 258)])
-    vset(("sx", 2, 576, 4), 0.0)
-    vset(("sx", 3, 576, 4), 0.0)
-    vtt(("g8", 0, 8), ("zb", 512, 544, 4), ("sc", 632, 640), OP.mult)
-    vsum(G, ("g8", 0, 8))
-    vts(FH, G, M32, M32, OP.add, OP.subtract)
-    vts(("sx", 0, 512, 4), ("ir", 0, 128), FH, G, OP.add, OP.is_equal)
-    vts(("sx", 1, 512, 4), ("ir", 0, 128), FH, G, OP.add, OP.is_equal)
-    vts(("sx", 512, 576, 4), ("ict", 0, 16), FH, CHI, OP.is_equal, OP.mult)
-    vts(("sx", 513, 576, 4), ("ict", 0, 16), FH, CLO, OP.is_equal, OP.mult)
-    quant("qs", 0, ("sx", 0, 576))
-    mm("sc", 2, "qs", 0, "qs", 16)
-    vset(("rst", 0, 256), 0.0)
-    vts(("offs", 0, 16), ("sc", 1136, 1152), 128.0, None, OP.add)
+    def zeros():
+        for l in ("lv1", "lv2"):
+            dma("y", u8(T, l, 256, 258), u8(T, "qx", 128, 130), [("qx", 128, 130)], [(l, 256, 258)])
+            dma("y", T[l + "_s"][:, 256:258], T["qx_s"][:, 128:130], [("qx_s", 128, 130)], [(l + "_s", 256, 258)])
+    H["zeros"] = zeros
 
-    def to_relays(kind, buf, w, dstbuf, sem):
+    H["qx"] = lambda: quant("qx", 0, ("xt", 0, 520))
+    H["cells"] = lambda: mm("sc", 0, "qx", 0, "qc", 0)
+    H["top"] = lambda: vscan(("pmc", 0, 8), ("zt", 0, 8), ("sc", 0, 8), BIG, OP.add, OP.max)
+    H["from0"] = lambda: vts(("zb", 512, 544, 4), ("pmc", 0, 8), ("pmc", 7, 8), None, OP.is_ge)
+    H["from1"] = lambda: vts(("zb", 519, 544, 4), ("pmc", 0, 7), ("pmc", 7, 8), None, OP.is_ge)
+    H["qo"] = lambda: quant("qo", 0, ("zb", 32, 544))
+    H["earlier"] = lambda: mm("sc", 1, "qtri", 0, "qo", 0)
+    H["sx0"] = lambda: act(("sx", 1, 576, 2), ("zr", 0, 288), AF.Copy)
+    H["G"] = lambda: vscan(("g8", 0, 8), ("zb", 515, 544, 4), ("sc", 632, 640), 0.0, OP.mult, OP.max)
+    H["FH"] = lambda: vts(FH, G, M32, M32, OP.add, OP.subtract)
+    H["sx1"] = lambda: vts(("sx", 0, 512, 2), ("ir", 0, 256), FH, G, OP.add, OP.is_equal)
+    H["sx2"] = lambda: vts(("sx", 512, 576, 4), ("ict", 0, 16), FH, CHI, OP.is_equal, OP.mult)
+    H["sx3"] = lambda: vts(("sx", 514, 576, 4), ("ict", 0, 16), FH, CLO, OP.is_equal, OP.mult)
+    H["qs"] = lambda: quant("qs", 0, ("sx", 0, 576))
+    H["lists"] = lambda: mm("sc", 2, "qs", 0, "qs", 16)
+    H["offs"] = lambda: vts(("offs", 0, 16), ("sc", 1136, 1152), 128.0, None, OP.add)
+
+    def to_relays(kind, buf, w, dstbuf, sem, step=64):
         codes = SCRATCH[buf][2] == F8
         parts = []
         for i, rc in enumerate(pl[kind]):
@@ -415,118 +427,90 @@ def home_program(g, core, T, topo):
             if codes:
                 parts.append((rc, es[k:k + FF], sem, u8(T, dstbuf, 0, w), u8(T, buf, w * i, w * i + w)))
             else:
-                parts.append((rc, es[k:k + FF], sem, T[dstbuf][:, 0:w], T[buf][:, w * i:w * i + w]))
-        fused([(buf, 0, 2 * w)], parts)
+                parts.append((rc, es[k:k + FF], sem, T[dstbuf][:, 0:w], T[buf][:, step * i:step * i + w]))
+        fused([(buf, 0, step + w)], parts)
 
-    def to_near(buf, w, dstbuf, place, sem):
+    def to_near(buf, w, dstbuf, place, sem, step=32):
         codes = SCRATCH[buf][2] == F8
-        parts = []
+        parts, n = [], 0
         for k, d in enumerate(near):
             if d == me:
                 continue
-            a, dc, n = place(d), T.cores[d], len(parts)
+            a, dc = place(d), T.cores[d]
             es = topo.engines(core, dc)
-            es = es[len(es) - FM:] if d in pl["near"][1] else es[FN * n:FN * n + FN]
+            if d in pl["here"]:
+                es = es[len(es) - FM:]
+            else:
+                es = es[FN * n:FN * n + FN]
+                n += 1
             if codes:
                 parts.append((dc, es, sem, u8(T, dstbuf, a, a + w), u8(T, buf, w * k, w * k + w)))
             else:
-                parts.append((dc, es, sem, T[dstbuf][:, a:a + w], T[buf][:, w * k:w * k + w]))
-        fused([(buf, 0, 4 * w)], parts)
+                parts.append((dc, es, sem, T[dstbuf][:, a:a + w], T[buf][:, step * k:step * k + w]))
+        fused([(buf, 0, 3 * step + w)], parts)
 
-    pick("sf", 0, "qx", 130, "offs", 0, 8)
-    to_relays("codes", "sf", 64, "rz", "rzc")
-    to_relays("scales", "sf_s", 64, "rz_s", "rzs")
-    pick("sn", 0, "qx", 130, "offs", 8, 16)
+    H["sf.c"] = lambda: pick_codes("sf", 0, "qx", 130, "offs", 0, 8)
+    H["sf.s"] = lambda: pick_scales("sf", 0, "qx", 130, "offs", 0, 8)
+    H["sn.c"] = lambda: pick_codes("sn", 0, "qx", 130, "offs", 8, 16)
+    H["sn.s"] = lambda: pick_scales("sn", 0, "qx", 130, "offs", 8, 16)
+    H["own"] = lambda: pick("zn", 32 * own, "qx", 130, "offs", 8 + 2 * own, 10 + 2 * own)
+    H["f.c"] = lambda: to_relays("codes", "sf", 64, "rz", "rzc")
+    H["f.s"] = lambda: to_relays("scales", "sf_s", 64, "rz_s", "rzs")
+    H["n.c"] = lambda: to_near("sn", 32, "zn", lambda d: 32 * own, "azn")
+    H["n.s"] = lambda: to_near("sn_s", 32, "zn_s", lambda d: 32 * own, "azn")
 
-    def at_near(d):
-        p = plan(T, topo, T.cores[d])
-        return 32 * (p["near"][0] + p["near"][1]).index(me)
-    to_near("sn", 32, "zn", at_near, "azn")
-    to_near("sn_s", 32, "zn_s", at_near, "azn")
-
-    def keep(dst, d0, src, s0):
-        dma("y", u8(T, dst, d0, d0 + 32), u8(T, src, s0, s0 + 32), [(src, s0, s0 + 32)], [(dst, d0, d0 + 32)])
-        dma("y", T[dst + "_s"][:, d0:d0 + 32], T[src + "_s"][:, s0:s0 + 32], [(src + "_s", s0, s0 + 32)], [(dst + "_s", d0, d0 + 32)])
-    keep("zn", 32 * own, "sn", 32 * own)
-    book("b2", HS1)
-    act(("gm", 0, 520), ("gp", 0, 520), AF.Copy, scale=-1.0)
-
-    for k, (sh, m) in enumerate(((0, 15), (5, 7), (4, 1), (4, 7), (0, 3))):
-        o = ("ic", k, k + 1)
-        if sh:
-            vts(o, ("ip", 0, 1), sh, m, OP.arith_shift_right, OP.bitwise_and)
-        else:
-            vts(o, ("ip", 0, 1), m, None, OP.bitwise_and)
-    vcopy(("cf", 0, 5), ("ic", 0, 5))
-    vts(HQ128, HQ, 128.0, None, OP.mult)
-    vts(E0, U1, -1.0, 1.0, OP.mult, OP.add)
-    vset(("rst", 0, 256, 128), BIG)
-    for h in range(4):
-        vts(("w16", 128 * h, 128 * h + 128), ("ik", 0, 128), -64.0 * h, R16, OP.add, OP.is_equal)
-    quant("qw16", 0, ("w16", 0, 512))
-    vts(("mxx", 0, 32), ("imx", 0, 32), P16, None, OP.is_equal)
-    vts(("offc", 0, 2), ("zt", 0, 2), P3, None, OP.add)
-    vset(("xb", 64, 544), 0.0)
-
-    def relocate(x, n4, bank):
+    def relocate(x, n4, w0, bank):
         ql, v = "ql" + x, (544 if x == "n" else 0)
-        o, w, f, m = ("xm" + x, 0, 32), (n4, 0, 4), ("offc", 0, 2), ("mxx", 0, 32)
+        w, f, hi, lo = (n4, w0, w0 + 8), ("offc", 0, 2), ("xb", v, v + 32), ("xb", v + 32, v + 64)
         a = 64 if x == "n" else 0
         k = 512 * bank + (120 if x == "n" else 0)
 
-        def spread():
-            op("v", lambda: g.vector.tensor_tensor(ap(o), ap(w).indirect(ap(f)), ap(m), OP.mult), [w, f, m], [o])
+        def high():
+            op("v", lambda: g.vector.tensor_scalar(ap(hi), ap(w).indirect(ap(f)), M16, M16, OP.add, OP.subtract), [w, f], [hi])
+
+        def low():
+            op("v", lambda: g.vector.tensor_tensor(ap(lo), ap(w).indirect(ap(f)), ap(hi), OP.subtract), [w, f, hi], [lo])
 
         def products():
             mm("sc", bank, "qw16", 0, ql, 0, True, False)
             mm("sc", bank, "qw16", 0, ql, 8, False, True)
-        return (spread, lambda: vts(("xb", v, v + 32), o, M16, M16, OP.add, OP.subtract),
-                lambda: vtt(("xb", v + 32, v + 64), o, ("xb", v, v + 32), OP.subtract),
-                lambda: quant(ql, 0, ("xb", a, a + 544)), products), ("sc", k, k + 8)
+        return (high, low, lambda: quant(ql, 0, ("xb", a, a + 544)), products), ("sc", k, k + 8)
 
     def home_list():
-        vts(T0, G, -112.0, M256, OP.add, OP.add)
-        vts(T1, T0, M256, 0.25, OP.subtract, OP.mult)
-        vts(T2, T1, -4.0, G, OP.mult, OP.add)
-        vts(T3, T2, 2.0 * CAPP - 16, 0.5, OP.is_lt, OP.mult)
-        vts(T4, T2, T1, 15.0 - 512.0, OP.add, OP.add)
-        vtt(T5, T4, T3, OP.mult)
-        vts(("n4h", 0, 4), ("zt", 0, 4), T5, None, OP.add)
-        fs, ls = relocate("n", "n4h", 3)
-        for f in fs:
-            f()
-        vts(("offh", 0, 8), ls, 256.0, None, OP.add)
+        fs, ls = relocate("n", "n4h", 0, 3)
+        return [lambda: vts(T5, G, -112.0, M256, OP.add, OP.add),
+                lambda: vts(T1, T5, M256, 0.25, OP.subtract, OP.mult),
+                lambda: vts(T2, T1, -4.0, G, OP.mult, OP.add),
+                lambda: vts(T3, T2, 2.0 * CAPP - 16, 0.5, OP.is_lt, OP.mult),
+                lambda: vts(T4, T2, T1, 15.0, OP.subtract, OP.add),
+                lambda: vts(("n4h", 1, 5), ("zt", 0, 4), T4, T3, OP.add, OP.mult),
+                fs[0], fs[1], fs[2], fs[3], lambda: vts(("offh", 0, 8), ls, 256.0, None, OP.add)]
 
     def level(x, l):
-        win, bk, pm, n4, nn, off, sa = ("z" if l == 1 else "rq") + x, "qb%d" % l, "pm" + x, "n4" + x, "nn" + x, "off%d%s" % (l, x), "sa" + x
-        b0 = 0 if x == "n" else 2
-        fs, ls = relocate(x, n4, b0)
-        a, b = ls[1], ls[2]
+        win, bk, pm, n4, off = ("z" if l == 1 else "rq") + x, "qb%d" % l, "pm" + x, "n4" + x, "off%d%s" % (l, x)
+        b0, w0 = (0 if x == "n" else 2), 8 * (l - 1)
+        fs, ls = relocate(x, n4, w0, b0)
         v = ("v%d%s" % (l, x), 0, bk, 512, off, 0, 8)
 
         def score():
             for i in range(2):
                 mm("sc", b0 + i, win, 0, bk, 256 * i, True, True, 256)
 
-        def scan(i):
-            k = 512 * (b0 + i)
-            vscan((pm, 256 * i, 256 * i + 256), ("rst", 0, 256), ("sc", k, k + 256), 0.0, OP.add, OP.max)
+        def scan(h):
+            k = 512 * (b0 + h // 2) + 128 * (h % 2)
+            vscan((pm, 128 * h, 128 * h + 128), ("zr", 0, 128), ("sc", k, k + 128), BIG, OP.add, OP.max)
 
-        def tally(i):
-            for h in range(2 * i, 2 * i + 2):
-                act(("jk", 128 * h, 128 * h + 128), (pm, 128 * h, 128 * h + 128), AF.Sign, bias=(pm, 128 * h + 127, 128 * h + 128),
-                    scale=-1.0, acc=(n4, h, h + 1))
-
-        def parts():
-            act((sa, 0, 4), ("sc", a, b, 2), AF.Copy, scale=E0)
-            act((sa, 4, 8), ("sc", a + 1, b, 2), AF.Copy, scale=U1)
+        def tally(h):
+            act(("jk", 128 * h, 128 * h + 128), (pm, 128 * h, 128 * h + 128), AF.Sign, bias=(pm, 128 * h + 127, 128 * h + 128),
+                scale=-1.0, acc=(n4, w0 + h + 1, w0 + h + 2))
 
         d = {"place%d" % i: f for i, f in enumerate(fs)}
-        for i in range(2):
+        for i in range(4):
             d.update({"scan%d" % i: lambda i=i: scan(i), "count%d" % i: lambda i=i: tally(i)})
         d.update({"score": score, "list": lambda: vts((off, 0, 8), ls, HQ128, None, OP.add), "codes": lambda: pick_codes(*v),
-                  "scales": lambda: pick_scales(*v), "parts": parts,
-                  "number": lambda: vtt((nn, l - 1, 8, 2), (sa, 0, 4), (sa, 4, 8), OP.add),
+                  "scales": lambda: pick_scales(*v),
+                  "number": lambda: act(("nb" + x, 4 * l - 4, 4 * l), (n4, w0 + 1, w0 + 5), AF.Copy),
+                  "own": lambda: pick("lv%d" % l, 32 * me, bk, 512, off, 2 * own, 2 * own + 2),
                   "codesback": lambda: back(x, l, True), "scalesback": lambda: back(x, l, False)})
         return d
 
@@ -540,7 +524,6 @@ def home_program(g, core, T, topo):
             to_near(v, 32, lv, lambda d: 32 * me, "hv%dn" % l)
         else:
             to_near(v + "_s", 32, lv + "_s", lambda d: 32 * me, "hv%dn" % l)
-            keep(lv, 32 * me, v, 32 * own)
 
     def given(x):
         for b in range(4):
@@ -558,15 +541,16 @@ def home_program(g, core, T, topo):
             vcopy(o, i)
 
     def near_numbers():
-        to_near("nnn", 2, "lan", lambda d: 2 * me, "hnn")
-        dma("y", T.lan[:, 2 * me:2 * me + 2], T.nnn[:, 2 * own:2 * own + 2], [("nnn", 2 * own, 2 * own + 2)], [("lan", 2 * me, 2 * me + 2)])
+        to_near("nbn", 8, "xw", lambda d: 32 * me, "hnn", 0)
+        act(("xw", 32 * me, 32 * me + 8), ("nbn", 0, 8), AF.Copy)
 
     def last():
-        vset(("xw", 0, 256), 0.0)
+        for r in range(8):
+            act(("xw", 32 * r + 8, 32 * r + 32), ("zr", 0, 24), AF.Copy)
         vset(("xtw", 256, 288), -1.0)
 
     def steps():
-        d = {}
+        d = dict(H)
         for x in "nf":
             for l in (1, 2):
                 d.update({"%s%d.%s" % (x.upper(), l, n): f for n, f in level(x, l).items()})
@@ -577,9 +561,10 @@ def home_program(g, core, T, topo):
         for b in range(4):
             d["qe%d" % b] = lambda b=b: quant("qe", 128 * b, ("gp", 3 - b, 515 - b))
             d["qm%d" % b] = lambda b=b: quant("qm", 128 * b, ("gm", 3 - b, 515 - b))
-        d.update({"hl": home_list, "fin": last,
+        d.update({"hl%d" % i: f for i, f in enumerate(home_list())})
+        d.update({"fin": last,
                   "qb1": lambda: quant("qb1", 0, ("b1t", 0, 2048)), "qb2": lambda: quant("qb2", 0, ("b2t", 0, 2048)),
-                  "qw": lambda: quant("qw", 0, ("wt", 0, 512)), "f.nums": lambda: to_relays("codes", "nnf", 4, "rn", "rnc"),
+                  "qw": lambda: quant("qw", 0, ("wt", 0, 512)), "f.nums": lambda: to_relays("codes", "nbf", 8, "rn", "rnc", 0),
                   "n.nums": near_numbers})
         return d
 
@@ -597,18 +582,15 @@ def home_program(g, core, T, topo):
     pick("h1", 0, "lv1", 258, "offh", 0, 8)
     store(1)
     mm("sc", 3, "qw", 0, "h1", 0, True, False)
+    vtr(("xtw", 0, 256), ("xw", 0, 256))
+    o, w, f = ("wnt", 0, 128), ("xtw", 0, 288), ("offh", 0, 8)
+    op("v", lambda: g.vector.tensor_copy(ap(o), ap(w).indirect(ap(f))), [w, f], [o])
+    dma("y", T.wn[:], T.wnt[32 * own:32 * own + 8, 0:128], [o], [], True)
     pick("h2", 0, "lv2", 258, "offh", 0, 8)
     mm("sc", 3, "qw", 0, "h2", 0, False, True)
     store(2)
-    for l in range(2):
-        vcopy(("xw", l, 256, 32), ("lan", l, 16, 2))
-    vtr(("xtw", 0, 256), ("xw", 0, 256))
     act(("yt", 0, 128), ("sc", 1536, 1664), AF.Copy)
     dma("s", T.y[:], T.yt[:], [("yt", 0, 128)], [], True)
-    o, w, f = ("wnt", 0, 128), ("xtw", 0, 288), ("offh", 0, 8)
-    op("v", lambda: g.vector.tensor_copy(ap(o), ap(w).indirect(ap(f))), [w, f], [o])
-    for l in range(2):
-        dma("ys"[l], T.wn[4 * l:4 * l + 4, :], T.wnt[l:128:32, 0:128], [o], [], True)
     for s in total:
         if waited.get(s, 0) < total[s]:
             g.wait_ge(T.sem[s], total[s])

@@ -1,66 +1,49 @@
 from concourse.bass import DstId, RemoteDMATransfer
-from concourse.mybir import dt, AluOpType, ActivationFunctionType
+from concourse.mybir import dt, AluOpType as OP, ActivationFunctionType as AF, AxisListType
 
-OP = AluOpType
-AF = ActivationFunctionType
 F8 = "float8_e4m3fn_x4"
-
 SCRATCH = {}
-
-
-def _codes(name, n):
-    SCRATCH[name] = ("sbuf", [128, n], F8)
-    SCRATCH[name + "_s"] = ("sbuf", [128, n], "uint8")
-
-
-def _buf(name, n, ty="float32"):
-    SCRATCH[name] = ("sbuf", [128, n], ty)
-
-
-for _n, _w in (("qx", 130), ("qc", 128), ("qo", 128), ("qtri", 128), ("qs", 144), ("qw16", 128), ("qln", 136), ("qlf", 136),
-               ("qb1", 512), ("qb2", 512), ("qw", 128), ("qe", 512), ("qm", 512),
-               ("sf", 128), ("sn", 128), ("zn", 128), ("zf", 128),
+for _n, _w in (("qx", 138), ("qo", 128), ("qtri", 128), ("qs", 160), ("qw16", 128), ("qln", 136), ("qlf", 136),
+               ("qb1", 512), ("qb2", 512), ("qw", 128), ("qe", 512), ("qm", 512), ("sf", 128), ("sn", 128), ("zn", 128), ("zf", 128),
                ("v1n", 128), ("v1f", 128), ("v2n", 128), ("v2f", 128), ("rqn", 128), ("rqf", 128),
                ("lv1", 384), ("lv2", 384), ("h1", 128), ("h2", 128), ("rz", 64), ("rv1", 64), ("rv2", 64)):
-    _codes(_n, _w)
-for _n, _w in (("xt", 520), ("zr", 512), ("zb", 544), ("xb", 608), ("sx", 576), ("b1t", 2048), ("b2t", 2048), ("wt", 512), ("onb", 520),
-               ("gp", 520), ("gm", 520), ("tri", 512), ("w16", 512), ("ir", 256), ("itr", 128), ("ik", 128), ("imx", 2),
-               ("nbn", 8), ("nbf", 8), ("rn", 8),
-               ("ict", 16), ("jk", 512), ("rtn", 512), ("rtf", 512), ("xw", 256), ("xtw", 288)):
-    _buf(_n, _w, "bfloat16")
-for _n, _w in (("pmn", 512), ("pmf", 512), ("cf", 32), ("c256", 8), ("tok", 1), ("pmc", 8), ("g8", 8),
-               ("n4n", 16), ("n4f", 16), ("n4h", 16), ("zt", 16), ("eq", 2), ("wnt", 128), ("yt", 128)):
-    _buf(_n, _w)
-_buf("ip", 2, "int32")
-_buf("ic", 8, "int32")
-for _n, _w in (("offc", 2), ("offs", 16), ("offh", 8), ("off1n", 8), ("off1f", 8), ("off2n", 8), ("off2f", 8)):
-    _buf(_n, _w, "uint16")
+    SCRATCH[_n] = ("sbuf", [128, _w], F8)
+    SCRATCH[_n + "_s"] = ("sbuf", [128, _w], "uint8")
+for _t, _l in (("bfloat16", (("xt", 552), ("zr", 512), ("zb", 544), ("xb", 608), ("sx", 640), ("b1r", 512), ("b2r", 512), ("b1t", 2048),
+                             ("b2t", 2048), ("wt", 512), ("onb", 520), ("gp", 520), ("gm", 520), ("tri", 512), ("w16", 512), ("ir", 256),
+                             ("itr", 128), ("ik", 128), ("imx", 2), ("nbn", 8), ("nbf", 8), ("rn", 8), ("ic8", 8), ("ict", 32), ("cnt", 2),
+                             ("mkb", 4), ("jkn", 512), ("jkf", 512), ("rtn", 512), ("rtf", 512), ("xw", 256), ("xtw", 288))),
+               ("float32", (("pmn", 512), ("pmf", 512), ("cf", 32), ("tok", 1), ("pmc", 8), ("c4", 4), ("mkf", 4), ("zm", 4),
+                            ("n4n", 16), ("n4f", 16), ("n4h", 16), ("zt", 16), ("eq", 2), ("wnt", 128), ("yt", 128))),
+               ("int32", (("ip", 2), ("ic", 8))),
+               ("uint16", (("offc", 2), ("offs", 16), ("offh", 8), ("off1n", 8), ("off1f", 8), ("off2n", 8), ("off2f", 8)))):
+    for _n, _w in _l:
+        SCRATCH[_n] = ("sbuf", [128, _w], _t)
 SCRATCH["sc"] = ("psum", [128, 2048], "float32")
 SCRATCH["dd"] = ("psum", [128, 2048], "float32")
 
-SEMAPHORES = (["ev", "es", "et", "ep", "sent", "st"] + ["l%d" % i for i in range(40)]
-              + ["azn", "azf", "hv1n", "hv1f", "hv2n", "hv2f", "hnn", "hnf"]
-              + ["rzc", "rzs", "r1c", "r1s", "rnc", "r2c", "r2s"])
+SEMAPHORES = (["ev", "es", "et", "ep", "sent", "st"] + ["l%d" % i for i in range(8)]
+              + ["azn", "azf", "hv1n", "hv1f", "hv2n", "hv2f", "hnn", "hnf"] + ["rzc", "rzs", "r1c", "r1s", "rnc", "r2c", "r2s"])
 
 CAPP = 32
-FN = 4
-FM = 8
-FF = 4
-FR = 4
+FN, FM, FF, FR = 4, 8, 8, 4
 BIG = -9e29
-M16, M32, M256 = 1.5 * 2.0 ** 27, 1.5 * 2.0 ** 28, 1.5 * 2.0 ** 31
+M16 = 1.5 * 2.0 ** 27
 PLANS = {}
 ORDER = """
-zr zb zt onb xt k15 k256 tri1 tri3 tri0 qc b10 qx sx0 gp chi cells tri2 top qtri n4f from0 from1 b20 qo wt earlier n4h zeros clo G FH
-sx3 sx2 b21 sx1 b13 b23 qs hq b12 r16 b11 b22 lists offs sf.s n4n sf.c sn.c p16 cf qe2 f.c gm w160 e0 w163 own qe3 w162 qb1 f.s n.c
-qm0 w161 qm1 qe0 sn.s qm2 n.s qw16 eq xb qe1 offc N1.score N1.scan0 N1.scan1 N1.scan2 N1.count0 n.given N1.count1 N1.count2 hl0
-N1.scan3 N1.count3 qm3 N1.place0 N1.place1 N1.place2 qb2 N1.place3 N1.list N1.codes F1.score N1.scales F1.scan0 F1.scan1 F1.scan3
-n.minus F1.count0 n.rest0 n.rest2 F1.count1 n.rest1 n.rest3 F1.count3 F1.scan2 n.repack F1.count2 F1.place0 hl1 f.given N1.number
-F1.place1 N2.score N2.scan1 N2.count1 F1.place2 N2.scan0 N1.codesback N2.count0 N2.scan3 N1.scalesback N2.scan2 F1.place3 F1.list
-N2.count3 N2.count2 F1.codes N2.place0 qw hl2 F1.scales N2.place1 F1.codesback F1.scalesback f.minus f.rest1 N2.place2 f.rest0
-f.rest2 f.rest3 F1.number N2.place3 f.repack N2.number n.nums F2.score F2.scan0 F2.scan1 F2.count0 F2.scan2 F2.count1 F2.count2
-F2.scan3 F2.count3 F2.number f.nums hl3 hl4 F2.place0 F2.place1 F2.place2 F2.place3 N2.list hl5 N2.codes F2.list N2.scales
-F2.scales F2.codes hl6 F2.codesback F2.scalesback N1.own fin N2.own hl7 hl8 hl9 N2.scalesback N2.codesback hl10"""
+i.itr i.tok ict0 ldx:y zr onb ldc:s xt i.ic8 tri2 tri1 ldw:s i.t0 zb:s i.ip1 ict1 tri0 qx i.ir cells i.ip0 tri3 zt qtri top ict2 from0 sx0:s
+from1 chi ldb2:s qo cs clo earlier mhi cnt mlo ldb1:s i.ik sx1 n4f:s xw7:s qs gp r16 p16 hq gm:s lists i.c4 i.imx offs cf sf.s sf.c w160
+sn.s own.s e0 mkf f.c sn.c f.s qe1 b20:s qm0 n.c b11:s own.c n.s eq xw3:s xw1:s xw2:p zm mkb w161 b10:s qe3 b13:v b23:s w163 qm1 qe2 b12:v
+w162 hl0 b21:s n4n:s xw5:p b22:v qb1 hl1 N1.score2 xb:s qe0 n4h:v N1.score0 qb2 xw0:p N1.scan3 N1.scan2 N1.scan1 N1.count3:s N1.count2:s
+N1.scan0 offc n.given N1.count1:s qw16 hl2 N1.count0:s N1.place0 N1.place1 N1.place2 qm2 N1.place3 qm3 N1.list F1.score3 F1.score2 F1.score0
+N1.codes N1.scales:s F1.scan3 n.minus F1.scan2 F1.count3:s F1.scan0 F1.count2:s F1.scan1 N1.codesback xw4:p F1.count0:s n.rest0:v
+F1.count1:s n.rest2:s n.rest1:v F1.place0 F1.place1 F1.place2 n.rest3:s f.given n.repack F1.place3 F1.number:s N2.score0 qw F1.list F1.codes
+F1.scales:s N2.scan0 f.minus N2.scan1 f.rest0:v N2.count0:s f.rest2:v N1.scalesback f.rest1:s N1.number:v f.rest3:s N2.score2 f.repack
+N2.scan3 F2.score2 F2.score3 F2.score1 F2.score0 N2.scan2 F2.scan2 N2.count1:s N2.count3:s F2.scan3 N2.count2:s F1.scalesback F2.scan1
+F2.scan0 N2.number:v F2.count2:s N2.place0 F2.count3:s F2.count1:s F2.count0:s F1.codesback F2.place0 F2.place1 F2.place2 N2.place1
+F2.place3 N1.owns:s n.nums F2.number:s N2.place2 F2.list f.nums F2.codes N2.place3 F2.scales:s xw6:s hl3 N2.list N2.owns:s hl4 n.numo:s
+N2.codes N2.scales:s hl5 lz1 lz2 xtw F2.codesback wn0 N2.ownc F2.scalesback hl6 hl7 N1.ownc N2.codesback h1.s N2.scalesback h1.c os12:s
+os13:s wn1 os11:y h2.c wn2:y os10:y oc1:s h2.s oc2:y y1 y2 yc:v os20:s os22:s os23:y os21:s ys:y"""
 
 
 def plan(T, topo, core):
@@ -72,8 +55,7 @@ def plan(T, topo, core):
     far = [c for c in cs if c not in here and c not in plane]
     g0 = [c for c in far if c in topo.cores_of(far[0])]
     g1 = [c for c in far if c not in g0]
-    rel = [c for c in topo.cores_of(core) if c not in cs and topo.die(c) == topo.die(core)
-           and all(topo.may_write(c, d) for d in far)]
+    rel = [c for c in topo.cores_of(core) if c not in cs and topo.die(c) == topo.die(core) and all(topo.may_write(c, d) for d in far)]
     srel = []
     for grp in (g0, g1):
         cand = [c for c in range(256) if topo.mates(c, grp[0]) and topo.die(c) == topo.die(core) and topo.same_plane(core, c)
@@ -81,16 +63,12 @@ def plan(T, topo, core):
         users = [c for c in cs if topo.same_plane(c, cand[0]) and topo.die(c) == topo.die(core)]
         srel.append(cand[users.index(core)])
     rk = T.rank_of
+    m = 0 if topo.host(g0[0]) == topo.host(core) else 1
     PLANS[core] = {"near": sorted([[rk(c) for c in plane], [rk(c) for c in here]]), "here": [rk(c) for c in here],
-                   "far": [[rk(c) for c in g0], [rk(c) for c in g1]], "codes": rel[:2], "scales": srel}
+                   "far": [[rk(c) for c in g0], [rk(c) for c in g1]],
+                   "codes": [rel[0] if i == m else srel[i] for i in range(2)], "scales": [srel[i] if i == m else rel[1] for i in range(2)],
+                   "nums": [rel[0] if i == m else rel[1] for i in range(2)]}
     return PLANS[core]
-
-
-def bits(es):
-    m = 0
-    for e in es:
-        m |= 1 << e
-    return m
 
 
 def rank_program(g, core, T, topo):
@@ -102,11 +80,11 @@ def rank_program(g, core, T, topo):
 
 def xfer(T, topo, src, dst, engs, sem, out, in_):
     rid, pid = topo.addr(dst, src)
-    return RemoteDMATransfer(dst_ids=[DstId(rid=rid, pnc=pid)], dma_engine_mask=bits(engs), remote_sem=T.sem[sem], src=in_, dst=out)
+    return RemoteDMATransfer(dst_ids=[DstId(rid=rid, pnc=pid)], dma_engine_mask=sum(1 << e for e in engs), remote_sem=T.sem[sem], src=in_, dst=out)
 
 
-def u8(T, name, a, b):
-    return T[name][:, a:b].bitcast(dt.uint8)
+def cols(T, name, a, b):
+    return T[name][:, a:b].bitcast(dt.uint8) if SCRATCH[name][2] == F8 else T[name][:, a:b]
 
 
 def relay_program(g, core, T, topo):
@@ -121,29 +99,23 @@ def relay_program(g, core, T, topo):
         return
     sent = [0]
 
-    def hand(wait, sem, mk):
+    def hand(wait, n, sem, out, o, in_, w, step):
         ts = []
-        g.wait_ge(T.sem[wait], FF)
+        g.wait_ge(T.sem[wait], n)
         for j, d in enumerate(grp):
             dst = T.cores[d]
-            es = topo.engines(core, dst)[FR * j:FR * j + FR]
             pd = plan(T, topo, dst)
-            at = (pd["far"][0] + pd["far"][1]).index(src)
-            out, in_ = mk(j, at)
-            ts.append(xfer(T, topo, core, dst, es, sem, out, in_))
+            a = 32 * (pd["far"][0] + pd["far"][1]).index(src) if o is None else o
+            ts.append(xfer(T, topo, core, dst, topo.engines(core, dst)[FR * j:FR * j + FR], sem, cols(T, out, a, a + w), cols(T, in_, step * j, step * j + w)))
             sent[0] += FR
         g.remote_dma_fused(ts, local_sem=T.sem.sent)
 
-    o = 32 * src
-    if role == "codes":
-        hand("rzc", "azf", lambda j, at: (u8(T, "zf", 32 * at, 32 * at + 32), u8(T, "rz", 32 * j, 32 * j + 32)))
-        hand("r1c", "hv1f", lambda j, at: (u8(T, "lv1", o, o + 32), u8(T, "rv1", 32 * j, 32 * j + 32)))
-        hand("rnc", "hnf", lambda j, at: (T["xw"][:, o:o + 8], T["rn"][:, 0:8]))
-        hand("r2c", "hv2f", lambda j, at: (u8(T, "lv2", o, o + 32), u8(T, "rv2", 32 * j, 32 * j + 32)))
-    else:
-        hand("rzs", "azf", lambda j, at: (T["zf_s"][:, 32 * at:32 * at + 32], T["rz_s"][:, 32 * j:32 * j + 32]))
-        hand("r1s", "hv1f", lambda j, at: (T["lv1_s"][:, o:o + 32], T["rv1_s"][:, 32 * j:32 * j + 32]))
-        hand("r2s", "hv2f", lambda j, at: (T["lv2_s"][:, o:o + 32], T["rv2_s"][:, 32 * j:32 * j + 32]))
+    o, s, k = 32 * src, ("" if role == "codes" else "_s"), role[0]
+    hand("rz" + k, FF // 2, "azf", "zf" + s, None, "rz" + s, 32, 32)
+    hand("r1" + k, FF, "hv1f", "lv1" + s, o, "rv1" + s, 32, 32)
+    if core in topo.cores_of(T.cores[src]):
+        hand("rnc", FF // 2, "hnf", "xw", o, "rn", 8, 0)
+    hand("r2" + k, FF, "hv2f", "lv2" + s, o, "rv2" + s, 32, 32)
     g.wait_ge(T.sem.sent, sent[0])
 
 
@@ -161,9 +133,7 @@ def home_program(g, core, T, topo):
         if a[1] >= b[2] or b[1] >= a[2]:
             return False
         s, t = (a[3] if len(a) > 3 else 1), (b[3] if len(b) > 3 else 1)
-        if s > 1 and s == t and a[1] % s != b[1] % s:
-            return False
-        return True
+        return not (s > 1 and s == t and a[1] % s != b[1] % s)
 
     def need(e, reads, writes):
         deps = []
@@ -171,9 +141,7 @@ def home_program(g, core, T, topo):
             for r in rs:
                 ps = r[0] in PS
                 for (q, qw, qe, ev, clk) in hist.get(r[0], []):
-                    if (wr or qw or (ps and qe != e)) and clash(r, q):
-                        if ps and e == "t" and qe == "t":
-                            continue
+                    if (wr or qw or (ps and qe != e)) and clash(r, q) and not (ps and e == "t" and qe == "t"):
                         deps.append((ev, clk))
         best = {}
         for ev, clk in deps:
@@ -196,7 +164,11 @@ def home_program(g, core, T, topo):
         for r in writes:
             hist.setdefault(r[0], []).append((r, True, e, ev, clk))
 
+    def bank(r):
+        return (r[0], r[1] - r[1] % 512, r[1] - r[1] % 512 + 512) if r[0] in PS else r
+
     def op(e, call, reads, writes):
+        reads = [bank(r) for r in reads]
         need(e, reads, writes)
         count[e] += 1
         ev = (engsem[e], count[e])
@@ -208,16 +180,13 @@ def home_program(g, core, T, topo):
 
     nl = [0]
 
-    def dma(e, out, in_, reads, writes, store=False):
+    def dma(e, out, in_, reads, writes):
         need(e, reads, writes)
-        if store:
-            s = "st"
-        else:
-            s = "l%d" % nl[0]
-            nl[0] += 1
+        s = "l%d" % nl[0] if writes else "st"
         total[s] = total.get(s, 0) + 16
         queue[e].dma_start(out, in_).then_inc(T.sem[s], 16)
-        if not store:
+        if writes:
+            nl[0] += 1
             clk = dict(known[e])
             clk[s] = 16
             note(e, reads, writes, (s, 16), clk)
@@ -228,160 +197,150 @@ def home_program(g, core, T, topo):
 
     def fused(reads, parts):
         need("p", reads, [])
-        ts = [xfer(T, topo, core, d, es, sem, out, in_) for (d, es, sem, out, in_) in parts]
         total["sent"] = total.get("sent", 0) + sum(len(p[1]) for p in parts)
-        g.remote_dma_fused(ts, local_sem=T.sem.sent)
+        g.remote_dma_fused([xfer(T, topo, core, *p) for p in parts], local_sem=T.sem.sent)
 
     def ap(r):
+        if not isinstance(r, tuple):
+            return r
         return T[r[0]][:, r[1]:r[2]:r[3]] if len(r) > 3 and r[3] > 1 else T[r[0]][:, r[1]:r[2]]
 
-    def isr(x):
-        return isinstance(x, tuple)
+    def rs(*a):
+        return [x for x in a if isinstance(x, tuple)]
+
+    V = g.vector
 
     def vcopy(o, i):
-        op("v", lambda: g.vector.tensor_copy(ap(o), ap(i)), [i], [o])
+        op("v", lambda: V.tensor_copy(ap(o), ap(i)), [i], [o])
 
     def vset(o, c):
-        op("v", lambda: g.vector.memset(ap(o), c), [], [o])
+        op("v", lambda: V.memset(ap(o), c), [], [o])
 
-    def vts(o, i, s1, s2, op0, op1=None):
-        rd = [i] + [s for s in (s1, s2) if isr(s)]
-        a1 = ap(s1) if isr(s1) else s1
-        a2 = ap(s2) if isr(s2) else s2
-        if op1 is None:
-            op("v", lambda: g.vector.tensor_scalar(ap(o), ap(i), a1, None, op0), rd, [o])
-        else:
-            op("v", lambda: g.vector.tensor_scalar(ap(o), ap(i), a1, a2, op0, op1), rd, [o])
+    def vts(o, i, s1, s2, *ops):
+        op("v", lambda: V.tensor_scalar(ap(o), ap(i), ap(s1), ap(s2), *ops), rs(i, s1, s2), [o])
 
     def vtt(o, a, b, o0):
-        op("v", lambda: g.vector.tensor_tensor(ap(o), ap(a), ap(b), o0), [a, b], [o])
+        op("v", lambda: V.tensor_tensor(ap(o), ap(a), ap(b), o0), [a, b], [o])
 
-    def vscan(o, d0, d1, init, o0, o1):
-        op("v", lambda: g.vector.tensor_tensor_scan(ap(o), ap(d0), ap(d1), init, o0, o1), [d0, d1], [o])
+    def vscan(o, d0, d1):
+        op("v", lambda: V.tensor_tensor_scan(ap(o), ap(d0), ap(d1), BIG, OP.add, OP.max), [d0, d1], [o])
 
-    def vtr(o, i):
-        op("v", lambda: g.vector.transpose(ap(o), ap(i)), [i], [o])
+    def vred(o, i, o0):
+        op("v", lambda: V.tensor_reduce(ap(o), ap(i), AxisListType.X, o0), [i], [o])
 
     def quant(o, n0, i):
         w = (i[2] - i[1]) // 4
         a, b = (o, n0, n0 + w), (o + "_s", n0, n0 + w)
-        op("v", lambda: g.vector.quantize_mx(ap(a), ap(b), ap(i)), [i], [a, b])
+        op("v", lambda: V.quantize_mx(ap(a), ap(b), ap(i)), [i], [a, b])
 
-    def act(o, i, f, bias=None, scale=None, acc=None):
-        rd, kw, wr = [i], {}, [o]
-        if bias is not None:
-            kw["bias"] = ap(bias) if isr(bias) else bias
-            if isr(bias):
-                rd.append(bias)
-        if scale is not None:
-            kw["scale"] = ap(scale) if isr(scale) else scale
-            if isr(scale):
-                rd.append(scale)
-        if acc is not None:
-            kw["accum_out"] = ap(acc)
-            wr.append(acc)
-        op("s", lambda: g.scalar.activation(ap(o), ap(i), f, **kw), rd, wr)
+    def act(o, i, f, **kw):
+        op("s", lambda: g.scalar.activation(ap(o), ap(i), f, **{k: ap(v) for k, v in kw.items()}),
+           rs(i, kw.get("bias"), kw.get("scale")), rs(o, kw.get("accum_out")))
+
+    def iota(o, pat, base, cm):
+        kw = {} if o[0] == "ip" else {"allow_small_or_imprecise_dtypes": True}
+        op("p", lambda: g.iota(ap(o), pat, base, cm, **kw), [], [o])
+
+    def copy(e, o, i):
+        if e == "s":
+            act(o, i, AF.Copy)
+        else:
+            vcopy(o, i)
+
+    def times(e, o, i, c, cf):
+        if e == "s":
+            act(o, i, AF.Copy, scale=cf)
+        else:
+            vts(o, i, c, None, OP.mult)
+
+    def fill(e, o):
+        n = len(range(*o[1:]))
+        if e == "s":
+            act(o, ("zr", 0, n), AF.Copy)
+        elif e == "p":
+            iota(o, [[0, n]], 0, 0)
+        else:
+            vset(o, 0.0)
 
     def pick_codes(o, o0, win, w1, off, c0, c1):
         oc, wc, of = (o, o0, o0 + 16 * (c1 - c0)), (win, 0, w1), (off, c0, c1)
-        op("v", lambda: g.vector.tensor_copy(ap(oc).bitcast(dt.uint32), ap(wc).bitcast(dt.uint32).indirect(ap(of))), [wc, of], [oc])
+        op("v", lambda: V.tensor_copy(ap(oc).bitcast(dt.uint32), ap(wc).bitcast(dt.uint32).indirect(ap(of))), [wc, of], [oc])
 
-    def pick_scales(o, o0, win, w1, off, c0, c1):
+    def pick_scales(e, o, o0, win, w1, off, c0, c1):
         osn, ws, of = (o + "_s", o0, o0 + 16 * (c1 - c0)), (win + "_s", 0, w1), (off, c0, c1)
-        op("s", lambda: g.scalar.activation(ap(osn), ap(ws).indirect(ap(of)), AF.Copy), [ws, of], [osn])
+        if e == "s":
+            op("s", lambda: g.scalar.activation(ap(osn), ap(ws).indirect(ap(of)), AF.Copy), [ws, of], [osn])
+        else:
+            op("v", lambda: V.tensor_copy(ap(osn), ap(ws).indirect(ap(of))), [ws, of], [osn])
 
-    def pick(*a):
-        pick_codes(*a)
-        pick_scales(*a)
+    H = {}
 
-    def mm(ps, bank, l, l0, r, r0, start=True, stop=True, n=128):
-        o = (ps, 512 * bank, 512 * bank + n)
-        a, sa, b, sb = (l, l0, l0 + 128), (l + "_s", l0, l0 + 128), (r, r0, r0 + n), (r + "_s", r0, r0 + n)
-        op("t", lambda: g.tensor.matmul_mx(ap(o), ap(a), ap(sa), ap(b), ap(sb), start, stop), [a, sa, b, sb], [(ps, 512 * bank, 512 * bank + 512)])
+    def picks(c, s, *a):
+        H[c] = lambda: pick_codes(*a)
+        H[s] = lambda e="s": pick_scales(e, *a)
 
-    dma("y", T.xt[:, 0:512], T.x[:], [], [("xt", 0, 512)])
-    dma("s", T.zb[:, 0:32], T.co[:, 0:32], [], [("zb", 0, 32)])
-
-    def book(b, h):
-        act((b + "t", 512 * h, 512 * h + 512), ("zr", 0, 512), AF.Copy)
-        dma("y", T[b + "t"][32 * h:32 * h + 32, 512 * h:512 * h + 512], T[b][32 * h:32 * h + 32, :], [], [(b + "t", 512 * h, 512 * h + 512)])
+    def mm(ps, b, l, l0, r, r0, start=True, stop=True, n=128):
+        o = (ps, 512 * b, 512 * b + n)
+        a, sa, c, sb = (l, l0, l0 + 128), (l + "_s", l0, l0 + 128), (r, r0, r0 + n), (r + "_s", r0, r0 + n)
+        op("t", lambda: g.tensor.matmul_mx(ap(o), ap(a), ap(sa), ap(c), ap(sb), start, stop), [a, sa, c, sb] + ([] if start else [o]), [bank(o)])
 
     near, far = pl["near"][0] + pl["near"][1], pl["far"][0] + pl["far"][1]
     own = near.index(me)
 
-    def both(n, a, b):
-        return [(n, a, b), (n + "_s", a, b)]
+    def both(n, at):
+        return [(n + s, 32 * a, 32 * a + 32) for a in at for s in ("", "_s")]
 
-    nw, hw1, hw2, nn_ = [], [], [], []
-    for k, r in enumerate(near):
-        if r != me:
-            nw += both("zn", 32 * k, 32 * k + 32)
-            hw1 += both("lv1", 32 * r, 32 * r + 32)
-            hw2 += both("lv2", 32 * r, 32 * r + 32)
-            nn_.append(("xw", 32 * r, 32 * r + 8))
-    from_near = 2 * FN + FM
-    arrive("azn", 2 * from_near, nw)
-    arrive("hv1n", 2 * from_near, hw1)
-    arrive("hv2n", 2 * from_near, hw2)
-    arrive("hnn", from_near, nn_)
-    arrive("azf", 4 * 2 * FR, both("zf", 0, 128))
-    hw1, hw2, nn_ = [], [], []
-    for r in far:
-        hw1 += both("lv1", 32 * r, 32 * r + 32)
-        hw2 += both("lv2", 32 * r, 32 * r + 32)
-        nn_.append(("xw", 32 * r, 32 * r + 8))
-    arrive("hv1f", 4 * 2 * FR, hw1)
-    arrive("hv2f", 4 * 2 * FR, hw2)
-    arrive("hnf", 4 * FR, nn_)
+    others = [r for r in near if r != me]
+    arrive("azn", 2 * (2 * FN + FM), both("zn", [near.index(r) for r in others]))
+    arrive("azf", 8 * FR, both("zf", range(4)))
+    for x, who, n in (("n", others, 2 * FN + FM), ("f", far, 4 * FR)):
+        arrive("hv1" + x, 2 * n, both("lv1", who))
+        arrive("hv2" + x, 2 * n, both("lv2", who))
+        arrive("hn" + x, n, [("xw", 32 * r, 32 * r + 8) for r in who])
 
-    def iota(o, pat, base, cm):
-        if o[0] == "ip":
-            op("p", lambda: g.iota(ap(o), pat, base, cm), [], [o])
-        else:
-            op("p", lambda: g.iota(ap(o), pat, base, cm, allow_small_or_imprecise_dtypes=True), [], [o])
-
-    def C(k):
-        return ("cf", k, k + 1)
-    R16, HQ128, P16, E0, CHI, CLO, FH, T0, T1, T2, T3, T4, T5 = [C(k) for k in range(13)]
-    G = ("g8", 7, 8)
-    TOK = ("tok", 0, 1)
+    R16, HQ128, P16, E0, CHI, CLO, CS, T0, T1, T2 = [("cf", k, k + 1) for k in range(10)]
+    CNT, TOK = ("cnt", 0, 1), ("tok", 0, 1)
     pf = [q[0] // 2 for q in pl["far"]]
     pn = [q[0] // 2 for q in pl["near"]]
-    iota(("c256", 0, 8), [[-256, 8]], 2048, 0)
-    iota(TOK, [[0, 1]], 0, 1)
-    iota(T0, [[0, 1]], -128, 1)
-    iota(("itr", 0, 128), [[1, 128]], 0, 0)
-    iota(("ir", 0, 256), [[0, 8], [2, 16], [0, 2]], -15, 0)
-    iota(("ict", 0, 8), [[-512 * (pf[1] - pf[0]), 2], [-256, 2], [32, 2]], 2048 - 512 * pf[0], 0)
-    iota(("ict", 8, 16), [[-512 * (pn[1] - pn[0]), 2], [-256, 2], [32, 2]], 2048 - 512 * pn[0], 0)
-    iota(("ip", 0, 1), [[1, 1]], 0, 1)
-    iota(("ip", 1, 2), [[1, 1]], 0, 4)
-    iota(("ik", 0, 128), [[0, 2], [1, 16], [64, 4]], 0, 0)
-    iota(("imx", 0, 2), [[16, 2]], 1, 0)
 
-    H = {}
+    H["ldx"] = lambda e: dma(e, T.xt[:, 0:512], T.x[:], [], [("xt", 0, 512)])
+    H["ldc"] = lambda e: dma(e, T.xt[:, 520:552], T.co[:, 0:32], [], [("xt", 520, 552)])
+    H["ldb1"] = lambda e: dma(e, T.b1r[:], T.b1[:], [], [("b1r", 0, 512)])
+    H["ldb2"] = lambda e: dma(e, T.b2r[:], T.b2[:], [], [("b2r", 0, 512)])
+    H["ldw"] = lambda e: dma(e, T.wt[:], T.w[:], [], [("wt", 0, 512)])
+    H["i.tok"] = lambda: iota(TOK, [[0, 1]], 0, 1)
+    H["i.t0"] = lambda: iota(T0, [[0, 1]], -128, 1)
+    H["i.itr"] = lambda: iota(("itr", 0, 128), [[1, 128]], 0, 0)
+    H["i.ir"] = lambda: iota(("ir", 0, 256), [[0, 8], [1, 16], [16, 2]], 128, 0)
+    H["i.ic8"] = lambda: iota(("ic8", 0, 8), [[-2 * (pn[0] - pf[0]), 2], [-2 * (pf[1] - pf[0]), 2], [-1, 2]], 8 - 2 * pf[0], 0)
+    H["i.ip0"] = lambda: iota(("ip", 0, 1), [[1, 1]], 0, 1)
+    H["i.ip1"] = lambda: iota(("ip", 1, 2), [[1, 1]], 0, 4)
+    H["i.c4"] = lambda: iota(("c4", 0, 4), [[128, 4]], 0, 0)
+    H["i.ik"] = lambda: iota(("ik", 0, 128), [[0, 2], [1, 16], [64, 4]], 0, 0)
+    H["i.imx"] = lambda: iota(("imx", 0, 2), [[16, 2]], 1, 0)
     H["zr"] = lambda: vset(("zr", 0, 512), 0.0)
-    H["zb"] = lambda: act(("zb", 32, 544), ("zr", 0, 512), AF.Copy)
+    H["zb"] = lambda e: fill(e, ("zb", 32, 544))
     for h in range(4):
-        H["b1%d" % h] = lambda h=h: book("b1", h)
-        H["b2%d" % h] = lambda h=h: book("b2", h)
+        for b in ("b1", "b2"):
+            H[b + str(h)] = lambda e, b=b, h=h: times(e, (b + "t", 512 * h, 512 * h + 512), (b + "r", 0, 512), ("mkb", h, h + 1), ("mkf", h, h + 1))
         H["w16%d" % h] = lambda h=h: vts(("w16", 128 * h, 128 * h + 128), ("ik", 0, 128), -64.0 * h, R16, OP.add, OP.is_equal)
-    H["wt"] = lambda: dma("y", T.wt[:], T.w[:], [], [("wt", 0, 512)])
+        H["qe%d" % h] = lambda b=h: quant("qe", 128 * b, ("gp", 3 - b, 515 - b))
+        H["qm%d" % h] = lambda b=h: quant("qm", 128 * b, ("gm", 3 - b, 515 - b))
+    H["mkb"] = lambda: vts(("mkb", 0, 4), ("c4", 0, 4), HQ128, None, OP.is_equal)
+    H["mkf"] = lambda: vts(("mkf", 0, 4), ("c4", 0, 4), HQ128, None, OP.is_equal)
     H["xt"] = lambda: vset(("xt", 512, 520), 0.0)
     H["zt"] = lambda: vset(("zt", 0, 16), 0.0)
+    H["zm"] = lambda: vset(("zm", 0, 4), -128.0)
     H["onb"] = lambda: vset(("onb", 0, 520), 1.0)
     H["gp"] = lambda: op("p", lambda: g.affine_select(T.gp[:, 0:520], T.onb[:, 0:520], [[-1, 520]], OP.is_equal, 0.0, 3, 4),
                          [("onb", 0, 520)], [("gp", 0, 520)])
-    H["gm"] = lambda: act(("gm", 0, 520), ("gp", 0, 520), AF.Copy, scale=-1.0)
+    H["gm"] = lambda e: times(e, ("gm", 0, 520), ("gp", 0, 520), -1.0, -1.0)
     H["chi"] = lambda: vts(CHI, T0, M16, M16, OP.add, OP.subtract)
     H["clo"] = lambda: vtt(CLO, T0, CHI, OP.subtract)
-    H["tri0"] = lambda: vts(("tri", 0, 512, 4), ("itr", 0, 128), TOK, 2.0, OP.is_gt, OP.mult)
-    H["tri1"] = lambda: vts(("tri", 1, 512, 4), ("itr", 0, 128), TOK, None, OP.is_equal)
-    H["tri2"] = lambda: vts(("tri", 2, 512, 4), ("itr", 0, 128), TOK, None, OP.is_equal)
-    H["tri3"] = lambda: vts(("tri", 3, 512, 4), ("itr", 0, 128), TOK, -2.0, OP.is_gt, OP.mult)
-    H["k15"] = lambda: vset(("zb", 514, 544, 4), -15.0)
-    H["k256"] = lambda: vcopy(("zb", 513, 544, 4), ("c256", 0, 8))
-    H["qc"] = lambda: quant("qc", 0, ("zb", 0, 512))
+    H["tri1"] = lambda: vts(("tri", 1, 512, 4), ("itr", 0, 128), TOK, 128.0, OP.is_equal, OP.mult)
+    H["tri2"] = lambda: vts(("tri", 2, 512, 4), ("itr", 0, 128), TOK, None, OP.is_gt)
+    H["tri0"] = lambda: vtt(("tri", 0, 512, 4), ("tri", 1, 512, 4), ("tri", 2, 512, 4), OP.add)
+    H["tri3"] = lambda: vts(("tri", 3, 512, 4), ("tri", 0, 512, 4), -1.0, None, OP.mult)
     H["qtri"] = lambda: quant("qtri", 0, ("tri", 0, 512))
     H["r16"] = lambda: vts(("ic", 0, 1), ("ip", 0, 1), 15, None, OP.bitwise_and)
     H["hq"] = lambda: vts(("ic", 1, 2), ("ip", 1, 2), 384, None, OP.bitwise_and)
@@ -391,206 +350,148 @@ def home_program(g, core, T, topo):
     H["eq"] = lambda: vts(("eq", 0, 2), ("imx", 0, 2), E0, 5.0, OP.add, OP.min)
     H["offc"] = lambda: vts(("offc", 0, 2), ("eq", 0, 2), 0.0, None, OP.max)
     for n4 in ("n4n", "n4f", "n4h"):
-        H[n4] = lambda n4=n4: act((n4, 0, 16), ("zr", 0, 16), AF.Copy)
-    H["xb"] = lambda: act(("xb", 64, 544), ("zr", 0, 480), AF.Copy)
+        H[n4] = lambda e, n4=n4: fill(e, (n4, 0, 16))
+    H["xb"] = lambda e: fill(e, ("xb", 64, 544))
     H["qw16"] = lambda: quant("qw16", 0, ("w16", 0, 512))
+    H["lz1"] = lambda: quant("lv1", 256, ("zr", 0, 512))
+    H["lz2"] = lambda: quant("lv2", 256, ("zr", 0, 512))
+    for r in range(8):
+        H["xw%d" % r] = lambda e, r=r: fill(e, ("xw", 32 * r + 8, 32 * r + 32))
+    H["xtw"] = lambda: vset(("xtw", 256, 288), -1.0)
+    H["ict0"] = lambda: vset(("ict", 0, 32), 0.0)
+    H["ict1"] = lambda: vcopy(("ict", 0, 32, 4), ("ic8", 0, 8))
+    H["ict2"] = lambda: vcopy(("ict", 3, 32, 4), ("ic8", 0, 8))
+    H["sx0"] = lambda e: fill(e, ("sx", 1, 640, 2))
 
-    def zeros():
-        for l in ("lv1", "lv2"):
-            dma("y", u8(T, l, 256, 258), u8(T, "qx", 128, 130), [("qx", 128, 130)], [(l, 256, 258)])
-            dma("y", T[l + "_s"][:, 256:258], T["qx_s"][:, 128:130], [("qx_s", 128, 130)], [(l + "_s", 256, 258)])
-    H["zeros"] = zeros
-
-    H["qx"] = lambda: quant("qx", 0, ("xt", 0, 520))
-    H["cells"] = lambda: mm("sc", 0, "qx", 0, "qc", 0)
-    H["top"] = lambda: vscan(("pmc", 0, 8), ("zt", 0, 8), ("sc", 0, 8), BIG, OP.add, OP.max)
+    H["qx"] = lambda: quant("qx", 0, ("xt", 0, 552))
+    H["cells"] = lambda: mm("sc", 0, "qx", 0, "qx", 10)
+    H["top"] = lambda: vscan(("pmc", 0, 8), ("zt", 0, 8), ("sc", 120, 128))
     H["from0"] = lambda: vts(("zb", 512, 544, 4), ("pmc", 0, 8), ("pmc", 7, 8), None, OP.is_ge)
     H["from1"] = lambda: vts(("zb", 519, 544, 4), ("pmc", 0, 7), ("pmc", 7, 8), None, OP.is_ge)
     H["qo"] = lambda: quant("qo", 0, ("zb", 32, 544))
     H["earlier"] = lambda: mm("sc", 1, "qtri", 0, "qo", 0)
-    H["sx0"] = lambda: act(("sx", 1, 576, 2), ("zr", 0, 288), AF.Copy)
-    H["G"] = lambda: vscan(("g8", 0, 8), ("zb", 515, 544, 4), ("sc", 632, 640), 0.0, OP.mult, OP.max)
-    H["FH"] = lambda: vts(FH, G, M32, M32, OP.add, OP.subtract)
-    H["sx1"] = lambda: vts(("sx", 0, 512, 2), ("ir", 0, 256), FH, G, OP.add, OP.is_equal)
-    H["sx2"] = lambda: vts(("sx", 512, 576, 4), ("ict", 0, 16), FH, CHI, OP.is_equal, OP.mult)
-    H["sx3"] = lambda: vts(("sx", 514, 576, 4), ("ict", 0, 16), FH, CLO, OP.is_equal, OP.mult)
-    H["qs"] = lambda: quant("qs", 0, ("sx", 0, 576))
-    H["lists"] = lambda: mm("sc", 2, "qs", 0, "qs", 16)
+    H["cs"] = lambda: vred(CS, ("zb", 512, 544, 4), OP.add)
+    H["mhi"] = lambda: vts(("sx", 512, 576, 2), ("ict", 0, 32), CS, CHI, OP.is_equal, OP.mult)
+    H["mlo"] = lambda: vts(("sx", 576, 640, 2), ("ict", 0, 32), CS, CLO, OP.is_equal, OP.mult)
+    H["cnt"] = lambda: vred(CNT, ("sc", 632, 640), OP.max)
+    H["sx1"] = lambda: vts(("sx", 0, 512, 2), ("ir", 0, 256), CNT, None, OP.is_equal)
+    H["qs"] = lambda: quant("qs", 0, ("sx", 0, 640))
+    H["lists"] = lambda: [mm("sc", 2, "qs", 0, "qs", 16 + 16 * i, i == 0, i == 1) for i in range(2)]
     H["offs"] = lambda: vts(("offs", 0, 16), ("sc", 1136, 1152), 128.0, None, OP.add)
 
-    def to_relays(kind, buf, w, dstbuf, sem, step=64):
-        codes = SCRATCH[buf][2] == F8
+    def to_relays(kind, buf, w, dstbuf, sem, step=64, side=None):
         parts = []
         for i, rc in enumerate(pl[kind]):
             es = topo.engines(core, rc)
-            k = (len(es) - 2 * FF) + FF * i
-            if codes:
-                parts.append((rc, es[k:k + FF], sem, u8(T, dstbuf, 0, w), u8(T, buf, w * i, w * i + w)))
-            else:
-                parts.append((rc, es[k:k + FF], sem, T[dstbuf][:, 0:w], T[buf][:, step * i:step * i + w]))
+            es = es[len(es) - FF:]
+            if side is not None:
+                es = es[side::2]
+            if kind == "nums":
+                es = es[4 * i:4 * i + 4]
+            parts.append((rc, es, sem, cols(T, dstbuf, 0, w), cols(T, buf, step * i, step * i + w)))
         fused([(buf, 0, step + w)], parts)
 
-    def to_near(buf, w, dstbuf, place, sem, step=32):
-        codes = SCRATCH[buf][2] == F8
+    def to_near(buf, w, dstbuf, a, sem, step=32):
         parts, n = [], 0
         for k, d in enumerate(near):
-            if d == me:
-                continue
-            a, dc = place(d), T.cores[d]
-            es = topo.engines(core, dc)
-            if d in pl["here"]:
-                es = es[len(es) - FM:]
-            else:
-                es = es[FN * n:FN * n + FN]
-                n += 1
-            if codes:
-                parts.append((dc, es, sem, u8(T, dstbuf, a, a + w), u8(T, buf, w * k, w * k + w)))
-            else:
-                parts.append((dc, es, sem, T[dstbuf][:, a:a + w], T[buf][:, step * k:step * k + w]))
+            if d != me:
+                es = topo.engines(core, T.cores[d])
+                if d in pl["here"]:
+                    es = es[len(es) - FM:]
+                else:
+                    es = es[FN * n:FN * n + FN]
+                    n += 1
+                parts.append((T.cores[d], es, sem, cols(T, dstbuf, a, a + w), cols(T, buf, step * k, step * k + w)))
         fused([(buf, 0, 3 * step + w)], parts)
 
-    H["sf.c"] = lambda: pick_codes("sf", 0, "qx", 130, "offs", 0, 8)
-    H["sf.s"] = lambda: pick_scales("sf", 0, "qx", 130, "offs", 0, 8)
-    H["sn.c"] = lambda: pick_codes("sn", 0, "qx", 130, "offs", 8, 16)
-    H["sn.s"] = lambda: pick_scales("sn", 0, "qx", 130, "offs", 8, 16)
-    H["own"] = lambda: pick("zn", 32 * own, "qx", 130, "offs", 8 + 2 * own, 10 + 2 * own)
-    H["f.c"] = lambda: to_relays("codes", "sf", 64, "rz", "rzc")
-    H["f.s"] = lambda: to_relays("scales", "sf_s", 64, "rz_s", "rzs")
-    H["n.c"] = lambda: to_near("sn", 32, "zn", lambda d: 32 * own, "azn")
-    H["n.s"] = lambda: to_near("sn_s", 32, "zn_s", lambda d: 32 * own, "azn")
+    picks("sf.c", "sf.s", "sf", 0, "qx", 130, "offs", 0, 8)
+    picks("sn.c", "sn.s", "sn", 0, "qx", 130, "offs", 8, 16)
+    picks("own.c", "own.s", "zn", 32 * own, "qx", 130, "offs", 8 + 2 * own, 10 + 2 * own)
+    H["f.c"] = lambda: to_relays("codes", "sf", 64, "rz", "rzc", 64, 0)
+    H["f.s"] = lambda: to_relays("scales", "sf_s", 64, "rz_s", "rzs", 64, 1)
+    H["n.c"] = lambda: to_near("sn", 32, "zn", 32 * own, "azn")
+    H["n.s"] = lambda: to_near("sn_s", 32, "zn_s", 32 * own, "azn")
 
-    def relocate(x, n4, w0, bank):
+    def relocate(x, n4, w0, b):
         ql, v = "ql" + x, (544 if x == "n" else 0)
         w, f, hi, lo = (n4, w0, w0 + 8), ("offc", 0, 2), ("xb", v, v + 32), ("xb", v + 32, v + 64)
         a = 64 if x == "n" else 0
-        k = 512 * bank + (120 if x == "n" else 0)
+        k = 512 * b + (120 if x == "n" else 0)
+        return [lambda: op("v", lambda: V.tensor_scalar(ap(hi), ap(w).indirect(ap(f)), M16, M16, OP.add, OP.subtract), [w, f], [hi]),
+                lambda: op("v", lambda: V.tensor_tensor(ap(lo), ap(w).indirect(ap(f)), ap(hi), OP.subtract), [w, f, hi], [lo]),
+                lambda: quant(ql, 0, ("xb", a, a + 544)),
+                lambda: [mm("sc", b, "qw16", 0, ql, 8 * i, i == 0, i == 1) for i in range(2)]], ("sc", k, k + 8)
 
-        def high():
-            op("v", lambda: g.vector.tensor_scalar(ap(hi), ap(w).indirect(ap(f)), M16, M16, OP.add, OP.subtract), [w, f], [hi])
-
-        def low():
-            op("v", lambda: g.vector.tensor_tensor(ap(lo), ap(w).indirect(ap(f)), ap(hi), OP.subtract), [w, f, hi], [lo])
-
-        def products():
-            mm("sc", bank, "qw16", 0, ql, 0, True, False)
-            mm("sc", bank, "qw16", 0, ql, 8, False, True)
-        return (high, low, lambda: quant(ql, 0, ("xb", a, a + 544)), products), ("sc", k, k + 8)
-
-    def home_list():
-        fs, ls = relocate("n", "n4h", 0, 3)
-        return [lambda: vts(T5, G, -112.0, M256, OP.add, OP.add),
-                lambda: vts(T1, T5, M256, 0.25, OP.subtract, OP.mult),
-                lambda: vts(T2, T1, -4.0, G, OP.mult, OP.add),
-                lambda: vts(T3, T2, 2.0 * CAPP - 16, 0.5, OP.is_lt, OP.mult),
-                lambda: vts(T4, T2, T1, 15.0, OP.subtract, OP.add),
-                lambda: vts(("n4h", 1, 5), ("zt", 0, 4), T4, T3, OP.add, OP.mult),
-                fs[0], fs[1], fs[2], fs[3], lambda: vts(("offh", 0, 8), ls, 256.0, None, OP.add)]
+    fs, ls = relocate("n", "n4h", 0, 3)
+    for i, f in enumerate([lambda: vts(T1, CS, -32.0, CNT, OP.mult, OP.add),
+                           lambda: vts(T2, CNT, 128.0 + CAPP, None, OP.is_lt),
+                           lambda: vts(("n4h", 1, 5), ("zm", 0, 4), T1, T2, OP.add, OP.mult)]
+                          + fs + [lambda ls=ls: vts(("offh", 0, 8), ls, 256.0, None, OP.add)]):
+        H["hl%d" % i] = f
 
     def level(x, l):
         win, bk, pm, n4, off = ("z" if l == 1 else "rq") + x, "qb%d" % l, "pm" + x, "n4" + x, "off%d%s" % (l, x)
-        b0, w0 = (0 if x == "n" else 2), 8 * (l - 1)
+        b0, w0, N, v, lv = (0 if x == "n" else 2), 8 * (l - 1), "%s%d." % (x.upper(), l), "v%d%s" % (l, x), "lv%d" % l
         fs, ls = relocate(x, n4, w0, b0)
-        v = ("v%d%s" % (l, x), 0, bk, 512, off, 0, 8)
-
-        def score():
-            for i in range(2):
-                mm("sc", b0 + i, win, 0, bk, 256 * i, True, True, 256)
+        parts = {"F1.": [("sc", 3, 0, 2), ("sc", 2, 2, 1), ("sc", 1, 3, 1)], "F2.": [("dd", h, h, 1) for h in range(4)]}.get(N, [("sc", 0, 0, 2), ("sc", 1, 2, 2)])
 
         def scan(h):
-            k = 512 * (b0 + h // 2) + 128 * (h % 2)
-            vscan((pm, 128 * h, 128 * h + 128), ("zr", 0, 128), ("sc", k, k + 128), BIG, OP.add, OP.max)
+            ps, b, h0, n = [q for q in parts if q[2] <= h < q[2] + q[3]][0]
+            k = 512 * b + 128 * (h - h0)
+            vscan((pm, 128 * h, 128 * h + 128), ("zr", 0, 128), (ps, k, k + 128))
 
-        def tally(h):
-            act(("jk", 128 * h, 128 * h + 128), (pm, 128 * h, 128 * h + 128), AF.Sign, bias=(pm, 128 * h + 127, 128 * h + 128),
-                scale=-1.0, acc=(n4, w0 + h + 1, w0 + h + 2))
+        def tally(h, e):
+            act(("jk" + x, 128 * h, 128 * h + 128), (pm, 128 * h, 128 * h + 128), AF.Sign, bias=(pm, 128 * h + 127, 128 * h + 128), scale=-1.0,
+                accum_out=(n4, w0 + h + 1, w0 + h + 2))
 
-        d = {"place%d" % i: f for i, f in enumerate(fs)}
+        def back(s):
+            if x == "f":
+                to_relays("scales" if s else "codes", v + s, 64, "rv%d" % l + s, "r%d%s" % (l, "s" if s else "c"))
+            else:
+                to_near(v + s, 32, lv + s, 32 * me, "hv%dn" % l)
+
         for i in range(4):
-            d.update({"scan%d" % i: lambda i=i: scan(i), "count%d" % i: lambda i=i: tally(i)})
-        d.update({"score": score, "list": lambda: vts((off, 0, 8), ls, HQ128, None, OP.add), "codes": lambda: pick_codes(*v),
-                  "scales": lambda: pick_scales(*v),
-                  "number": lambda: act(("nb" + x, 4 * l - 4, 4 * l), (n4, w0 + 1, w0 + 5), AF.Copy),
-                  "own": lambda: pick("lv%d" % l, 32 * me, bk, 512, off, 2 * own, 2 * own + 2),
-                  "codesback": lambda: back(x, l, True), "scalesback": lambda: back(x, l, False)})
-        return d
+            H.update({N + "place%d" % i: fs[i], N + "scan%d" % i: lambda i=i: scan(i), N + "count%d" % i: lambda e="s", i=i: tally(i, e)})
+        for ps, b, h0, n in parts:
+            H[N + "score%d" % h0] = lambda ps=ps, b=b, h0=h0, n=n: mm(ps, b, win, 0, bk, 128 * h0, True, True, 128 * n)
+        picks(N + "codes", N + "scales", v, 0, bk, 512, off, 0, 8)
+        picks(N + "ownc", N + "owns", lv, 32 * me, bk, 512, off, 2 * own, 2 * own + 2)
+        H.update({N + "list": lambda: vts((off, 0, 8), ls, HQ128, None, OP.add),
+                  N + "number": lambda e="s": copy(e, ("nb" + x, 4 * l - 4, 4 * l), (n4, w0 + 1, w0 + 5)),
+                  N + "codesback": lambda: back(""), N + "scalesback": lambda: back("_s")})
 
-    def back(x, l, codes):
-        v, lv = "v%d%s" % (l, x), "lv%d" % l
-        if x == "f" and codes:
-            to_relays("codes", v, 64, "rv%d" % l, "r%dc" % l)
-        elif x == "f":
-            to_relays("scales", v + "_s", 64, "rv%d_s" % l, "r%ds" % l)
-        elif codes:
-            to_near(v, 32, lv, lambda d: 32 * me, "hv%dn" % l)
-        else:
-            to_near(v + "_s", 32, lv + "_s", lambda d: 32 * me, "hv%dn" % l)
-
-    def given(x):
+    for x in "nf":
+        level(x, 1)
+        level(x, 2)
+        H[x + ".given"] = lambda x=x: [mm("dd", b, "qe", 128 * b, "z" + x, 0, True, False) for b in range(4)]
+        H[x + ".minus"] = lambda x=x: [mm("dd", b, "qm", 128 * b, "v1" + x, 0, False, True) for b in range(4)]
+        H[x + ".repack"] = lambda x=x: quant("rq" + x, 0, ("rt" + x, 0, 512))
         for b in range(4):
-            mm("dd", b, "qe", 128 * b, "z" + x, 0, True, False)
+            H[x + ".rest%d" % b] = lambda e, x=x, b=b: copy(e, ("rt" + x, b, 512, 4), ("dd", 512 * b, 512 * b + 128))
+    H["qb1"] = lambda: quant("qb1", 0, ("b1t", 0, 2048))
+    H["qb2"] = lambda: quant("qb2", 0, ("b2t", 0, 2048))
+    H["qw"] = lambda: quant("qw", 0, ("wt", 0, 512))
+    H["f.nums"] = lambda: to_relays("nums", "nbf", 8, "rn", "rnc", 0)
+    H["n.nums"] = lambda: to_near("nbn", 8, "xw", 32 * me, "hnn", 0)
+    H["n.numo"] = lambda e="s": copy(e, ("xw", 32 * me, 32 * me + 8), ("nbn", 0, 8))
 
-    def minus(x):
-        for b in range(4):
-            mm("dd", b, "qm", 128 * b, "v1" + x, 0, False, True)
-
-    def rest(x, b):
-        o, i = ("rt" + x, b, 512, 4), ("dd", 512 * b, 512 * b + 128)
-        if b % 2:
-            act(o, i, AF.Copy)
-        else:
-            vcopy(o, i)
-
-    def near_numbers():
-        to_near("nbn", 8, "xw", lambda d: 32 * me, "hnn", 0)
-        act(("xw", 32 * me, 32 * me + 8), ("nbn", 0, 8), AF.Copy)
-
-    def last():
-        for r in range(8):
-            act(("xw", 32 * r + 8, 32 * r + 32), ("zr", 0, 24), AF.Copy)
-        vset(("xtw", 256, 288), -1.0)
-
-    def steps():
-        d = dict(H)
-        for x in "nf":
-            for l in (1, 2):
-                d.update({"%s%d.%s" % (x.upper(), l, n): f for n, f in level(x, l).items()})
-            d.update({x + ".given": lambda x=x: given(x), x + ".minus": lambda x=x: minus(x),
-                      x + ".repack": lambda x=x: quant("rq" + x, 0, ("rt" + x, 0, 512))})
-            for b in range(4):
-                d[x + ".rest%d" % b] = lambda x=x, b=b: rest(x, b)
-        for b in range(4):
-            d["qe%d" % b] = lambda b=b: quant("qe", 128 * b, ("gp", 3 - b, 515 - b))
-            d["qm%d" % b] = lambda b=b: quant("qm", 128 * b, ("gm", 3 - b, 515 - b))
-        d.update({"hl%d" % i: f for i, f in enumerate(home_list())})
-        d.update({"fin": last,
-                  "qb1": lambda: quant("qb1", 0, ("b1t", 0, 2048)), "qb2": lambda: quant("qb2", 0, ("b2t", 0, 2048)),
-                  "qw": lambda: quant("qw", 0, ("wt", 0, 512)), "f.nums": lambda: to_relays("codes", "nbf", 8, "rn", "rnc", 0),
-                  "n.nums": near_numbers})
-        return d
-
-    todo = steps()
-    for name in ORDER.split():
-        todo[name]()
-
-    def store(l):
-        h = "h%d" % l
-        o = 128 * (l - 1)
-        dma("y", T.oc[:, 4 * o:4 * o + 512], u8(T, h, 0, 128), [(h, 0, 128)], [], True)
+    for l in (1, 2):
+        h, o = "h%d" % l, 128 * (l - 1)
+        picks(h + ".c", h + ".s", h, 0, "lv%d" % l, 258, "offh", 0, 8)
+        H["oc%d" % l] = lambda e, h=h, o=o: dma(e, T.oc[:, 4 * o:4 * o + 512], cols(T, h, 0, 128), [(h, 0, 128)], [])
         for k in range(4):
-            dma("y" if k % 2 else "s", T.osc[4 * k:4 * k + 4, o:o + 128], T[h + "_s"][32 * k:32 * k + 4, 0:128], [(h + "_s", 0, 128)], [], True)
-
-    pick("h1", 0, "lv1", 258, "offh", 0, 8)
-    store(1)
-    mm("sc", 3, "qw", 0, "h1", 0, True, False)
-    vtr(("xtw", 0, 256), ("xw", 0, 256))
+            H["os%d%d" % (l, k)] = lambda e, h=h, o=o, k=k: dma(e, T.osc[4 * k:4 * k + 4, o:o + 128], T[h + "_s"][32 * k:32 * k + 4, 0:128],
+                                                                [(h + "_s", 0, 128)], [])
+        H["y%d" % l] = lambda h=h, l=l: mm("sc", 3, "qw", 0, h, 0, l == 1, l == 2)
+    H["wn0"] = lambda: op("v", lambda: V.transpose(T.xtw[:, 0:256], T.xw[:, 0:256]), [("xw", 0, 256)], [("xtw", 0, 256)])
     o, w, f = ("wnt", 0, 128), ("xtw", 0, 288), ("offh", 0, 8)
-    op("v", lambda: g.vector.tensor_copy(ap(o), ap(w).indirect(ap(f))), [w, f], [o])
-    dma("y", T.wn[:], T.wnt[32 * own:32 * own + 8, 0:128], [o], [], True)
-    pick("h2", 0, "lv2", 258, "offh", 0, 8)
-    mm("sc", 3, "qw", 0, "h2", 0, False, True)
-    store(2)
-    act(("yt", 0, 128), ("sc", 1536, 1664), AF.Copy)
-    dma("s", T.y[:], T.yt[:], [("yt", 0, 128)], [], True)
+    H["wn1"] = lambda: op("v", lambda: V.tensor_copy(ap(o), ap(w).indirect(ap(f))), [w, f], [o])
+    H["wn2"] = lambda e: dma(e, T.wn[:], T.wnt[32 * own:32 * own + 8, 0:128], [o], [])
+    H["yc"] = lambda e: copy(e, ("yt", 0, 128), ("sc", 1536, 1664))
+    H["ys"] = lambda e: dma(e, T.y[:], T.yt[:], [("yt", 0, 128)], [])
+
+    for name in ORDER.split():
+        H[name.split(":")[0]](*name.split(":")[1:])
     for s in total:
         if waited.get(s, 0) < total[s]:
             g.wait_ge(T.sem[s], total[s])

@@ -6,44 +6,43 @@ SCRATCH = {}
 for _n, _w in (("qx", 138), ("qo", 128), ("qtri", 128), ("qs", 160), ("qw16", 128), ("qln", 136), ("qlf", 136),
                ("qb1", 512), ("qb2", 512), ("qw", 128), ("qe", 512), ("qm", 512), ("sf", 128), ("sn", 128), ("zn", 128), ("zf", 128),
                ("v1n", 128), ("v1f", 128), ("v2n", 128), ("v2f", 128), ("rqn", 128), ("rqf", 128),
-               ("lv1", 384), ("lv2", 384), ("h1", 128), ("h2", 128), ("rz", 64), ("rv1", 64), ("rv2", 64)):
+               ("lv1", 384), ("lv2", 384), ("h1", 128), ("h2", 128), ("px", 256), ("rz", 128), ("rv1", 64), ("rv2", 64)):
     SCRATCH[_n] = ("sbuf", [128, _w], F8)
     SCRATCH[_n + "_s"] = ("sbuf", [128, _w], "uint8")
 for _t, _l in (("bfloat16", (("xt", 552), ("zr", 512), ("zb", 544), ("xb", 608), ("sx", 640), ("b1r", 512), ("b2r", 512), ("b1t", 2048),
                              ("b2t", 2048), ("wt", 512), ("onb", 520), ("gp", 520), ("gm", 520), ("tri", 512), ("w16", 512), ("ir", 256),
-                             ("itr", 128), ("ik", 128), ("imx", 2), ("nbn", 8), ("nbf", 8), ("rn", 8), ("ic8", 8), ("ict", 32), ("cnt", 2),
+                             ("itr", 128), ("ik", 128), ("nbn", 8), ("nbf", 8), ("rn", 8), ("ic8", 8), ("ict", 32), ("cnt", 2),
                              ("mkb", 4), ("jkn", 512), ("jkf", 512), ("rtn", 512), ("rtf", 512), ("xw", 256), ("xtw", 288))),
-               ("float32", (("pmn", 512), ("pmf", 512), ("cf", 32), ("tok", 1), ("pmc", 8), ("c4", 4), ("mkf", 4), ("zm", 4),
+               ("float32", (("pmn", 512), ("pmf", 512), ("cf", 32), ("tok", 1), ("pmc", 8), ("mkf", 4), ("zm", 4),
                             ("n4n", 16), ("n4f", 16), ("n4h", 16), ("zt", 16), ("eq", 2), ("wnt", 128), ("yt", 128))),
-               ("int32", (("ip", 2), ("ic", 8))),
-               ("uint16", (("offc", 2), ("offs", 16), ("offh", 8), ("off1n", 8), ("off1f", 8), ("off2n", 8), ("off2f", 8)))):
+               ("uint16", (("offc", 2), ("rl", 8), ("pl", 8), ("offs", 16), ("offh", 8), ("off1n", 8), ("off1f", 8), ("off2n", 8), ("off2f", 8)))):
     for _n, _w in _l:
         SCRATCH[_n] = ("sbuf", [128, _w], _t)
 SCRATCH["sc"] = ("psum", [128, 2048], "float32")
 SCRATCH["dd"] = ("psum", [128, 2048], "float32")
 
 SEMAPHORES = (["ev", "es", "et", "ep", "sent", "st"] + ["l%d" % i for i in range(8)]
-              + ["azn", "azf", "hv1n", "hv1f", "hv2n", "hv2f", "hnn", "hnf"] + ["rzc", "rzs", "r1c", "r1s", "rnc", "r2c", "r2s"])
+              + ["azn", "azf", "hv1n", "hv1f", "hv2n", "hv2f", "hnn", "hnf"] + ["apx", "apl", "rzc", "rzs", "rzl", "r1c", "r1s", "rnc", "r2c", "r2s"])
 
 CAPP = 32
-FN, FM, FF, FR = 4, 8, 8, 4
+FN, FM, FF, FR, FP = 4, 8, 8, 4, 4
 BIG = -9e29
 M16 = 1.5 * 2.0 ** 27
 PLANS = {}
 ORDER = """
-i.itr i.tok ict0 ldx:y zr onb ldc:s xt i.ic8 tri2 tri1 ldw:s i.t0 zb:s i.ip1 ict1 tri0 qx i.ir cells i.ip0 tri3 zt qtri top ict2 from0 sx0:s
-from1 chi ldb2:s qo cs clo earlier mhi cnt mlo ldb1:s i.ik sx1 n4f:s xw7:s qs gp r16 p16 hq gm:s lists i.c4 i.imx offs cf sf.s sf.c w160
-sn.s own.s e0 mkf f.c sn.c f.s qe1 b20:s qm0 n.c b11:s own.c n.s eq xw3:s xw1:s xw2:p zm mkb w161 b10:s qe3 b13:v b23:s w163 qm1 qe2 b12:v
-w162 hl0 b21:s n4n:s xw5:p b22:v qb1 hl1 N1.score2 xb:s qe0 n4h:v N1.score0 qb2 xw0:p N1.scan3 N1.scan2 N1.scan1 N1.count3:s N1.count2:s
-N1.scan0 offc n.given N1.count1:s qw16 hl2 N1.count0:s N1.place0 N1.place1 N1.place2 qm2 N1.place3 qm3 N1.list F1.score3 F1.score2 F1.score0
-N1.codes N1.scales:s F1.scan3 n.minus F1.scan2 F1.count3:s F1.scan0 F1.count2:s F1.scan1 N1.codesback xw4:p F1.count0:s n.rest0:v
-F1.count1:s n.rest2:s n.rest1:v F1.place0 F1.place1 F1.place2 n.rest3:s f.given n.repack F1.place3 F1.number:s N2.score0 qw F1.list F1.codes
-F1.scales:s N2.scan0 f.minus N2.scan1 f.rest0:v N2.count0:s f.rest2:v N1.scalesback f.rest1:s N1.number:v f.rest3:s N2.score2 f.repack
-N2.scan3 F2.score2 F2.score3 F2.score1 F2.score0 N2.scan2 F2.scan2 N2.count1:s N2.count3:s F2.scan3 N2.count2:s F1.scalesback F2.scan1
-F2.scan0 N2.number:v F2.count2:s N2.place0 F2.count3:s F2.count1:s F2.count0:s F1.codesback F2.place0 F2.place1 F2.place2 N2.place1
-F2.place3 N1.owns:s n.nums F2.number:s N2.place2 F2.list f.nums F2.codes N2.place3 F2.scales:s xw6:s hl3 N2.list N2.owns:s hl4 n.numo:s
-N2.codes N2.scales:s hl5 lz1 lz2 xtw F2.codesback wn0 N2.ownc F2.scalesback hl6 hl7 N1.ownc N2.codesback h1.s N2.scalesback h1.c os12:s
-os13:s wn1 os11:y h2.c wn2:y os10:y oc1:s h2.s oc2:y y1 y2 yc:v os20:s os22:s os23:y os21:s ys:y"""
+i.tok zt xt zm ldc:s onb zr zb:s ict0 p160 sx0:s xb:s hq0 i.ic8 i.itr i.ir n4f:s tri2 ldx:y tri1 xw3:v qx chi tri0 ict2 cells top clo xw7:s
+ict1 from0 from1 tri3 ldb1:s qo qtri earlier cs n4h:s xw5:s hq p16 mkf mlo ldw:y cnt p.s mhi xw4:v sx1 xtw qs hl0 xw0:s lists lz2 pz p.c mkb
+n4n:s b10:s offs qw xw1:s b11:s sn.s p.l sn.c e0 i.ik ldb2:y r16 b12:s b13:v own.c xw6:s lz1 eq w163 w162 b22:s offc n.c n.s xw2:v hl1 own.s
+w160 w161 gp qb1 qw16 hl2 qe2 qe3 qe0 N1.score2 sf.c N1.scan3 b21:s N1.score0 sf.s N1.scan1 N1.scan0 N1.scan2 N1.count3:s fown.c gm:v
+N1.count1:s f.s N1.count0:s N1.count2:s qe1 fown.s f.c qm3 N1.place0 qm0 N1.place1 qm1 b20:s N1.place2 qm2 b23:s N1.number:s F1.score2
+F1.scan2 F1.count2:s F1.scan3 F1.score0 F1.scan0 F1.count3:s F1.count0:s F1.scan1 F1.count1:s N1.place3 n.given N1.list N1.codes F1.place0
+N1.scales:s F1.place1 F1.place2 F1.number:s n.minus n.rest0:v n.rest2:v n.rest1:s F1.place3 n.rest3:s F1.list F1.scales:s f.given F1.codes
+qb2 n.repack f.minus f.rest0:s N2.score2 f.rest2:v N1.codesback f.rest1:s f.rest3:s f.repack N2.scan3 N1.owns:s N2.score0 F2.score0
+N2.count3:s N2.scan0 N2.count0:s F2.score1 F2.score3 F2.scan0 F1.codesback F2.score2 F2.scan1 F2.count0:s F2.scan3 F2.count1:s
+F1.scalesback F2.scan2 N2.scan1 F2.count3:s N1.ownc N2.scan2 N1.scalesback F2.count2:s F2.number:s F2.place0 N2.count1:s f.nums N2.count2:s
+F2.place1 F2.place2 N2.place0 N2.number:s N2.place1 F2.place3 F2.list F2.scales:s F2.codes N2.place2 hl3 n.numo:v N2.place3 hl4 N2.list
+n.nums N2.scales:s hl5 N2.codes hl6 F2.codesback hl7 wn0 h1.s F2.scalesback wn1 N2.ownc N2.codesback N2.owns:s h1.c N2.scalesback h2.c
+os10:s wn2:y os12:s y1 oc1:y os13:s os11:s h2.s oc2:s os22:s os20:y y2 yc:v os23:y ys:y os21:s"""
 
 
 def plan(T, topo, core):
@@ -67,7 +66,8 @@ def plan(T, topo, core):
     PLANS[core] = {"near": sorted([[rk(c) for c in plane], [rk(c) for c in here]]), "here": [rk(c) for c in here],
                    "far": [[rk(c) for c in g0], [rk(c) for c in g1]],
                    "codes": [rel[0] if i == m else srel[i] for i in range(2)], "scales": [srel[i] if i == m else rel[1] for i in range(2)],
-                   "nums": [rel[0] if i == m else rel[1] for i in range(2)]}
+                   "nums": [rel[0] if i == m else rel[1] for i in range(2)], "out": [rel[0], srel[m], rel[1]],
+                   "proxy": [rk(c) for c in (g0, g1)[m] if topo.die(c) == topo.die(core)][0]}
     return PLANS[core]
 
 
@@ -99,19 +99,23 @@ def relay_program(g, core, T, topo):
         return
     sent = [0]
 
-    def hand(wait, n, sem, out, o, in_, w, step):
+    def hand(wait, n, sem, out, a, in_, w, step):
         ts = []
         g.wait_ge(T.sem[wait], n)
         for j, d in enumerate(grp):
             dst = T.cores[d]
-            pd = plan(T, topo, dst)
-            a = 32 * (pd["far"][0] + pd["far"][1]).index(src) if o is None else o
             ts.append(xfer(T, topo, core, dst, topo.engines(core, dst)[FR * j:FR * j + FR], sem, cols(T, out, a, a + w), cols(T, in_, step * j, step * j + w)))
             sent[0] += FR
         g.remote_dma_fused(ts, local_sem=T.sem.sent)
 
     o, s, k = 32 * src, ("" if role == "codes" else "_s"), role[0]
-    hand("rz" + k, FF // 2, "azf", "zf" + s, None, "rz" + s, 32, 32)
+    p = plan(T, topo, T.cores[src])
+    to = T.cores[p["proxy"]]
+    jobs = [[("rzc", "apx", "px", 0, "rz", 64)], [("rzc", "apx", "px", 64, "rz", 64)], [("rzs", "apx", "px_s", 0, "rz_s", 128), ("rzl", "apl", "pl", 0, "rl", 8)]]
+    for wait, sem, out, a, in_, w in (jobs[p["out"].index(core)] if core in p["out"] else []):
+        g.wait_ge(T.sem[wait], FP if wait != "rzl" else FF)
+        g.remote_dma_fused([xfer(T, topo, core, to, topo.engines(core, to), sem, cols(T, out, a, a + w), cols(T, in_, 0, w))], local_sem=T.sem.sent)
+        sent[0] += len(topo.engines(core, to))
     hand("r1" + k, FF, "hv1f", "lv1" + s, o, "rv1" + s, 32, 32)
     if core in topo.cores_of(T.cores[src]):
         hand("rnc", FF // 2, "hnf", "xw", o, "rn", 8, 0)
@@ -238,8 +242,7 @@ def home_program(g, core, T, topo):
            rs(i, kw.get("bias"), kw.get("scale")), rs(o, kw.get("accum_out")))
 
     def iota(o, pat, base, cm):
-        kw = {} if o[0] == "ip" else {"allow_small_or_imprecise_dtypes": True}
-        op("p", lambda: g.iota(ap(o), pat, base, cm, **kw), [], [o])
+        op("p", lambda: g.iota(ap(o), pat, base, cm, allow_small_or_imprecise_dtypes=True), [], [o])
 
     def copy(e, o, i):
         if e == "s":
@@ -285,20 +288,22 @@ def home_program(g, core, T, topo):
         op("t", lambda: g.tensor.matmul_mx(ap(o), ap(a), ap(sa), ap(c), ap(sb), start, stop), [a, sa, c, sb] + ([] if start else [o]), [bank(o)])
 
     near, far = pl["near"][0] + pl["near"][1], pl["far"][0] + pl["far"][1]
-    own = near.index(me)
+    own, at = near.index(me), far.index(pl["proxy"])
 
-    def both(n, at):
-        return [(n + s, 32 * a, 32 * a + 32) for a in at for s in ("", "_s")]
+    def both(n, where):
+        return [(n + s, 32 * a, 32 * a + 32) for a in where for s in ("", "_s")]
 
     others = [r for r in near if r != me]
     arrive("azn", 2 * (2 * FN + FM), both("zn", [near.index(r) for r in others]))
-    arrive("azf", 8 * FR, both("zf", range(4)))
+    arrive("azf", 2 * (2 * FN + FM), both("zf", [k for k in range(4) if k != at]))
+    arrive("apx", 24, [("px", 0, 128), ("px_s", 0, 128)])
+    arrive("apl", 8, [("pl", 0, 8)])
     for x, who, n in (("n", others, 2 * FN + FM), ("f", far, 4 * FR)):
         arrive("hv1" + x, 2 * n, both("lv1", who))
         arrive("hv2" + x, 2 * n, both("lv2", who))
         arrive("hn" + x, n, [("xw", 32 * r, 32 * r + 8) for r in who])
 
-    R16, HQ128, P16, E0, CHI, CLO, CS, T0, T1, T2 = [("cf", k, k + 1) for k in range(10)]
+    R16, HQ128, P16, E0, CHI, CLO, CS, T0, T1, T2, T3 = [("cf", k, k + 1) for k in range(11)]
     CNT, TOK = ("cnt", 0, 1), ("tok", 0, 1)
     pf = [q[0] // 2 for q in pl["far"]]
     pn = [q[0] // 2 for q in pl["near"]]
@@ -309,15 +314,10 @@ def home_program(g, core, T, topo):
     H["ldb2"] = lambda e: dma(e, T.b2r[:], T.b2[:], [], [("b2r", 0, 512)])
     H["ldw"] = lambda e: dma(e, T.wt[:], T.w[:], [], [("wt", 0, 512)])
     H["i.tok"] = lambda: iota(TOK, [[0, 1]], 0, 1)
-    H["i.t0"] = lambda: iota(T0, [[0, 1]], -128, 1)
     H["i.itr"] = lambda: iota(("itr", 0, 128), [[1, 128]], 0, 0)
     H["i.ir"] = lambda: iota(("ir", 0, 256), [[0, 8], [1, 16], [16, 2]], 128, 0)
     H["i.ic8"] = lambda: iota(("ic8", 0, 8), [[-2 * (pn[0] - pf[0]), 2], [-2 * (pf[1] - pf[0]), 2], [-1, 2]], 8 - 2 * pf[0], 0)
-    H["i.ip0"] = lambda: iota(("ip", 0, 1), [[1, 1]], 0, 1)
-    H["i.ip1"] = lambda: iota(("ip", 1, 2), [[1, 1]], 0, 4)
-    H["i.c4"] = lambda: iota(("c4", 0, 4), [[128, 4]], 0, 0)
     H["i.ik"] = lambda: iota(("ik", 0, 128), [[0, 2], [1, 16], [64, 4]], 0, 0)
-    H["i.imx"] = lambda: iota(("imx", 0, 2), [[16, 2]], 1, 0)
     H["zr"] = lambda: vset(("zr", 0, 512), 0.0)
     H["zb"] = lambda e: fill(e, ("zb", 32, 544))
     for h in range(4):
@@ -326,8 +326,8 @@ def home_program(g, core, T, topo):
         H["w16%d" % h] = lambda h=h: vts(("w16", 128 * h, 128 * h + 128), ("ik", 0, 128), -64.0 * h, R16, OP.add, OP.is_equal)
         H["qe%d" % h] = lambda b=h: quant("qe", 128 * b, ("gp", 3 - b, 515 - b))
         H["qm%d" % h] = lambda b=h: quant("qm", 128 * b, ("gm", 3 - b, 515 - b))
-    H["mkb"] = lambda: vts(("mkb", 0, 4), ("c4", 0, 4), HQ128, None, OP.is_equal)
-    H["mkf"] = lambda: vts(("mkf", 0, 4), ("c4", 0, 4), HQ128, None, OP.is_equal)
+    H["mkb"] = lambda: vts(("mkb", 0, 4), ("itr", 0, 4), 128.0, HQ128, OP.mult, OP.is_equal)
+    H["mkf"] = lambda: vts(("mkf", 0, 4), ("itr", 0, 4), 128.0, HQ128, OP.mult, OP.is_equal)
     H["xt"] = lambda: vset(("xt", 512, 520), 0.0)
     H["zt"] = lambda: vset(("zt", 0, 16), 0.0)
     H["zm"] = lambda: vset(("zm", 0, 4), -128.0)
@@ -335,19 +335,20 @@ def home_program(g, core, T, topo):
     H["gp"] = lambda: op("p", lambda: g.affine_select(T.gp[:, 0:520], T.onb[:, 0:520], [[-1, 520]], OP.is_equal, 0.0, 3, 4),
                          [("onb", 0, 520)], [("gp", 0, 520)])
     H["gm"] = lambda e: times(e, ("gm", 0, 520), ("gp", 0, 520), -1.0, -1.0)
-    H["chi"] = lambda: vts(CHI, T0, M16, M16, OP.add, OP.subtract)
-    H["clo"] = lambda: vtt(CLO, T0, CHI, OP.subtract)
+    H["chi"] = lambda: vts(CHI, TOK, M16 - 128.0, M16, OP.add, OP.subtract)
+    H["clo"] = lambda: vts(CLO, TOK, -128.0, CHI, OP.add, OP.subtract)
     H["tri1"] = lambda: vts(("tri", 1, 512, 4), ("itr", 0, 128), TOK, 128.0, OP.is_equal, OP.mult)
     H["tri2"] = lambda: vts(("tri", 2, 512, 4), ("itr", 0, 128), TOK, None, OP.is_gt)
     H["tri0"] = lambda: vtt(("tri", 0, 512, 4), ("tri", 1, 512, 4), ("tri", 2, 512, 4), OP.add)
     H["tri3"] = lambda: vts(("tri", 3, 512, 4), ("tri", 0, 512, 4), -1.0, None, OP.mult)
     H["qtri"] = lambda: quant("qtri", 0, ("tri", 0, 512))
-    H["r16"] = lambda: vts(("ic", 0, 1), ("ip", 0, 1), 15, None, OP.bitwise_and)
-    H["hq"] = lambda: vts(("ic", 1, 2), ("ip", 1, 2), 384, None, OP.bitwise_and)
-    H["p16"] = lambda: vts(("ic", 2, 3), ("ip", 0, 1), 4, None, OP.arith_shift_right)
-    H["cf"] = lambda: vcopy(("cf", 0, 3), ("ic", 0, 3))
-    H["e0"] = lambda: vts(E0, P16, -20.0, TOK, OP.mult, OP.add)
-    H["eq"] = lambda: vts(("eq", 0, 2), ("imx", 0, 2), E0, 5.0, OP.add, OP.min)
+    H["hq0"] = lambda: vts(T0, TOK, -15.5, 2 * M16, OP.add, OP.add)
+    H["hq"] = lambda: vts(HQ128, T0, 2 * M16, 4.0, OP.subtract, OP.mult)
+    H["p160"] = lambda: vts(T3, TOK, -7.5, M16, OP.add, OP.add)
+    H["p16"] = lambda: vts(P16, T3, M16, None, OP.subtract)
+    H["r16"] = lambda: vts(R16, TOK, P16, None, OP.subtract)
+    H["e0"] = lambda: vts(E0, P16, -1.25, TOK, OP.mult, OP.add)
+    H["eq"] = lambda: vts(("eq", 0, 2), ("itr", 1, 18, 16), E0, 5.0, OP.add, OP.min)
     H["offc"] = lambda: vts(("offc", 0, 2), ("eq", 0, 2), 0.0, None, OP.max)
     for n4 in ("n4n", "n4f", "n4h"):
         H[n4] = lambda e, n4=n4: fill(e, (n4, 0, 16))
@@ -355,6 +356,7 @@ def home_program(g, core, T, topo):
     H["qw16"] = lambda: quant("qw16", 0, ("w16", 0, 512))
     H["lz1"] = lambda: quant("lv1", 256, ("zr", 0, 512))
     H["lz2"] = lambda: quant("lv2", 256, ("zr", 0, 512))
+    H["pz"] = lambda: quant("px", 128, ("zr", 0, 512))
     for r in range(8):
         H["xw%d" % r] = lambda e, r=r: fill(e, ("xw", 32 * r + 8, 32 * r + 32))
     H["xtw"] = lambda: vset(("xtw", 256, 288), -1.0)
@@ -379,13 +381,11 @@ def home_program(g, core, T, topo):
     H["lists"] = lambda: [mm("sc", 2, "qs", 0, "qs", 16 + 16 * i, i == 0, i == 1) for i in range(2)]
     H["offs"] = lambda: vts(("offs", 0, 16), ("sc", 1136, 1152), 128.0, None, OP.add)
 
-    def to_relays(kind, buf, w, dstbuf, sem, step=64, side=None):
+    def to_relays(kind, buf, w, dstbuf, sem, step=64):
         parts = []
         for i, rc in enumerate(pl[kind]):
             es = topo.engines(core, rc)
             es = es[len(es) - FF:]
-            if side is not None:
-                es = es[side::2]
             if kind == "nums":
                 es = es[4 * i:4 * i + 4]
             parts.append((rc, es, sem, cols(T, dstbuf, 0, w), cols(T, buf, step * i, step * i + w)))
@@ -404,11 +404,19 @@ def home_program(g, core, T, topo):
                 parts.append((T.cores[d], es, sem, cols(T, dstbuf, a, a + w), cols(T, buf, step * k, step * k + w)))
         fused([(buf, 0, 3 * step + w)], parts)
 
-    picks("sf.c", "sf.s", "sf", 0, "qx", 130, "offs", 0, 8)
+    def out(i, k, n):
+        es = topo.engines(core, pl["out"][i])
+        return es[len(es) - FF:][k:k + n]
+
+    H["p.c"] = lambda: fused([("qx", 0, 128)], [(pl["out"][i], out(i, 0, FP), "rzc", cols(T, "rz", 0, 64), cols(T, "qx", 64 * i, 64 * i + 64)) for i in range(2)])
+    H["p.s"] = lambda: fused([("qx_s", 0, 128)], [(pl["out"][2], out(2, FF - FP, FP), "rzs", cols(T, "rz_s", 0, 128), cols(T, "qx_s", 0, 128))])
+    H["p.l"] = lambda: fused([("offs", 0, 8)], [(pl["out"][2], out(2, 0, FF), "rzl", cols(T, "rl", 0, 8), cols(T, "offs", 0, 8))])
+    picks("sf.c", "sf.s", "sf", 0, "px", 130, "pl", 0, 8)
+    picks("fown.c", "fown.s", "zf", 32 * at, "px", 130, "pl", 2 * own, 2 * own + 2)
     picks("sn.c", "sn.s", "sn", 0, "qx", 130, "offs", 8, 16)
     picks("own.c", "own.s", "zn", 32 * own, "qx", 130, "offs", 8 + 2 * own, 10 + 2 * own)
-    H["f.c"] = lambda: to_relays("codes", "sf", 64, "rz", "rzc", 64, 0)
-    H["f.s"] = lambda: to_relays("scales", "sf_s", 64, "rz_s", "rzs", 64, 1)
+    H["f.c"] = lambda: to_near("sf", 32, "zf", 32 * at, "azf")
+    H["f.s"] = lambda: to_near("sf_s", 32, "zf_s", 32 * at, "azf")
     H["n.c"] = lambda: to_near("sn", 32, "zn", 32 * own, "azn")
     H["n.s"] = lambda: to_near("sn_s", 32, "zn_s", 32 * own, "azn")
 
@@ -433,7 +441,7 @@ def home_program(g, core, T, topo):
         win, bk, pm, n4, off = ("z" if l == 1 else "rq") + x, "qb%d" % l, "pm" + x, "n4" + x, "off%d%s" % (l, x)
         b0, w0, N, v, lv = (0 if x == "n" else 2), 8 * (l - 1), "%s%d." % (x.upper(), l), "v%d%s" % (l, x), "lv%d" % l
         fs, ls = relocate(x, n4, w0, b0)
-        parts = {"F1.": [("sc", 3, 0, 2), ("sc", 2, 2, 1), ("sc", 1, 3, 1)], "F2.": [("dd", h, h, 1) for h in range(4)]}.get(N, [("sc", 0, 0, 2), ("sc", 1, 2, 2)])
+        parts = [("dd", h, h, 1) for h in range(4)] if N == "F2." else [("sc", b0, 0, 2), ("sc", b0 + 1, 2, 2)]
 
         def scan(h):
             ps, b, h0, n = [q for q in parts if q[2] <= h < q[2] + q[3]][0]

from concourse.bass import DstId, RemoteDMATransfer
from concourse.mybir import dt, AluOpType as OP, ActivationFunctionType as AF, AxisListType

F8 = "float8_e4m3fn_x4"
SCRATCH = {}
for _n, _w in (("qx", 138), ("qo", 128), ("qtri", 128), ("qs", 160), ("qw16", 128), ("qln", 136), ("qlf", 136),
               ("qb1", 512), ("qb2", 512), ("qw", 128), ("qe", 512), ("qm", 512), ("sf", 128), ("sn", 128), ("zn", 128), ("zf", 128),
               ("v1n", 128), ("v1f", 128), ("v2n", 128), ("v2f", 128), ("rqn", 128), ("rqf", 128),
               ("lv1", 384), ("lv2", 384), ("h1", 128), ("h2", 128), ("px", 256), ("rz", 128), ("rv1", 64), ("rv2", 64)):
    SCRATCH[_n] = ("sbuf", [128, _w], F8)
    SCRATCH[_n + "_s"] = ("sbuf", [128, _w], "uint8")
for _t, _l in (("bfloat16", (("xt", 552), ("zr", 512), ("zb", 544), ("xb", 608), ("sx", 640), ("b1r", 512), ("b2r", 512), ("b1t", 2048),
                             ("b2t", 2048), ("wt", 512), ("onb", 520), ("gp", 520), ("gm", 520), ("tri", 512), ("w16", 512), ("ir", 256),
                             ("itr", 128), ("ik", 128), ("nbn", 8), ("nbf", 8), ("rn", 8), ("ic8", 8), ("ict", 32), ("cnt", 2),
                             ("mkb", 4), ("jkn", 512), ("jkf", 512), ("rtn", 512), ("rtf", 512), ("xw", 256), ("xtw", 288))),
               ("float32", (("pmn", 512), ("pmf", 512), ("cf", 32), ("tok", 1), ("pmc", 8), ("mkf", 4), ("zm", 4),
                            ("n4n", 16), ("n4f", 16), ("n4h", 16), ("zt", 16), ("eq", 2), ("wnt", 128), ("yt", 128))),
               ("uint16", (("offc", 2), ("rl", 8), ("pl", 8), ("offs", 16), ("offh", 8), ("off1n", 8), ("off1f", 8), ("off2n", 8), ("off2f", 8)))):
    for _n, _w in _l:
        SCRATCH[_n] = ("sbuf", [128, _w], _t)
SCRATCH["sc"] = ("psum", [128, 2048], "float32")
SCRATCH["dd"] = ("psum", [128, 2048], "float32")

SEMAPHORES = (["ev", "es", "et", "ep", "sent", "st"] + ["l%d" % i for i in range(8)]
              + ["azn", "azf", "hv1n", "hv1f", "hv2n", "hv2f", "hnn", "hnf"] + ["apx", "apl", "rzc", "rzs", "rzl", "r1c", "r1s", "rnc", "r2c", "r2s"])

CAPP = 32
FN, FM, FF, FR, FP = 4, 8, 8, 4, 4
BIG = -9e29
M16 = 1.5 * 2.0 ** 27
PLANS = {}
ORDER = """
i.tok zt xt zm ldc:s onb zr zb:s ict0 p160 sx0:s xb:s hq0 i.ic8 i.itr i.ir n4f:s tri2 ldx:y tri1 xw3:v qx chi tri0 ict2 cells top clo xw7:s
ict1 from0 from1 tri3 ldb1:s qo qtri earlier cs n4h:s xw5:s hq p16 mkf mlo ldw:y cnt p.s mhi xw4:v sx1 xtw qs hl0 xw0:s lists lz2 pz p.c mkb
n4n:s b10:s offs qw xw1:s b11:s sn.s p.l sn.c e0 i.ik ldb2:y r16 b12:s b13:v own.c xw6:s lz1 eq w163 w162 b22:s offc n.c n.s xw2:v hl1 own.s
w160 w161 gp qb1 qw16 hl2 qe2 qe3 qe0 N1.score2 sf.c N1.scan3 b21:s N1.score0 sf.s N1.scan1 N1.scan0 N1.scan2 N1.count3:s fown.c gm:v
N1.count1:s f.s N1.count0:s N1.count2:s qe1 fown.s f.c qm3 N1.place0 qm0 N1.place1 qm1 b20:s N1.place2 qm2 b23:s N1.number:s F1.score2
F1.scan2 F1.count2:s F1.scan3 F1.score0 F1.scan0 F1.count3:s F1.count0:s F1.scan1 F1.count1:s N1.place3 n.given N1.list N1.codes F1.place0
N1.scales:s F1.place1 F1.place2 F1.number:s n.minus n.rest0:v n.rest2:v n.rest1:s F1.place3 n.rest3:s F1.list F1.scales:s f.given F1.codes
qb2 n.repack f.minus f.rest0:s N2.score2 f.rest2:v N1.codesback f.rest1:s f.rest3:s f.repack N2.scan3 N1.owns:s N2.score0 F2.score0
N2.count3:s N2.scan0 N2.count0:s F2.score1 F2.score3 F2.scan0 F1.codesback F2.score2 F2.scan1 F2.count0:s F2.scan3 F2.count1:s
F1.scalesback F2.scan2 N2.scan1 F2.count3:s N1.ownc N2.scan2 N1.scalesback F2.count2:s F2.number:s F2.place0 N2.count1:s f.nums N2.count2:s
F2.place1 F2.place2 N2.place0 N2.number:s N2.place1 F2.place3 F2.list F2.scales:s F2.codes N2.place2 hl3 n.numo:v N2.place3 hl4 N2.list
n.nums N2.scales:s hl5 N2.codes hl6 F2.codesback hl7 wn0 h1.s F2.scalesback wn1 N2.ownc N2.codesback N2.owns:s h1.c N2.scalesback h2.c
os10:s wn2:y os12:s y1 oc1:y os13:s os11:s h2.s oc2:s os22:s os20:y y2 yc:v os23:y ys:y os21:s"""


def plan(T, topo, core):
    if core in PLANS:
        return PLANS[core]
    cs = list(T.cores)
    here = [c for c in cs if c in topo.cores_of(core)]
    plane = [c for c in cs if c not in here and topo.same_plane(core, c)]
    far = [c for c in cs if c not in here and c not in plane]
    g0 = [c for c in far if c in topo.cores_of(far[0])]
    g1 = [c for c in far if c not in g0]
    rel = [c for c in topo.cores_of(core) if c not in cs and topo.die(c) == topo.die(core) and all(topo.may_write(c, d) for d in far)]
    srel = []
    for grp in (g0, g1):
        cand = [c for c in range(256) if topo.mates(c, grp[0]) and topo.die(c) == topo.die(core) and topo.same_plane(core, c)
                and all(topo.may_write(c, d) for d in grp)]
        users = [c for c in cs if topo.same_plane(c, cand[0]) and topo.die(c) == topo.die(core)]
        srel.append(cand[users.index(core)])
    rk = T.rank_of
    m = 0 if topo.host(g0[0]) == topo.host(core) else 1
    PLANS[core] = {"near": sorted([[rk(c) for c in plane], [rk(c) for c in here]]), "here": [rk(c) for c in here],
                   "far": [[rk(c) for c in g0], [rk(c) for c in g1]],
                   "codes": [rel[0] if i == m else srel[i] for i in range(2)], "scales": [srel[i] if i == m else rel[1] for i in range(2)],
                   "nums": [rel[0] if i == m else rel[1] for i in range(2)], "out": [rel[0], srel[m], rel[1]],
                   "proxy": [rk(c) for c in (g0, g1)[m] if topo.die(c) == topo.die(core)][0]}
    return PLANS[core]


def rank_program(g, core, T, topo):
    if T.rank_of(core) is None:
        relay_program(g, core, T, topo)
    else:
        home_program(g, core, T, topo)


def xfer(T, topo, src, dst, engs, sem, out, in_):
    rid, pid = topo.addr(dst, src)
    return RemoteDMATransfer(dst_ids=[DstId(rid=rid, pnc=pid)], dma_engine_mask=sum(1 << e for e in engs), remote_sem=T.sem[sem], src=in_, dst=out)


def cols(T, name, a, b):
    return T[name][:, a:b].bitcast(dt.uint8) if SCRATCH[name][2] == F8 else T[name][:, a:b]


def relay_program(g, core, T, topo):
    src, grp, role = None, None, None
    for c in T.cores:
        p = plan(T, topo, c)
        for i in range(2):
            for k in ("codes", "scales"):
                if p[k][i] == core:
                    src, grp, role = T.rank_of(c), p["far"][i], k
    if src is None:
        return
    sent = [0]

    def hand(wait, n, sem, out, a, in_, w, step):
        ts = []
        g.wait_ge(T.sem[wait], n)
        for j, d in enumerate(grp):
            dst = T.cores[d]
            ts.append(xfer(T, topo, core, dst, topo.engines(core, dst)[FR * j:FR * j + FR], sem, cols(T, out, a, a + w), cols(T, in_, step * j, step * j + w)))
            sent[0] += FR
        g.remote_dma_fused(ts, local_sem=T.sem.sent)

    o, s, k = 32 * src, ("" if role == "codes" else "_s"), role[0]
    p = plan(T, topo, T.cores[src])
    to = T.cores[p["proxy"]]
    jobs = [[("rzc", "apx", "px", 0, "rz", 64)], [("rzc", "apx", "px", 64, "rz", 64)], [("rzs", "apx", "px_s", 0, "rz_s", 128), ("rzl", "apl", "pl", 0, "rl", 8)]]
    for wait, sem, out, a, in_, w in (jobs[p["out"].index(core)] if core in p["out"] else []):
        g.wait_ge(T.sem[wait], FP if wait != "rzl" else FF)
        g.remote_dma_fused([xfer(T, topo, core, to, topo.engines(core, to), sem, cols(T, out, a, a + w), cols(T, in_, 0, w))], local_sem=T.sem.sent)
        sent[0] += len(topo.engines(core, to))
    hand("r1" + k, FF, "hv1f", "lv1" + s, o, "rv1" + s, 32, 32)
    if core in topo.cores_of(T.cores[src]):
        hand("rnc", FF // 2, "hnf", "xw", o, "rn", 8, 0)
    hand("r2" + k, FF, "hv2f", "lv2" + s, o, "rv2" + s, 32, 32)
    g.wait_ge(T.sem.sent, sent[0])


def home_program(g, core, T, topo):
    me = T.rank_of(core)
    pl = plan(T, topo, core)
    queue = {"v": g.vector, "s": g.scalar, "t": g.tensor, "p": g, "y": g.sync}
    engsem = {"v": "ev", "s": "es", "t": "et", "p": "ep"}
    known = {e: {} for e in queue}
    count = {e: 0 for e in queue}
    total, waited, hist = {}, {}, {}
    PS = ("sc", "dd")

    def clash(a, b):
        if a[1] >= b[2] or b[1] >= a[2]:
            return False
        s, t = (a[3] if len(a) > 3 else 1), (b[3] if len(b) > 3 else 1)
        return not (s > 1 and s == t and a[1] % s != b[1] % s)

    def need(e, reads, writes):
        deps = []
        for rs, wr in ((reads, False), (writes, True)):
            for r in rs:
                ps = r[0] in PS
                for (q, qw, qe, ev, clk) in hist.get(r[0], []):
                    if (wr or qw or (ps and qe != e)) and clash(r, q) and not (ps and e == "t" and qe == "t"):
                        deps.append((ev, clk))
        best = {}
        for ev, clk in deps:
            if known[e].get(ev[0], 0) < ev[1] and (ev[0] not in best or best[ev[0]][0] < ev[1]):
                best[ev[0]] = (ev[1], clk)
        for s in list(best):
            v = best[s][0]
            if any(o != s and best[o][1].get(s, 0) >= v for o in best):
                del best[s]
        for s, (v, clk) in best.items():
            queue[e].wait_ge(T.sem[s], v)
            waited[s] = max(waited.get(s, 0), v)
            for k2, v2 in clk.items():
                known[e][k2] = max(known[e].get(k2, 0), v2)
            known[e][s] = max(known[e].get(s, 0), v)

    def note(e, reads, writes, ev, clk):
        for r in reads:
            hist.setdefault(r[0], []).append((r, False, e, ev, clk))
        for r in writes:
            hist.setdefault(r[0], []).append((r, True, e, ev, clk))

    def bank(r):
        return (r[0], r[1] - r[1] % 512, r[1] - r[1] % 512 + 512) if r[0] in PS else r

    def op(e, call, reads, writes):
        reads = [bank(r) for r in reads]
        need(e, reads, writes)
        count[e] += 1
        ev = (engsem[e], count[e])
        call().then_inc(T.sem[ev[0]], 1)
        total[ev[0]] = count[e]
        clk = dict(known[e])
        clk[ev[0]] = ev[1]
        note(e, reads, writes, ev, clk)

    nl = [0]

    def dma(e, out, in_, reads, writes):
        need(e, reads, writes)
        s = "l%d" % nl[0] if writes else "st"
        total[s] = total.get(s, 0) + 16
        queue[e].dma_start(out, in_).then_inc(T.sem[s], 16)
        if writes:
            nl[0] += 1
            clk = dict(known[e])
            clk[s] = 16
            note(e, reads, writes, (s, 16), clk)

    def arrive(sem, n, writes):
        total[sem] = n
        note("r", [], writes, (sem, n), {sem: n})

    def fused(reads, parts):
        need("p", reads, [])
        total["sent"] = total.get("sent", 0) + sum(len(p[1]) for p in parts)
        g.remote_dma_fused([xfer(T, topo, core, *p) for p in parts], local_sem=T.sem.sent)

    def ap(r):
        if not isinstance(r, tuple):
            return r
        return T[r[0]][:, r[1]:r[2]:r[3]] if len(r) > 3 and r[3] > 1 else T[r[0]][:, r[1]:r[2]]

    def rs(*a):
        return [x for x in a if isinstance(x, tuple)]

    V = g.vector

    def vcopy(o, i):
        op("v", lambda: V.tensor_copy(ap(o), ap(i)), [i], [o])

    def vset(o, c):
        op("v", lambda: V.memset(ap(o), c), [], [o])

    def vts(o, i, s1, s2, *ops):
        op("v", lambda: V.tensor_scalar(ap(o), ap(i), ap(s1), ap(s2), *ops), rs(i, s1, s2), [o])

    def vtt(o, a, b, o0):
        op("v", lambda: V.tensor_tensor(ap(o), ap(a), ap(b), o0), [a, b], [o])

    def vscan(o, d0, d1):
        op("v", lambda: V.tensor_tensor_scan(ap(o), ap(d0), ap(d1), BIG, OP.add, OP.max), [d0, d1], [o])

    def vred(o, i, o0):
        op("v", lambda: V.tensor_reduce(ap(o), ap(i), AxisListType.X, o0), [i], [o])

    def quant(o, n0, i):
        w = (i[2] - i[1]) // 4
        a, b = (o, n0, n0 + w), (o + "_s", n0, n0 + w)
        op("v", lambda: V.quantize_mx(ap(a), ap(b), ap(i)), [i], [a, b])

    def act(o, i, f, **kw):
        op("s", lambda: g.scalar.activation(ap(o), ap(i), f, **{k: ap(v) for k, v in kw.items()}),
           rs(i, kw.get("bias"), kw.get("scale")), rs(o, kw.get("accum_out")))

    def iota(o, pat, base, cm):
        op("p", lambda: g.iota(ap(o), pat, base, cm, allow_small_or_imprecise_dtypes=True), [], [o])

    def copy(e, o, i):
        if e == "s":
            act(o, i, AF.Copy)
        else:
            vcopy(o, i)

    def times(e, o, i, c, cf):
        if e == "s":
            act(o, i, AF.Copy, scale=cf)
        else:
            vts(o, i, c, None, OP.mult)

    def fill(e, o):
        n = len(range(*o[1:]))
        if e == "s":
            act(o, ("zr", 0, n), AF.Copy)
        elif e == "p":
            iota(o, [[0, n]], 0, 0)
        else:
            vset(o, 0.0)

    def pick_codes(o, o0, win, w1, off, c0, c1):
        oc, wc, of = (o, o0, o0 + 16 * (c1 - c0)), (win, 0, w1), (off, c0, c1)
        op("v", lambda: V.tensor_copy(ap(oc).bitcast(dt.uint32), ap(wc).bitcast(dt.uint32).indirect(ap(of))), [wc, of], [oc])

    def pick_scales(e, o, o0, win, w1, off, c0, c1):
        osn, ws, of = (o + "_s", o0, o0 + 16 * (c1 - c0)), (win + "_s", 0, w1), (off, c0, c1)
        if e == "s":
            op("s", lambda: g.scalar.activation(ap(osn), ap(ws).indirect(ap(of)), AF.Copy), [ws, of], [osn])
        else:
            op("v", lambda: V.tensor_copy(ap(osn), ap(ws).indirect(ap(of))), [ws, of], [osn])

    H = {}

    def picks(c, s, *a):
        H[c] = lambda: pick_codes(*a)
        H[s] = lambda e="s": pick_scales(e, *a)

    def mm(ps, b, l, l0, r, r0, start=True, stop=True, n=128):
        o = (ps, 512 * b, 512 * b + n)
        a, sa, c, sb = (l, l0, l0 + 128), (l + "_s", l0, l0 + 128), (r, r0, r0 + n), (r + "_s", r0, r0 + n)
        op("t", lambda: g.tensor.matmul_mx(ap(o), ap(a), ap(sa), ap(c), ap(sb), start, stop), [a, sa, c, sb] + ([] if start else [o]), [bank(o)])

    near, far = pl["near"][0] + pl["near"][1], pl["far"][0] + pl["far"][1]
    own, at = near.index(me), far.index(pl["proxy"])

    def both(n, where):
        return [(n + s, 32 * a, 32 * a + 32) for a in where for s in ("", "_s")]

    others = [r for r in near if r != me]
    arrive("azn", 2 * (2 * FN + FM), both("zn", [near.index(r) for r in others]))
    arrive("azf", 2 * (2 * FN + FM), both("zf", [k for k in range(4) if k != at]))
    arrive("apx", 24, [("px", 0, 128), ("px_s", 0, 128)])
    arrive("apl", 8, [("pl", 0, 8)])
    for x, who, n in (("n", others, 2 * FN + FM), ("f", far, 4 * FR)):
        arrive("hv1" + x, 2 * n, both("lv1", who))
        arrive("hv2" + x, 2 * n, both("lv2", who))
        arrive("hn" + x, n, [("xw", 32 * r, 32 * r + 8) for r in who])

    R16, HQ128, P16, E0, CHI, CLO, CS, T0, T1, T2, T3 = [("cf", k, k + 1) for k in range(11)]
    CNT, TOK = ("cnt", 0, 1), ("tok", 0, 1)
    pf = [q[0] // 2 for q in pl["far"]]
    pn = [q[0] // 2 for q in pl["near"]]

    H["ldx"] = lambda e: dma(e, T.xt[:, 0:512], T.x[:], [], [("xt", 0, 512)])
    H["ldc"] = lambda e: dma(e, T.xt[:, 520:552], T.co[:, 0:32], [], [("xt", 520, 552)])
    H["ldb1"] = lambda e: dma(e, T.b1r[:], T.b1[:], [], [("b1r", 0, 512)])
    H["ldb2"] = lambda e: dma(e, T.b2r[:], T.b2[:], [], [("b2r", 0, 512)])
    H["ldw"] = lambda e: dma(e, T.wt[:], T.w[:], [], [("wt", 0, 512)])
    H["i.tok"] = lambda: iota(TOK, [[0, 1]], 0, 1)
    H["i.itr"] = lambda: iota(("itr", 0, 128), [[1, 128]], 0, 0)
    H["i.ir"] = lambda: iota(("ir", 0, 256), [[0, 8], [1, 16], [16, 2]], 128, 0)
    H["i.ic8"] = lambda: iota(("ic8", 0, 8), [[-2 * (pn[0] - pf[0]), 2], [-2 * (pf[1] - pf[0]), 2], [-1, 2]], 8 - 2 * pf[0], 0)
    H["i.ik"] = lambda: iota(("ik", 0, 128), [[0, 2], [1, 16], [64, 4]], 0, 0)
    H["zr"] = lambda: vset(("zr", 0, 512), 0.0)
    H["zb"] = lambda e: fill(e, ("zb", 32, 544))
    for h in range(4):
        for b in ("b1", "b2"):
            H[b + str(h)] = lambda e, b=b, h=h: times(e, (b + "t", 512 * h, 512 * h + 512), (b + "r", 0, 512), ("mkb", h, h + 1), ("mkf", h, h + 1))
        H["w16%d" % h] = lambda h=h: vts(("w16", 128 * h, 128 * h + 128), ("ik", 0, 128), -64.0 * h, R16, OP.add, OP.is_equal)
        H["qe%d" % h] = lambda b=h: quant("qe", 128 * b, ("gp", 3 - b, 515 - b))
        H["qm%d" % h] = lambda b=h: quant("qm", 128 * b, ("gm", 3 - b, 515 - b))
    H["mkb"] = lambda: vts(("mkb", 0, 4), ("itr", 0, 4), 128.0, HQ128, OP.mult, OP.is_equal)
    H["mkf"] = lambda: vts(("mkf", 0, 4), ("itr", 0, 4), 128.0, HQ128, OP.mult, OP.is_equal)
    H["xt"] = lambda: vset(("xt", 512, 520), 0.0)
    H["zt"] = lambda: vset(("zt", 0, 16), 0.0)
    H["zm"] = lambda: vset(("zm", 0, 4), -128.0)
    H["onb"] = lambda: vset(("onb", 0, 520), 1.0)
    H["gp"] = lambda: op("p", lambda: g.affine_select(T.gp[:, 0:520], T.onb[:, 0:520], [[-1, 520]], OP.is_equal, 0.0, 3, 4),
                         [("onb", 0, 520)], [("gp", 0, 520)])
    H["gm"] = lambda e: times(e, ("gm", 0, 520), ("gp", 0, 520), -1.0, -1.0)
    H["chi"] = lambda: vts(CHI, TOK, M16 - 128.0, M16, OP.add, OP.subtract)
    H["clo"] = lambda: vts(CLO, TOK, -128.0, CHI, OP.add, OP.subtract)
    H["tri1"] = lambda: vts(("tri", 1, 512, 4), ("itr", 0, 128), TOK, 128.0, OP.is_equal, OP.mult)
    H["tri2"] = lambda: vts(("tri", 2, 512, 4), ("itr", 0, 128), TOK, None, OP.is_gt)
    H["tri0"] = lambda: vtt(("tri", 0, 512, 4), ("tri", 1, 512, 4), ("tri", 2, 512, 4), OP.add)
    H["tri3"] = lambda: vts(("tri", 3, 512, 4), ("tri", 0, 512, 4), -1.0, None, OP.mult)
    H["qtri"] = lambda: quant("qtri", 0, ("tri", 0, 512))
    H["hq0"] = lambda: vts(T0, TOK, -15.5, 2 * M16, OP.add, OP.add)
    H["hq"] = lambda: vts(HQ128, T0, 2 * M16, 4.0, OP.subtract, OP.mult)
    H["p160"] = lambda: vts(T3, TOK, -7.5, M16, OP.add, OP.add)
    H["p16"] = lambda: vts(P16, T3, M16, None, OP.subtract)
    H["r16"] = lambda: vts(R16, TOK, P16, None, OP.subtract)
    H["e0"] = lambda: vts(E0, P16, -1.25, TOK, OP.mult, OP.add)
    H["eq"] = lambda: vts(("eq", 0, 2), ("itr", 1, 18, 16), E0, 5.0, OP.add, OP.min)
    H["offc"] = lambda: vts(("offc", 0, 2), ("eq", 0, 2), 0.0, None, OP.max)
    for n4 in ("n4n", "n4f", "n4h"):
        H[n4] = lambda e, n4=n4: fill(e, (n4, 0, 16))
    H["xb"] = lambda e: fill(e, ("xb", 64, 544))
    H["qw16"] = lambda: quant("qw16", 0, ("w16", 0, 512))
    H["lz1"] = lambda: quant("lv1", 256, ("zr", 0, 512))
    H["lz2"] = lambda: quant("lv2", 256, ("zr", 0, 512))
    H["pz"] = lambda: quant("px", 128, ("zr", 0, 512))
    for r in range(8):
        H["xw%d" % r] = lambda e, r=r: fill(e, ("xw", 32 * r + 8, 32 * r + 32))
    H["xtw"] = lambda: vset(("xtw", 256, 288), -1.0)
    H["ict0"] = lambda: vset(("ict", 0, 32), 0.0)
    H["ict1"] = lambda: vcopy(("ict", 0, 32, 4), ("ic8", 0, 8))
    H["ict2"] = lambda: vcopy(("ict", 3, 32, 4), ("ic8", 0, 8))
    H["sx0"] = lambda e: fill(e, ("sx", 1, 640, 2))

    H["qx"] = lambda: quant("qx", 0, ("xt", 0, 552))
    H["cells"] = lambda: mm("sc", 0, "qx", 0, "qx", 10)
    H["top"] = lambda: vscan(("pmc", 0, 8), ("zt", 0, 8), ("sc", 120, 128))
    H["from0"] = lambda: vts(("zb", 512, 544, 4), ("pmc", 0, 8), ("pmc", 7, 8), None, OP.is_ge)
    H["from1"] = lambda: vts(("zb", 519, 544, 4), ("pmc", 0, 7), ("pmc", 7, 8), None, OP.is_ge)
    H["qo"] = lambda: quant("qo", 0, ("zb", 32, 544))
    H["earlier"] = lambda: mm("sc", 1, "qtri", 0, "qo", 0)
    H["cs"] = lambda: vred(CS, ("zb", 512, 544, 4), OP.add)
    H["mhi"] = lambda: vts(("sx", 512, 576, 2), ("ict", 0, 32), CS, CHI, OP.is_equal, OP.mult)
    H["mlo"] = lambda: vts(("sx", 576, 640, 2), ("ict", 0, 32), CS, CLO, OP.is_equal, OP.mult)
    H["cnt"] = lambda: vred(CNT, ("sc", 632, 640), OP.max)
    H["sx1"] = lambda: vts(("sx", 0, 512, 2), ("ir", 0, 256), CNT, None, OP.is_equal)
    H["qs"] = lambda: quant("qs", 0, ("sx", 0, 640))
    H["lists"] = lambda: [mm("sc", 2, "qs", 0, "qs", 16 + 16 * i, i == 0, i == 1) for i in range(2)]
    H["offs"] = lambda: vts(("offs", 0, 16), ("sc", 1136, 1152), 128.0, None, OP.add)

    def to_relays(kind, buf, w, dstbuf, sem, step=64):
        parts = []
        for i, rc in enumerate(pl[kind]):
            es = topo.engines(core, rc)
            es = es[len(es) - FF:]
            if kind == "nums":
                es = es[4 * i:4 * i + 4]
            parts.append((rc, es, sem, cols(T, dstbuf, 0, w), cols(T, buf, step * i, step * i + w)))
        fused([(buf, 0, step + w)], parts)

    def to_near(buf, w, dstbuf, a, sem, step=32):
        parts, n = [], 0
        for k, d in enumerate(near):
            if d != me:
                es = topo.engines(core, T.cores[d])
                if d in pl["here"]:
                    es = es[len(es) - FM:]
                else:
                    es = es[FN * n:FN * n + FN]
                    n += 1
                parts.append((T.cores[d], es, sem, cols(T, dstbuf, a, a + w), cols(T, buf, step * k, step * k + w)))
        fused([(buf, 0, 3 * step + w)], parts)

    def out(i, k, n):
        es = topo.engines(core, pl["out"][i])
        return es[len(es) - FF:][k:k + n]

    H["p.c"] = lambda: fused([("qx", 0, 128)], [(pl["out"][i], out(i, 0, FP), "rzc", cols(T, "rz", 0, 64), cols(T, "qx", 64 * i, 64 * i + 64)) for i in range(2)])
    H["p.s"] = lambda: fused([("qx_s", 0, 128)], [(pl["out"][2], out(2, FF - FP, FP), "rzs", cols(T, "rz_s", 0, 128), cols(T, "qx_s", 0, 128))])
    H["p.l"] = lambda: fused([("offs", 0, 8)], [(pl["out"][2], out(2, 0, FF), "rzl", cols(T, "rl", 0, 8), cols(T, "offs", 0, 8))])
    picks("sf.c", "sf.s", "sf", 0, "px", 130, "pl", 0, 8)
    picks("fown.c", "fown.s", "zf", 32 * at, "px", 130, "pl", 2 * own, 2 * own + 2)
    picks("sn.c", "sn.s", "sn", 0, "qx", 130, "offs", 8, 16)
    picks("own.c", "own.s", "zn", 32 * own, "qx", 130, "offs", 8 + 2 * own, 10 + 2 * own)
    H["f.c"] = lambda: to_near("sf", 32, "zf", 32 * at, "azf")
    H["f.s"] = lambda: to_near("sf_s", 32, "zf_s", 32 * at, "azf")
    H["n.c"] = lambda: to_near("sn", 32, "zn", 32 * own, "azn")
    H["n.s"] = lambda: to_near("sn_s", 32, "zn_s", 32 * own, "azn")

    def relocate(x, n4, w0, b):
        ql, v = "ql" + x, (544 if x == "n" else 0)
        w, f, hi, lo = (n4, w0, w0 + 8), ("offc", 0, 2), ("xb", v, v + 32), ("xb", v + 32, v + 64)
        a = 64 if x == "n" else 0
        k = 512 * b + (120 if x == "n" else 0)
        return [lambda: op("v", lambda: V.tensor_scalar(ap(hi), ap(w).indirect(ap(f)), M16, M16, OP.add, OP.subtract), [w, f], [hi]),
                lambda: op("v", lambda: V.tensor_tensor(ap(lo), ap(w).indirect(ap(f)), ap(hi), OP.subtract), [w, f, hi], [lo]),
                lambda: quant(ql, 0, ("xb", a, a + 544)),
                lambda: [mm("sc", b, "qw16", 0, ql, 8 * i, i == 0, i == 1) for i in range(2)]], ("sc", k, k + 8)

    fs, ls = relocate("n", "n4h", 0, 3)
    for i, f in enumerate([lambda: vts(T1, CS, -32.0, CNT, OP.mult, OP.add),
                           lambda: vts(T2, CNT, 128.0 + CAPP, None, OP.is_lt),
                           lambda: vts(("n4h", 1, 5), ("zm", 0, 4), T1, T2, OP.add, OP.mult)]
                          + fs + [lambda ls=ls: vts(("offh", 0, 8), ls, 256.0, None, OP.add)]):
        H["hl%d" % i] = f

    def level(x, l):
        win, bk, pm, n4, off = ("z" if l == 1 else "rq") + x, "qb%d" % l, "pm" + x, "n4" + x, "off%d%s" % (l, x)
        b0, w0, N, v, lv = (0 if x == "n" else 2), 8 * (l - 1), "%s%d." % (x.upper(), l), "v%d%s" % (l, x), "lv%d" % l
        fs, ls = relocate(x, n4, w0, b0)
        parts = [("dd", h, h, 1) for h in range(4)] if N == "F2." else [("sc", b0, 0, 2), ("sc", b0 + 1, 2, 2)]

        def scan(h):
            ps, b, h0, n = [q for q in parts if q[2] <= h < q[2] + q[3]][0]
            k = 512 * b + 128 * (h - h0)
            vscan((pm, 128 * h, 128 * h + 128), ("zr", 0, 128), (ps, k, k + 128))

        def tally(h, e):
            act(("jk" + x, 128 * h, 128 * h + 128), (pm, 128 * h, 128 * h + 128), AF.Sign, bias=(pm, 128 * h + 127, 128 * h + 128), scale=-1.0,
                accum_out=(n4, w0 + h + 1, w0 + h + 2))

        def back(s):
            if x == "f":
                to_relays("scales" if s else "codes", v + s, 64, "rv%d" % l + s, "r%d%s" % (l, "s" if s else "c"))
            else:
                to_near(v + s, 32, lv + s, 32 * me, "hv%dn" % l)

        for i in range(4):
            H.update({N + "place%d" % i: fs[i], N + "scan%d" % i: lambda i=i: scan(i), N + "count%d" % i: lambda e="s", i=i: tally(i, e)})
        for ps, b, h0, n in parts:
            H[N + "score%d" % h0] = lambda ps=ps, b=b, h0=h0, n=n: mm(ps, b, win, 0, bk, 128 * h0, True, True, 128 * n)
        picks(N + "codes", N + "scales", v, 0, bk, 512, off, 0, 8)
        picks(N + "ownc", N + "owns", lv, 32 * me, bk, 512, off, 2 * own, 2 * own + 2)
        H.update({N + "list": lambda: vts((off, 0, 8), ls, HQ128, None, OP.add),
                  N + "number": lambda e="s": copy(e, ("nb" + x, 4 * l - 4, 4 * l), (n4, w0 + 1, w0 + 5)),
                  N + "codesback": lambda: back(""), N + "scalesback": lambda: back("_s")})

    for x in "nf":
        level(x, 1)
        level(x, 2)
        H[x + ".given"] = lambda x=x: [mm("dd", b, "qe", 128 * b, "z" + x, 0, True, False) for b in range(4)]
        H[x + ".minus"] = lambda x=x: [mm("dd", b, "qm", 128 * b, "v1" + x, 0, False, True) for b in range(4)]
        H[x + ".repack"] = lambda x=x: quant("rq" + x, 0, ("rt" + x, 0, 512))
        for b in range(4):
            H[x + ".rest%d" % b] = lambda e, x=x, b=b: copy(e, ("rt" + x, b, 512, 4), ("dd", 512 * b, 512 * b + 128))
    H["qb1"] = lambda: quant("qb1", 0, ("b1t", 0, 2048))
    H["qb2"] = lambda: quant("qb2", 0, ("b2t", 0, 2048))
    H["qw"] = lambda: quant("qw", 0, ("wt", 0, 512))
    H["f.nums"] = lambda: to_relays("nums", "nbf", 8, "rn", "rnc", 0)
    H["n.nums"] = lambda: to_near("nbn", 8, "xw", 32 * me, "hnn", 0)
    H["n.numo"] = lambda e="s": copy(e, ("xw", 32 * me, 32 * me + 8), ("nbn", 0, 8))

    for l in (1, 2):
        h, o = "h%d" % l, 128 * (l - 1)
        picks(h + ".c", h + ".s", h, 0, "lv%d" % l, 258, "offh", 0, 8)
        H["oc%d" % l] = lambda e, h=h, o=o: dma(e, T.oc[:, 4 * o:4 * o + 512], cols(T, h, 0, 128), [(h, 0, 128)], [])
        for k in range(4):
            H["os%d%d" % (l, k)] = lambda e, h=h, o=o, k=k: dma(e, T.osc[4 * k:4 * k + 4, o:o + 128], T[h + "_s"][32 * k:32 * k + 4, 0:128],
                                                                [(h + "_s", 0, 128)], [])
        H["y%d" % l] = lambda h=h, l=l: mm("sc", 3, "qw", 0, h, 0, l == 1, l == 2)
    H["wn0"] = lambda: op("v", lambda: V.transpose(T.xtw[:, 0:256], T.xw[:, 0:256]), [("xw", 0, 256)], [("xtw", 0, 256)])
    o, w, f = ("wnt", 0, 128), ("xtw", 0, 288), ("offh", 0, 8)
    H["wn1"] = lambda: op("v", lambda: V.tensor_copy(ap(o), ap(w).indirect(ap(f))), [w, f], [o])
    H["wn2"] = lambda e: dma(e, T.wn[:], T.wnt[32 * own:32 * own + 8, 0:128], [o], [])
    H["yc"] = lambda e: copy(e, ("yt", 0, 128), ("sc", 1536, 1664))
    H["ys"] = lambda e: dma(e, T.y[:], T.yt[:], [("yt", 0, 128)], [])

    for name in ORDER.split():
        H[name.split(":")[0]](*name.split(":")[1:])
    for s in total:
        if waited.get(s, 0) < total[s]:
            g.wait_ge(T.sem[s], total[s])
